import numpy as np
import ml_dtypes


def mxq(x, axis, fmt="e4m3"):
    dtype, down = {"e4m3": (ml_dtypes.float8_e4m3fn, 7), "e5m2": (ml_dtypes.float8_e5m2, 14)}[fmt]
    v = np.moveaxis(np.asarray(x, np.float32).astype(ml_dtypes.bfloat16).astype(np.float64), axis, -1)
    blocks = v.reshape(v.shape[:-1] + (-1, 32))
    amax = np.abs(blocks).max(-1, keepdims=True)
    byte = np.maximum(np.where(amax > 0, np.frexp(amax)[1] - 1 + 127, 0) - down, 1)
    scale = np.exp2(byte - 127.0)
    codes = (blocks / scale).astype(np.float32).astype(dtype).astype(np.float64)
    return np.moveaxis((codes * scale).reshape(v.shape), -1, axis)


WIDE = False


def mx_kscale(k):
    if not WIDE:
        return np.ones(k)
    levels = np.array([10, -10, 5, -5, 0])
    if k % 512:
        return np.exp2(np.random.permutation(np.resize(levels, k // 32))).repeat(32)
    a = np.empty((k // 512, 16))
    for p in range(k // 512):
        a[p, :8] = np.random.permutation(np.resize(levels, 8))
        for g in range(8):
            far = levels[np.abs(levels - a[p, g]) >= 10]
            a[p, g + 8] = far[np.random.randint(len(far))]
    return np.exp2(a.ravel()).repeat(32)


def f64(x):
    return np.asarray(x).astype(np.float64)


def striped(idx):
    return np.tile(idx.reshape(-1, 16).T, (8, 1)).astype(np.uint16)


def unstriped(offs):
    return offs[:16].T.reshape(-1).astype(np.int64)


E2M1 = np.array([0.0, 0.5, 1.0, 1.5, 2.0, 3.0, 4.0, 6.0, -0.0, -0.5, -1.0, -1.5, -2.0, -3.0, -4.0, -6.0])


def pack_weight(w, fmt):
    k, n = w.shape
    w = f64(np.asarray(w, np.float32).astype(ml_dtypes.bfloat16)).reshape(k // 32, 32, n)
    amax = np.abs(w).max(1)
    if fmt == "e4m3":
        byte = np.frexp(amax)[1] - 1 + 127 - 7
    else:
        mant, ex = np.frexp(amax / 6.0)
        byte = np.where(mant > 0.5, ex, ex - 1) + 127
    byte = np.clip(np.where(amax > 0, byte, 1), 1, 254)
    scaled = (w * np.exp2(127.0 - byte)[:, None, :]).reshape(k, n).astype(np.float32)
    by_word = np.ascontiguousarray(scaled.reshape(k // 512, 128, 4, n).transpose(0, 1, 3, 2))
    if fmt == "e4m3":
        words = by_word.astype(ml_dtypes.float8_e4m3fn).view(np.uint8)
    else:
        c = by_word.astype(ml_dtypes.float4_e2m1fn).view(np.uint8) & 0xF
        words = (c[..., 0::2] | (c[..., 1::2] << 4)).reshape(k // 512, 128, 2 * n)
    return np.ascontiguousarray(words), np.ascontiguousarray(byte.astype(np.uint8).reshape(k // 512, 16, n))


def unpack_weight(words, scales, fmt):
    g, _, n = scales.shape
    words = np.ascontiguousarray(words).reshape(g, 128, n, -1)
    if fmt == "e4m3":
        vals = words.view(ml_dtypes.float8_e4m3fn).astype(np.float64)
    else:
        nib = np.empty((g, 128, n, 4), np.uint8)
        nib[..., 0::2] = words & 0xF
        nib[..., 1::2] = words >> 4
        vals = E2M1[nib]
    vals = vals * np.repeat(np.exp2(scales.astype(np.float64) - 127.0), 8, axis=1)[..., None]
    return vals.transpose(0, 1, 3, 2).reshape(g * 512, n)


def gelu(v):
    return 0.5 * v * (1.0 + np.tanh(np.sqrt(2.0 / np.pi) * (v + 0.044715 * v**3)))


K, H, N, T, S = 512, 2048, 512, 2048, 1024

def setup_inputs():
    n = np.random.standard_normal
    s = mx_kscale(K)[:, None]
    u = mx_kscale(H)[:, None]
    tab_words, tab_scales = pack_weight(n((K, T)) * s, "e4m3")
    wk = (n((K, H)) / np.sqrt(K) / s * np.sqrt(u).T).astype(np.float32)
    wr_words, wr_scales = pack_weight(n((K, N)) / np.sqrt(K) / s, "e2m1")
    wv_words, wv_scales = pack_weight(n((H, N)) / np.sqrt(H) / u, "e4m3")
    gT = n((N, T)).astype(np.float32)
    offs = striped(np.random.permutation(T)[:S])
    return {"tab_words": tab_words, "tab_scales": tab_scales, "offs": offs,
            "wk": wk, "wr_words": wr_words, "wr_scales": wr_scales,
            "wv_words": wv_words, "wv_scales": wv_scales, "gT": gT}

def reference(tab_words, tab_scales, offs, wk, wr_words, wr_scales, wv_words, wv_scales, gT):
    v = unpack_weight(tab_words, tab_scales, "e4m3")[:, unstriped(offs)]
    g = f64(gT)[:, unstriped(offs)]
    wr = unpack_weight(wr_words, wr_scales, "e2m1")
    wv = unpack_weight(wv_words, wv_scales, "e4m3")
    a = mxq(f64(wk), 0, "e4m3").T @ v
    h = np.square(np.maximum(a, 0.0))
    r = 1.0 / (1.0 + np.exp(-(wr.T @ v)))
    y = wv.T @ mxq(h, 0, "e4m3")
    return g + r * y

@@ -1,0 +1,281 @@
+from contextlib import ExitStack
+
+import concourse.mybir as mybir
+
+K, H, N, T, S = 512, 2048, 512, 2048, 1024
+FLOPS = 2 * S * (K * H + K * N + H * N)
+
+F32 = mybir.dt.float32
+BF16 = mybir.dt.bfloat16
+I32 = mybir.dt.int32
+U32 = mybir.dt.uint32
+U16 = mybir.dt.uint16
+U8 = mybir.dt.uint8
+FP8X4 = mybir.dt.float8_e4m3fn_x4
+FP4X4 = mybir.dt.float4_e2m1fn_x4
+ACT = mybir.ActivationFunctionType
+ALU = mybir.AluOpType
+
+P = 128
+PACK = 4
+PASS = P * PACK
+BLOCKS = PASS // 32
+QUADRANT = 32
+H_PASSES = H // PASS
+N_TILES = N // P
+LIST_ROWS = 16
+GROUP = 256
+GROUPS = S // GROUP
+BANK_TOKENS = 128
+
+CHUNKS = [(0, 256), (256, 256), (512, 256), (768, 128), (896, 128)]
+WIDE_CHUNKS = 3
+STEPS = [(c, b) for b in range(H_PASSES) for c in range(WIDE_CHUNKS)] + [
+    (c, b) for c in range(WIDE_CHUNKS, len(CHUNKS)) for b in range(H_PASSES)
+]
+VECTOR_RELU = {(0, 0), (1, 1), (3, 0), (7, 1)}
+VECTOR_SQUARE = {3, 17}
+GPSIMD_ADD_CHUNK = 0
+
+STAGE_BUFS = 5
+RELU_BUFS = 6
+SQUARE_BUFS = 8
+GATED_BUFS = 3
+KEY_BANKS = 4
+
+
+def tile_list_rwkv_channel_mix_kernel(
+    tc, tab_words, tab_scales, offs, wk, wr_words, wr_scales, wv_words, wv_scales, gT, out
+):
+    nc = tc.nc
+    with ExitStack() as ctx:
+        keep = ctx.enter_context(tc.tile_pool(name="keep", bufs=1))
+        ring = ctx.enter_context(tc.tile_pool(name="ring", bufs=STAGE_BUFS))
+        psum_key = ctx.enter_context(tc.psum_pool(name="psum_key", bufs=KEY_BANKS))
+        psum_value = ctx.enter_context(tc.psum_pool(name="psum_value", bufs=1))
+
+        offsets = keep.tile([P, S // LIST_ROWS], U16, name="offsets")
+        tab_w = keep.tile([P, T], I32, name="tab_w", align_bytes=64)
+        tab_s = keep.tile([P, T // 4], I32, name="tab_s", align_bytes=64)
+        wr_w = keep.tile([P, 2 * N], U8, name="wr_w", align_bytes=64)
+        wr_s = keep.tile([P, N], U8, name="wr_s", align_bytes=64)
+        wv_s = keep.tile([P, N], U8, name="wv_s", align_bytes=64)
+        wv_w = keep.tile([P, H_PASSES, N], I32, name="wv_w", align_bytes=64)
+
+        nc.vector.memset(tab_s[:], 0)
+        nc.vector.memset(wr_s[:].bitcast(I32), 0)
+        nc.vector.memset(wv_s[:].bitcast(I32), 0)
+
+        nc.sync.dma_start(offsets[:], offs)
+        nc.sync.dma_start(out=wr_w[:].bitcast(I32), in_=wr_words[0].bitcast(I32))
+        for r in range(PACK):
+            nc.sync.dma_start(out=tab_s[r:P:QUADRANT, :], in_=tab_scales[0, r:BLOCKS:PACK, :].bitcast(I32))
+        nc.sync.dma_start(out=tab_w[:], in_=tab_words[0].rearrange("p t i -> p (t i)").bitcast(I32))
+        for r in range(PACK):
+            nc.sync.dma_start(out=wr_s[r:P:QUADRANT, :].bitcast(I32), in_=wr_scales[0, r:BLOCKS:PACK, :].bitcast(I32))
+
+        wk_rows = wk.rearrange("(p j) c -> p j c", j=PACK)
+        wk_raw = []
+        g_tab = []
+
+        def load_wk(b):
+            block = ring.tile([P, PACK, PASS], F32, name="wk_raw%d" % b, tag="stage")
+            nc.sync.dma_start(out=block[:], in_=wk_rows[:, :, b * PASS : (b + 1) * PASS])
+            wk_raw.append(block)
+
+        def load_residual_table(n):
+            table = ring.tile([P, T], F32, name="g_tab%d" % n, tag="stage")
+            nc.sync.dma_start(out=table[:], in_=gT[n * P : (n + 1) * P, :])
+            g_tab.append(table)
+
+        for b in range(H_PASSES - 1):
+            load_wk(b)
+        nc.sync.dma_start(out=wv_w[:], in_=wv_words.rearrange("a p c i -> p a (c i)").bitcast(I32))
+        load_residual_table(0)
+        load_wk(H_PASSES - 1)
+        load_residual_table(1)
+        load_residual_table(2)
+        for q in range(P // QUADRANT):
+            nc.sync.dma_start(
+                out=wv_s[QUADRANT * q : QUADRANT * q + PACK * H_PASSES, :].bitcast(I32),
+                in_=wv_scales[:, PACK * q : PACK * (q + 1), :].bitcast(I32),
+            )
+        load_residual_table(3)
+
+        v_w = keep.tile([P, S], U32, name="v_w", align_bytes=64)
+        v_s = keep.tile([P, S], U8, name="v_s", align_bytes=64)
+        wk_bf = [keep.tile([P, PACK, P, PACK], BF16, name="wk_bf%d" % b, align_bytes=64) for b in range(H_PASSES)]
+        wk_w = [keep.tile([P, PASS], U32, name="wk_w%d" % b, align_bytes=64) for b in range(H_PASSES)]
+        wk_s = [keep.tile([P, PASS], U8, name="wk_s%d" % b, align_bytes=64) for b in range(H_PASSES)]
+        gate = [keep.tile([P, N_TILES, GROUP], F32, name="gate%d" % g) for g in range(GROUPS)]
+        resid = [keep.tile([P, N_TILES, GROUP], F32, name="resid%d" % g) for g in range(GROUPS)]
+        h_w = keep.tile([P, H_PASSES, S], U32, name="h_w", align_bytes=64)
+        h_s = keep.tile([P, H_PASSES, S], U8, name="h_s", align_bytes=64)
+
+        def listed(g):
+            return offsets[:, g * (GROUP // LIST_ROWS) : (g + 1) * (GROUP // LIST_ROWS)]
+
+        def gather_tokens(g):
+            cols = slice(g * GROUP, (g + 1) * GROUP)
+            nc.vector.tensor_copy(v_w[:, cols], tab_w[:].bitcast(U32).indirect(listed(g)))
+            nc.vector.tensor_copy(v_s[:, cols], tab_s[:].bitcast(U8).indirect(listed(g)))
+
+        def receptance(g):
+            cols = slice(g * GROUP, (g + 1) * GROUP)
+            for pair in range(N_TILES // 2):
+                z = psum_key.tile([P, 2, GROUP], F32, name="z", tag="key")
+                for i in range(2):
+                    n = 2 * pair + i
+                    nc.tensor.matmul_mx(
+                        out=z[:, i, :],
+                        lhsT=wr_w[:, 2 * P * n : 2 * P * (n + 1)].bitcast(FP4X4),
+                        lhsT_scale=wr_s[:, P * n : P * (n + 1)],
+                        rhs=v_w[:, cols].bitcast(FP8X4),
+                        rhs_scale=v_s[:, cols],
+                        start=True,
+                        stop=True,
+                    )
+                nc.scalar.activation(out=gate[g][:, 2 * pair : 2 * pair + 2, :], in_=z[:], func=ACT.Sigmoid)
+
+        def quantize_wk(b):
+            for half in range(2):
+                m0, m1 = half * P // 2, (half + 1) * P // 2
+                nc.vector.tensor_copy(
+                    out=wk_bf[b][:, :, m0:m1, :].rearrange("p t m j -> p m j t"),
+                    in_=wk_raw[b][:, :, PACK * m0 : PACK * m1].rearrange("p j (m t) -> p m j t", t=PACK),
+                )
+            nc.vector.quantize_mx(
+                out=wk_w[b][:].bitcast(FP8X4), scales=wk_s[b][:], in_=wk_bf[b][:].rearrange("p t m j -> p (t m j)")
+            )
+
+        def gather_residuals():
+            for n in range(N_TILES):
+                for g in range(GROUPS):
+                    nc.vector.tensor_copy(resid[g][:, n, :], g_tab[n][:].indirect(listed(g)))
+
+        relu_of = {}
+
+        def keys(s):
+            c, b = STEPS[s]
+            j0, width = CHUNKS[c]
+            x = ring.tile([P, width, PACK], F32, name="x", tag="x", bufs=RELU_BUFS)
+            relu_of[s] = x
+            for bank in range(width // BANK_TOKENS):
+                cols = slice(j0 + bank * BANK_TOKENS, j0 + (bank + 1) * BANK_TOKENS)
+                a = psum_key.tile([P, PACK, BANK_TOKENS], F32, name="a", tag="key")
+                for t in range(PACK):
+                    nc.tensor.matmul_mx(
+                        out=a[:, t, :],
+                        lhsT=wk_w[b][:, P * t : P * (t + 1)].bitcast(FP8X4),
+                        lhsT_scale=wk_s[b][:, P * t : P * (t + 1)],
+                        rhs=v_w[:, cols].bitcast(FP8X4),
+                        rhs_scale=v_s[:, cols],
+                        start=True,
+                        stop=True,
+                    )
+                dst = x[:, bank * BANK_TOKENS : (bank + 1) * BANK_TOKENS, :]
+                src = a[:].rearrange("p t j -> p j t")
+                if (s, bank) in VECTOR_RELU:
+                    nc.vector.tensor_scalar(out=dst, in0=src, scalar1=0.0, scalar2=None, op0=ALU.max)
+                else:
+                    nc.scalar.activation(out=dst, in_=src, func=ACT.Relu)
+
+        def square(s):
+            c, b = STEPS[s]
+            j0, width = CHUNKS[c]
+            cols = slice(j0, j0 + width)
+            h_bf = ring.tile([P, width, PACK], BF16, name="h_bf", tag="h_bf", align_bytes=64, bufs=SQUARE_BUFS)
+            x = relu_of[s]
+            if s in VECTOR_SQUARE:
+                nc.vector.tensor_tensor(out=h_bf[:], in0=x[:], in1=x[:], op=ALU.mult)
+            else:
+                nc.scalar.activation(out=h_bf[:], in_=x[:], func=ACT.Square)
+            nc.vector.quantize_mx(
+                out=h_w[:, b, cols].bitcast(FP8X4),
+                scales=h_s[:, b, cols],
+                in_=h_bf[:].rearrange("p j t -> p (j t)"),
+            )
+
+        y_of = {}
+
+        def values(c, b):
+            j0, width = CHUNKS[c]
+            cols = slice(j0, j0 + width)
+            if b == 0:
+                y_of[c] = [psum_value.tile([P, width], F32, name="y%d" % n, tag="y%d" % n) for n in range(N_TILES)]
+            for n in range(N_TILES):
+                nc.tensor.matmul_mx(
+                    out=y_of[c][n][:],
+                    lhsT=wv_w[:, b, P * n : P * (n + 1)].bitcast(FP8X4),
+                    lhsT_scale=wv_s[PACK * b : P, P * n : P * (n + 1)],
+                    rhs=h_w[:, b, cols].bitcast(FP8X4),
+                    rhs_scale=h_s[:, b, cols],
+                    start=(b == 0),
+                    stop=(b == H_PASSES - 1),
+                )
+
+        gated_of = {}
+
+        def gate_values(c, n):
+            j0, width = CHUNKS[c]
+            g, lo = divmod(j0, GROUP)
+            if n == 0:
+                gated_of[c] = ring.tile([P, N_TILES, width], F32, name="gated", tag="gated", bufs=GATED_BUFS)
+            nc.vector.tensor_tensor(
+                out=gated_of[c][:, n, :], in0=y_of[c][n][:], in1=gate[g][:, n, lo : lo + width], op=ALU.mult
+            )
+
+        out_rows = out.rearrange("(n p) j -> p n j", p=P)
+
+        def add_and_store(c, n0, n1):
+            j0, width = CHUNKS[c]
+            g, lo = divmod(j0, GROUP)
+            result = keep.tile([P, n1 - n0, width], F32, name="result%d_%d" % (c, n0))
+            if c == GPSIMD_ADD_CHUNK:
+                for n in range(n0, n1):
+                    nc.gpsimd.tensor_tensor(
+                        out=result[:, n - n0, :],
+                        in0=gated_of[c][:, n, :],
+                        in1=resid[g][:, n, lo : lo + width],
+                        op=ALU.add,
+                    )
+            else:
+                nc.vector.tensor_tensor(
+                    out=result[:], in0=gated_of[c][:, n0:n1, :], in1=resid[g][:, n0:n1, lo : lo + width], op=ALU.add
+                )
+            nc.sync.dma_start(out=out_rows[:, n0:n1, j0 : j0 + width], in_=result[:])
+
+        for g in range(GROUPS):
+            gather_tokens(g)
+            receptance(g)
+        quantize_wk(0)
+        keys(0)
+
+        last = len(CHUNKS) - 1
+        squared = set()
+        open_chunk = 0
+        passes_done = 0
+        for s in range(len(STEPS)):
+            if s + 1 < H_PASSES:
+                quantize_wk(s + 1)
+            if s + 1 == H_PASSES - 1:
+                gather_residuals()
+            if s + 1 < len(STEPS):
+                keys(s + 1)
+            square(s)
+            squared.add(STEPS[s])
+            while open_chunk <= last and (open_chunk, passes_done) in squared:
+                values(open_chunk, passes_done)
+                passes_done += 1
+                if passes_done == H_PASSES:
+                    if open_chunk < last:
+                        for n in range(N_TILES):
+                            gate_values(open_chunk, n)
+                    open_chunk += 1
+                    passes_done = 0
+
+        for c in range(last):
+            add_and_store(c, 0, N_TILES)
+        for n in range(N_TILES):
+            gate_values(last, n)
+            add_and_store(last, n, n + 1)

@@ -24,24 +24,33 @@ QUADRANT = 32
 H_PASSES = H // PASS
 N_TILES = N // P
 LIST_ROWS = 16
-GROUP = 256
-GROUPS = S // GROUP
-BANK_TOKENS = 128
+BANK = 512
+BANK_BYTES = 4 * BANK
+BANK_TOKENS = BANK // PACK
 
+GATHERS = [(0, 256), (256, 256), (512, 512)]
 CHUNKS = [(0, 256), (256, 256), (512, 256), (768, 128), (896, 128)]
-WIDE_CHUNKS = 3
-STEPS = [(c, b) for b in range(H_PASSES) for c in range(WIDE_CHUNKS)] + [
-    (c, b) for c in range(WIDE_CHUNKS, len(CHUNKS)) for b in range(H_PASSES)
+WOVEN_CHUNKS = 2
+STEPS = [(c, b) for b in range(H_PASSES) for c in range(WOVEN_CHUNKS)] + [
+    (c, b) for c in range(WOVEN_CHUNKS, len(CHUNKS)) for b in range(H_PASSES)
 ]
-VECTOR_RELU = {(0, 0), (1, 1), (3, 0), (7, 1)}
-VECTOR_SQUARE = {3, 17}
-GPSIMD_ADD_CHUNK = 0
+VECTOR_SQUARE = {1,2,3,4,5}
+VECTOR_RELU = set()
+LOADS = ["k0", "s", "k1", "k2", "k3", "v", "g0", "g1", "g2", "g3"]
 
-STAGE_BUFS = 5
-RELU_BUFS = 6
-SQUARE_BUFS = 8
-GATED_BUFS = 3
+FIRST_VALUE_STEP = 0
+PASSES_A_STEP = 2
+GPSIMD_ROUND = set()
+GPSIMD_SQUARE = set()
+RESID_GATHER = 512
+GPSIMD_ADD = set()
+FINISH_LAG = 0
+FUSED_TOKENS = 512
+HELD_SQUARE = 5
+RELU_BUFS = 7
+SQUARE_BUFS = 6
 KEY_BANKS = 4
+VALUE_BANKS = 8 - KEY_BANKS
 
 
 def tile_list_rwkv_channel_mix_kernel(
@@ -50,9 +59,22 @@ def tile_list_rwkv_channel_mix_kernel(
     nc = tc.nc
     with ExitStack() as ctx:
         keep = ctx.enter_context(tc.tile_pool(name="keep", bufs=1))
-        ring = ctx.enter_context(tc.tile_pool(name="ring", bufs=STAGE_BUFS))
-        psum_key = ctx.enter_context(tc.psum_pool(name="psum_key", bufs=KEY_BANKS))
-        psum_value = ctx.enter_context(tc.psum_pool(name="psum_value", bufs=1))
+        ring = ctx.enter_context(tc.tile_pool(name="ring", bufs=2))
+        shared = ctx.enter_context(tc.tile_pool(name="shared", bufs=1))
+        results = ctx.enter_context(tc.tile_pool(name="results", bufs=1))
+        psum = ctx.enter_context(tc.psum_pool(name="psum", bufs=1))
+        key_tiles = []
+        value_tiles = []
+
+        def key_bank(shape):
+            turn = len(key_tiles)
+            key_tiles.append(turn)
+            return psum.tile(shape, F32, name="key%d" % turn, offset=BANK_BYTES * (turn % KEY_BANKS))
+
+        def value_bank(shape):
+            turn = len(value_tiles)
+            value_tiles.append(turn)
+            return psum.tile(shape, F32, name="value%d" % turn, offset=BANK_BYTES * (KEY_BANKS + turn % VALUE_BANKS))
 
         offsets = keep.tile([P, S // LIST_ROWS], U16, name="offsets")
         tab_w = keep.tile([P, T], I32, name="tab_w", align_bytes=64)
@@ -69,63 +91,52 @@ def tile_list_rwkv_channel_mix_kernel(
         nc.sync.dma_start(offsets[:], offs)
         nc.sync.dma_start(out=wr_w[:].bitcast(I32), in_=wr_words[0].bitcast(I32))
         for r in range(PACK):
-            nc.sync.dma_start(out=tab_s[r:P:QUADRANT, :], in_=tab_scales[0, r:BLOCKS:PACK, :].bitcast(I32))
+            queue = nc.sync if r < PACK // 2 else nc.scalar
+            queue.dma_start(out=tab_s[r:P:QUADRANT, :], in_=tab_scales[0, r:BLOCKS:PACK, :].bitcast(I32))
         nc.sync.dma_start(out=tab_w[:], in_=tab_words[0].rearrange("p t i -> p (t i)").bitcast(I32))
         for r in range(PACK):
-            nc.sync.dma_start(out=wr_s[r:P:QUADRANT, :].bitcast(I32), in_=wr_scales[0, r:BLOCKS:PACK, :].bitcast(I32))
+            queue = nc.sync if r < PACK // 2 else nc.scalar
+            queue.dma_start(out=wr_s[r:P:QUADRANT, :].bitcast(I32), in_=wr_scales[0, r:BLOCKS:PACK, :].bitcast(I32))
 
         wk_rows = wk.rearrange("(p j) c -> p j c", j=PACK)
-        wk_raw = []
-        g_tab = []
-
-        def load_wk(b):
-            block = ring.tile([P, PACK, PASS], F32, name="wk_raw%d" % b, tag="stage")
-            nc.sync.dma_start(out=block[:], in_=wk_rows[:, :, b * PASS : (b + 1) * PASS])
-            wk_raw.append(block)
-
-        def load_residual_table(n):
-            table = ring.tile([P, T], F32, name="g_tab%d" % n, tag="stage")
-            nc.sync.dma_start(out=table[:], in_=gT[n * P : (n + 1) * P, :])
-            g_tab.append(table)
-
-        for b in range(H_PASSES - 1):
-            load_wk(b)
-        nc.sync.dma_start(out=wv_w[:], in_=wv_words.rearrange("a p c i -> p a (c i)").bitcast(I32))
-        load_residual_table(0)
-        load_wk(H_PASSES - 1)
-        load_residual_table(1)
-        load_residual_table(2)
-        for q in range(P // QUADRANT):
-            nc.sync.dma_start(
-                out=wv_s[QUADRANT * q : QUADRANT * q + PACK * H_PASSES, :].bitcast(I32),
-                in_=wv_scales[:, PACK * q : PACK * (q + 1), :].bitcast(I32),
-            )
-        load_residual_table(3)
+        wk_raw = [keep.tile([P, PACK, PASS], F32, name="wk_raw%d" % b) for b in range(H_PASSES - 1)]
+        wk_raw.append(shared.tile([P, PACK, PASS], F32, name="wk_raw_last", align_bytes=64, offset=0))
+        g_tab = [keep.tile([P, T], F32, name="g_tab%d" % n) for n in range(N_TILES)]
+        for load in LOADS:
+            if load[0] == "k":
+                b = int(load[1])
+                nc.sync.dma_start(out=wk_raw[b][:], in_=wk_rows[:, :, b * PASS : (b + 1) * PASS])
+            elif load[0] == "g":
+                n = int(load[1])
+                nc.sync.dma_start(out=g_tab[n][:], in_=gT[n * P : (n + 1) * P, :])
+            elif load[0] == "v":
+                nc.sync.dma_start(out=wv_w[:], in_=wv_words.rearrange("a p c i -> p a (c i)").bitcast(I32))
+            else:
+                for q in range(P // QUADRANT):
+                    nc.sync.dma_start(
+                        out=wv_s[QUADRANT * q : QUADRANT * q + PACK * H_PASSES, :].bitcast(I32),
+                        in_=wv_scales[:, PACK * q : PACK * (q + 1), :].bitcast(I32),
+                    )
 
         v_w = keep.tile([P, S], U32, name="v_w", align_bytes=64)
         v_s = keep.tile([P, S], U8, name="v_s", align_bytes=64)
-        wk_bf = [keep.tile([P, PACK, P, PACK], BF16, name="wk_bf%d" % b, align_bytes=64) for b in range(H_PASSES)]
         wk_w = [keep.tile([P, PASS], U32, name="wk_w%d" % b, align_bytes=64) for b in range(H_PASSES)]
         wk_s = [keep.tile([P, PASS], U8, name="wk_s%d" % b, align_bytes=64) for b in range(H_PASSES)]
-        gate = [keep.tile([P, N_TILES, GROUP], F32, name="gate%d" % g) for g in range(GROUPS)]
-        resid = [keep.tile([P, N_TILES, GROUP], F32, name="resid%d" % g) for g in range(GROUPS)]
+        gate = keep.tile([P, N_TILES, S], F32, name="gate")
+        resid = keep.tile([P, N_TILES, S - FUSED_TOKENS], F32, name="resid")
         h_w = keep.tile([P, H_PASSES, S], U32, name="h_w", align_bytes=64)
-        h_s = keep.tile([P, H_PASSES, S], U8, name="h_s", align_bytes=64)
+        h_s = shared.tile([P, H_PASSES, S], U8, name="h_s", align_bytes=64, offset=6 * S)
 
-        def listed(g):
-            return offsets[:, g * (GROUP // LIST_ROWS) : (g + 1) * (GROUP // LIST_ROWS)]
+        def listed(j0, width):
+            return offsets[:, j0 // LIST_ROWS : (j0 + width) // LIST_ROWS]
 
-        def gather_tokens(g):
-            cols = slice(g * GROUP, (g + 1) * GROUP)
-            nc.vector.tensor_copy(v_w[:, cols], tab_w[:].bitcast(U32).indirect(listed(g)))
-            nc.vector.tensor_copy(v_s[:, cols], tab_s[:].bitcast(U8).indirect(listed(g)))
-
-        def receptance(g):
-            cols = slice(g * GROUP, (g + 1) * GROUP)
-            for pair in range(N_TILES // 2):
-                z = psum_key.tile([P, 2, GROUP], F32, name="z", tag="key")
-                for i in range(2):
-                    n = 2 * pair + i
+        def receptance(j0, width):
+            cols = slice(j0, j0 + width)
+            share = BANK // width
+            for n0 in range(0, N_TILES, share):
+                z = key_bank([P, share, width])
+                for i in range(share):
+                    n = n0 + i
                     nc.tensor.matmul_mx(
                         out=z[:, i, :],
                         lhsT=wr_w[:, 2 * P * n : 2 * P * (n + 1)].bitcast(FP4X4),
@@ -135,23 +146,19 @@ def tile_list_rwkv_channel_mix_kernel(
                         start=True,
                         stop=True,
                     )
-                nc.scalar.activation(out=gate[g][:, 2 * pair : 2 * pair + 2, :], in_=z[:], func=ACT.Sigmoid)
+                nc.scalar.activation(out=gate[:, n0 : n0 + share, cols], in_=z[:], func=ACT.Sigmoid)
 
         def quantize_wk(b):
-            for half in range(2):
-                m0, m1 = half * P // 2, (half + 1) * P // 2
-                nc.vector.tensor_copy(
-                    out=wk_bf[b][:, :, m0:m1, :].rearrange("p t m j -> p m j t"),
-                    in_=wk_raw[b][:, :, PACK * m0 : PACK * m1].rearrange("p j (m t) -> p m j t", t=PACK),
-                )
+            wk_bf = ring.tile([P, PACK, P, PACK], BF16, name="wk_bf", tag="wk_bf", align_bytes=64, bufs=2)
+            dst = wk_bf[:].rearrange("p t m j -> p m j t")
+            src = wk_raw[b][:].rearrange("p j (m t) -> p m j t", t=PACK)
+            if b in GPSIMD_ROUND:
+                nc.gpsimd.tensor_scalar(out=dst, in0=src, scalar1=1.0, scalar2=0.0, op0=ALU.mult, op1=ALU.add)
+            else:
+                nc.vector.tensor_copy(out=dst, in_=src)
             nc.vector.quantize_mx(
-                out=wk_w[b][:].bitcast(FP8X4), scales=wk_s[b][:], in_=wk_bf[b][:].rearrange("p t m j -> p (t m j)")
+                out=wk_w[b][:].bitcast(FP8X4), scales=wk_s[b][:], in_=wk_bf[:].rearrange("p t m j -> p (t m j)")
             )
-
-        def gather_residuals():
-            for n in range(N_TILES):
-                for g in range(GROUPS):
-                    nc.vector.tensor_copy(resid[g][:, n, :], g_tab[n][:].indirect(listed(g)))
 
         relu_of = {}
 
@@ -162,7 +169,7 @@ def tile_list_rwkv_channel_mix_kernel(
             relu_of[s] = x
             for bank in range(width // BANK_TOKENS):
                 cols = slice(j0 + bank * BANK_TOKENS, j0 + (bank + 1) * BANK_TOKENS)
-                a = psum_key.tile([P, PACK, BANK_TOKENS], F32, name="a", tag="key")
+                a = key_bank([P, PACK, BANK_TOKENS])
                 for t in range(PACK):
                     nc.tensor.matmul_mx(
                         out=a[:, t, :],
@@ -184,9 +191,19 @@ def tile_list_rwkv_channel_mix_kernel(
             c, b = STEPS[s]
             j0, width = CHUNKS[c]
             cols = slice(j0, j0 + width)
-            h_bf = ring.tile([P, width, PACK], BF16, name="h_bf", tag="h_bf", align_bytes=64, bufs=SQUARE_BUFS)
+            if b == H_PASSES - 1 and c >= 1:
+                before, wide = CHUNKS[c - 1]
+                place = 4 * N_TILES * before + 2 * N_TILES * wide - PACK * width
+                h_bf = results.tile([P, width, PACK], BF16, name="h_last%d" % c, align_bytes=64, offset=place)
+            elif s in VECTOR_SQUARE and s <= HELD_SQUARE:
+                place = 2 * PACK * width * ((s - 1) % 3)
+                h_bf = shared.tile([P, width, PACK], BF16, name="h_held%d" % s, align_bytes=64, offset=place)
+            else:
+                h_bf = ring.tile([P, width, PACK], BF16, name="h_bf", tag="h_bf", align_bytes=64, bufs=SQUARE_BUFS)
             x = relu_of[s]
-            if s in VECTOR_SQUARE:
+            if s in GPSIMD_SQUARE:
+                nc.gpsimd.tensor_tensor(out=h_bf[:], in0=x[:], in1=x[:], op=ALU.mult)
+            elif s in VECTOR_SQUARE:
                 nc.vector.tensor_tensor(out=h_bf[:], in0=x[:], in1=x[:], op=ALU.mult)
             else:
                 nc.scalar.activation(out=h_bf[:], in_=x[:], func=ACT.Square)
@@ -197,85 +214,97 @@ def tile_list_rwkv_channel_mix_kernel(
             )
 
         y_of = {}
+        gated_of = {}
 
         def values(c, b):
             j0, width = CHUNKS[c]
             cols = slice(j0, j0 + width)
+            share = BANK // width
             if b == 0:
-                y_of[c] = [psum_value.tile([P, width], F32, name="y%d" % n, tag="y%d" % n) for n in range(N_TILES)]
+                y_of[c] = [value_bank([P, share, width]) for n in range(N_TILES // share)]
             for n in range(N_TILES):
                 nc.tensor.matmul_mx(
-                    out=y_of[c][n][:],
+                    out=y_of[c][n // share][:, n % share, :],
                     lhsT=wv_w[:, b, P * n : P * (n + 1)].bitcast(FP8X4),
                     lhsT_scale=wv_s[PACK * b : P, P * n : P * (n + 1)],
                     rhs=h_w[:, b, cols].bitcast(FP8X4),
                     rhs_scale=h_s[:, b, cols],
-                    start=(b == 0),
-                    stop=(b == H_PASSES - 1),
+                    start=(b == 0 and n % share == 0),
+                    stop=(b == H_PASSES - 1 and n % share == share - 1),
                 )
-
-        gated_of = {}
-
-        def gate_values(c, n):
-            j0, width = CHUNKS[c]
-            g, lo = divmod(j0, GROUP)
-            if n == 0:
-                gated_of[c] = ring.tile([P, N_TILES, width], F32, name="gated", tag="gated", bufs=GATED_BUFS)
-            nc.vector.tensor_tensor(
-                out=gated_of[c][:, n, :], in0=y_of[c][n][:], in1=gate[g][:, n, lo : lo + width], op=ALU.mult
-            )
 
         out_rows = out.rearrange("(n p) j -> p n j", p=P)
 
-        def add_and_store(c, n0, n1):
+        def finish(c):
             j0, width = CHUNKS[c]
-            g, lo = divmod(j0, GROUP)
-            result = keep.tile([P, n1 - n0, width], F32, name="result%d_%d" % (c, n0))
-            if c == GPSIMD_ADD_CHUNK:
-                for n in range(n0, n1):
-                    nc.gpsimd.tensor_tensor(
-                        out=result[:, n - n0, :],
-                        in0=gated_of[c][:, n, :],
-                        in1=resid[g][:, n, lo : lo + width],
-                        op=ALU.add,
-                    )
-            else:
+            cols = slice(j0, j0 + width)
+            share = BANK // width
+            half = N_TILES // 2
+            gated = [keep.tile([P, half, width], F32, name="gated%d_%d" % (c, i)) for i in range(2)]
+            gated_of[c] = gated
+            for i in range(2):
+                n0 = i * half
                 nc.vector.tensor_tensor(
-                    out=result[:], in0=gated_of[c][:, n0:n1, :], in1=resid[g][:, n0:n1, lo : lo + width], op=ALU.add
+                    out=gated[i][:],
+                    in0=y_of[c][n0 // share][:, n0 % share : n0 % share + half, :],
+                    in1=gate[:, n0 : n0 + half, cols],
+                    op=ALU.mult,
                 )
-            nc.sync.dma_start(out=out_rows[:, n0:n1, j0 : j0 + width], in_=result[:])
 
-        for g in range(GROUPS):
-            gather_tokens(g)
-            receptance(g)
-        quantize_wk(0)
+        def add_and_store(c):
+            j0, width = CHUNKS[c]
+            cols = slice(j0, j0 + width)
+            half = N_TILES // 2
+            gated = gated_of[c]
+            for i in range(2):
+                n0 = i * half
+                place = 4 * (N_TILES * j0 + n0 * width)
+                result = results.tile([P, half, width], F32, name="result%d_%d" % (c, i), align_bytes=64, offset=place)
+                if j0 < FUSED_TOKENS:
+                    for n in range(n0, n0 + half):
+                        nc.vector.tensor_tensor(
+                            out=result[:, n - n0, :],
+                            in0=g_tab[n][:].indirect(listed(j0, width)),
+                            in1=gated[i][:, n - n0, :],
+                            op=ALU.add,
+                        )
+                else:
+                    lo = j0 - FUSED_TOKENS
+                    nc.vector.tensor_tensor(
+                        out=result[:], in0=gated[i][:], in1=resid[:, n0 : n0 + half, lo : lo + width], op=ALU.add
+                    )
+                nc.sync.dma_start(out=out_rows[:, n0 : n0 + half, cols], in_=result[:])
+
+        nc.vector.tensor_copy(v_s[:], tab_s[:].bitcast(U8).indirect(offsets[:]))
+        for j0, width in GATHERS:
+            nc.vector.tensor_copy(v_w[:, j0 : j0 + width], tab_w[:].bitcast(U32).indirect(listed(j0, width)))
+            receptance(j0, width)
+        for load in LOADS:
+            if load[0] == "k":
+                quantize_wk(int(load[1]))
+            elif load[0] == "g":
+                n = int(load[1])
+                nc.vector.tensor_copy(resid[:, n, :], g_tab[n][:].indirect(listed(FUSED_TOKENS, S - FUSED_TOKENS)))
         keys(0)
 
-        last = len(CHUNKS) - 1
-        squared = set()
-        open_chunk = 0
-        passes_done = 0
+        waiting = []
+        summed = []
         for s in range(len(STEPS)):
-            if s + 1 < H_PASSES:
-                quantize_wk(s + 1)
-            if s + 1 == H_PASSES - 1:
-                gather_residuals()
             if s + 1 < len(STEPS):
                 keys(s + 1)
             square(s)
-            squared.add(STEPS[s])
-            while open_chunk <= last and (open_chunk, passes_done) in squared:
-                values(open_chunk, passes_done)
-                passes_done += 1
-                if passes_done == H_PASSES:
-                    if open_chunk < last:
-                        for n in range(N_TILES):
-                            gate_values(open_chunk, n)
-                    open_chunk += 1
-                    passes_done = 0
-
-        for c in range(last):
-            add_and_store(c, 0, N_TILES)
-        for n in range(N_TILES):
-            gate_values(last, n)
-            add_and_store(last, n, n + 1)
+            waiting.append(STEPS[s])
+            waiting.sort()
+            for turn in range(PASSES_A_STEP if s >= FIRST_VALUE_STEP else 0):
+                if waiting:
+                    c, b = waiting.pop(0)
+                    values(c, b)
+                    if b == H_PASSES - 1:
+                        summed.append((s + FINISH_LAG, c))
+            while summed and (summed[0][0] <= s or s == len(STEPS) - 1):
+                c = summed.pop(0)[1]
+                if c >= 1:
+                    add_and_store(c - 1)
+                finish(c)
+                if c == len(CHUNKS) - 1:
+                    add_and_store(c)

@@ -91,12 +91,10 @@ def tile_list_rwkv_channel_mix_kernel(
         nc.sync.dma_start(offsets[:], offs)
         nc.sync.dma_start(out=wr_w[:].bitcast(I32), in_=wr_words[0].bitcast(I32))
         for r in range(PACK):
-            queue = nc.sync if r < PACK // 2 else nc.scalar
-            queue.dma_start(out=tab_s[r:P:QUADRANT, :], in_=tab_scales[0, r:BLOCKS:PACK, :].bitcast(I32))
+            nc.sync.dma_start(out=tab_s[r:P:QUADRANT, :], in_=tab_scales[0, r:BLOCKS:PACK, :].bitcast(I32))
         nc.sync.dma_start(out=tab_w[:], in_=tab_words[0].rearrange("p t i -> p (t i)").bitcast(I32))
         for r in range(PACK):
-            queue = nc.sync if r < PACK // 2 else nc.scalar
-            queue.dma_start(out=wr_s[r:P:QUADRANT, :].bitcast(I32), in_=wr_scales[0, r:BLOCKS:PACK, :].bitcast(I32))
+            nc.sync.dma_start(out=wr_s[r:P:QUADRANT, :].bitcast(I32), in_=wr_scales[0, r:BLOCKS:PACK, :].bitcast(I32))
 
         wk_rows = wk.rearrange("(p j) c -> p j c", j=PACK)
         wk_raw = [keep.tile([P, PACK, PASS], F32, name="wk_raw%d" % b) for b in range(H_PASSES - 1)]

@@ -30,27 +30,22 @@ BANK_TOKENS = BANK // PACK
 
 GATHERS = [(0, 256), (256, 256), (512, 512)]
 CHUNKS = [(0, 256), (256, 256), (512, 256), (768, 128), (896, 128)]
+LAST_CHUNK = len(CHUNKS) - 1
+FUSED_TOKENS = 768
 WOVEN_CHUNKS = 2
+WOVEN_STEPS = WOVEN_CHUNKS * H_PASSES
 STEPS = [(c, b) for b in range(H_PASSES) for c in range(WOVEN_CHUNKS)] + [
     (c, b) for c in range(WOVEN_CHUNKS, len(CHUNKS)) for b in range(H_PASSES)
 ]
-VECTOR_SQUARE = {1,2,3,4,5}
-VECTOR_RELU = set()
-LOADS = ["k0", "s", "k1", "k2", "k3", "v", "g0", "g1", "g2", "g3"]
+EARLY_SQUARES = range(1, 5)
+VECTOR_SQUARES = set(EARLY_SQUARES) | {WOVEN_STEPS - 1}
+HELD_PLACES = 3
 
-FIRST_VALUE_STEP = 0
-PASSES_A_STEP = 2
-GPSIMD_ROUND = set()
-GPSIMD_SQUARE = set()
-RESID_GATHER = 512
-GPSIMD_ADD = set()
-FINISH_LAG = 0
-FUSED_TOKENS = 512
-HELD_SQUARE = 5
+ROUNDED_BUFS = 2
 RELU_BUFS = 7
-SQUARE_BUFS = 6
+SQUARE_BUFS = 7
 KEY_BANKS = 4
-VALUE_BANKS = 8 - KEY_BANKS
+VALUE_BANKS = 4
 
 
 def tile_list_rwkv_channel_mix_kernel(
@@ -59,22 +54,18 @@ def tile_list_rwkv_channel_mix_kernel(
     nc = tc.nc
     with ExitStack() as ctx:
         keep = ctx.enter_context(tc.tile_pool(name="keep", bufs=1))
-        ring = ctx.enter_context(tc.tile_pool(name="ring", bufs=2))
-        shared = ctx.enter_context(tc.tile_pool(name="shared", bufs=1))
+        ring = ctx.enter_context(tc.tile_pool(name="ring", bufs=ROUNDED_BUFS))
+        after_wk = ctx.enter_context(tc.tile_pool(name="after_wk", bufs=1))
         results = ctx.enter_context(tc.tile_pool(name="results", bufs=1))
         psum = ctx.enter_context(tc.psum_pool(name="psum", bufs=1))
-        key_tiles = []
-        value_tiles = []
 
-        def key_bank(shape):
-            turn = len(key_tiles)
-            key_tiles.append(turn)
-            return psum.tile(shape, F32, name="key%d" % turn, offset=BANK_BYTES * (turn % KEY_BANKS))
+        key_turns = []
+        value_turns = []
 
-        def value_bank(shape):
-            turn = len(value_tiles)
-            value_tiles.append(turn)
-            return psum.tile(shape, F32, name="value%d" % turn, offset=BANK_BYTES * (KEY_BANKS + turn % VALUE_BANKS))
+        def next_bank(turns, first, count, shape):
+            turn = len(turns)
+            turns.append(turn)
+            return psum.tile(shape, F32, name="bank%d_%d" % (first, turn), offset=BANK_BYTES * (first + turn % count))
 
         offsets = keep.tile([P, S // LIST_ROWS], U16, name="offsets")
         tab_w = keep.tile([P, T], I32, name="tab_w", align_bytes=64)
@@ -98,23 +89,18 @@ def tile_list_rwkv_channel_mix_kernel(
 
         wk_rows = wk.rearrange("(p j) c -> p j c", j=PACK)
         wk_raw = [keep.tile([P, PACK, PASS], F32, name="wk_raw%d" % b) for b in range(H_PASSES - 1)]
-        wk_raw.append(shared.tile([P, PACK, PASS], F32, name="wk_raw_last", align_bytes=64, offset=0))
+        wk_raw.append(after_wk.tile([P, PACK, PASS], F32, name="wk_raw_last", align_bytes=64, offset=0))
         g_tab = [keep.tile([P, T], F32, name="g_tab%d" % n) for n in range(N_TILES)]
-        for load in LOADS:
-            if load[0] == "k":
-                b = int(load[1])
-                nc.sync.dma_start(out=wk_raw[b][:], in_=wk_rows[:, :, b * PASS : (b + 1) * PASS])
-            elif load[0] == "g":
-                n = int(load[1])
-                nc.sync.dma_start(out=g_tab[n][:], in_=gT[n * P : (n + 1) * P, :])
-            elif load[0] == "v":
-                nc.sync.dma_start(out=wv_w[:], in_=wv_words.rearrange("a p c i -> p a (c i)").bitcast(I32))
-            else:
-                for q in range(P // QUADRANT):
-                    nc.sync.dma_start(
-                        out=wv_s[QUADRANT * q : QUADRANT * q + PACK * H_PASSES, :].bitcast(I32),
-                        in_=wv_scales[:, PACK * q : PACK * (q + 1), :].bitcast(I32),
-                    )
+        for b in range(H_PASSES):
+            nc.sync.dma_start(out=wk_raw[b][:], in_=wk_rows[:, :, b * PASS : (b + 1) * PASS])
+        for q in range(P // QUADRANT):
+            nc.sync.dma_start(
+                out=wv_s[QUADRANT * q : QUADRANT * q + PACK * H_PASSES, :].bitcast(I32),
+                in_=wv_scales[:, PACK * q : PACK * (q + 1), :].bitcast(I32),
+            )
+        nc.sync.dma_start(out=wv_w[:], in_=wv_words.rearrange("a p c i -> p a (c i)").bitcast(I32))
+        for n in range(N_TILES):
+            nc.sync.dma_start(out=g_tab[n][:], in_=gT[n * P : (n + 1) * P, :])
 
         v_w = keep.tile([P, S], U32, name="v_w", align_bytes=64)
         v_s = keep.tile([P, S], U8, name="v_s", align_bytes=64)
@@ -123,7 +109,8 @@ def tile_list_rwkv_channel_mix_kernel(
         gate = keep.tile([P, N_TILES, S], F32, name="gate")
         resid = keep.tile([P, N_TILES, S - FUSED_TOKENS], F32, name="resid")
         h_w = keep.tile([P, H_PASSES, S], U32, name="h_w", align_bytes=64)
-        h_s = shared.tile([P, H_PASSES, S], U8, name="h_s", align_bytes=64, offset=6 * S)
+        held_bytes = 2 * PACK * CHUNKS[0][1]
+        h_s = after_wk.tile([P, H_PASSES, S], U8, name="h_s", align_bytes=64, offset=HELD_PLACES * held_bytes)
 
         def listed(j0, width):
             return offsets[:, j0 // LIST_ROWS : (j0 + width) // LIST_ROWS]
@@ -132,7 +119,7 @@ def tile_list_rwkv_channel_mix_kernel(
             cols = slice(j0, j0 + width)
             share = BANK // width
             for n0 in range(0, N_TILES, share):
-                z = key_bank([P, share, width])
+                z = next_bank(key_turns, 0, KEY_BANKS, [P, share, width])
                 for i in range(share):
                     n = n0 + i
                     nc.tensor.matmul_mx(
@@ -147,13 +134,11 @@ def tile_list_rwkv_channel_mix_kernel(
                 nc.scalar.activation(out=gate[:, n0 : n0 + share, cols], in_=z[:], func=ACT.Sigmoid)
 
         def quantize_wk(b):
-            wk_bf = ring.tile([P, PACK, P, PACK], BF16, name="wk_bf", tag="wk_bf", align_bytes=64, bufs=2)
-            dst = wk_bf[:].rearrange("p t m j -> p m j t")
-            src = wk_raw[b][:].rearrange("p j (m t) -> p m j t", t=PACK)
-            if b in GPSIMD_ROUND:
-                nc.gpsimd.tensor_scalar(out=dst, in0=src, scalar1=1.0, scalar2=0.0, op0=ALU.mult, op1=ALU.add)
-            else:
-                nc.vector.tensor_copy(out=dst, in_=src)
+            wk_bf = ring.tile([P, PACK, P, PACK], BF16, name="wk_bf", tag="wk_bf", align_bytes=64)
+            nc.vector.tensor_copy(
+                out=wk_bf[:].rearrange("p t m j -> p m j t"),
+                in_=wk_raw[b][:].rearrange("p j (m t) -> p m j t", t=PACK),
+            )
             nc.vector.quantize_mx(
                 out=wk_w[b][:].bitcast(FP8X4), scales=wk_s[b][:], in_=wk_bf[:].rearrange("p t m j -> p (t m j)")
             )
@@ -167,7 +152,7 @@ def tile_list_rwkv_channel_mix_kernel(
             relu_of[s] = x
             for bank in range(width // BANK_TOKENS):
                 cols = slice(j0 + bank * BANK_TOKENS, j0 + (bank + 1) * BANK_TOKENS)
-                a = key_bank([P, PACK, BANK_TOKENS])
+                a = next_bank(key_turns, 0, KEY_BANKS, [P, PACK, BANK_TOKENS])
                 for t in range(PACK):
                     nc.tensor.matmul_mx(
                         out=a[:, t, :],
@@ -178,12 +163,11 @@ def tile_list_rwkv_channel_mix_kernel(
                         start=True,
                         stop=True,
                     )
-                dst = x[:, bank * BANK_TOKENS : (bank + 1) * BANK_TOKENS, :]
-                src = a[:].rearrange("p t j -> p j t")
-                if (s, bank) in VECTOR_RELU:
-                    nc.vector.tensor_scalar(out=dst, in0=src, scalar1=0.0, scalar2=None, op0=ALU.max)
-                else:
-                    nc.scalar.activation(out=dst, in_=src, func=ACT.Relu)
+                nc.scalar.activation(
+                    out=x[:, bank * BANK_TOKENS : (bank + 1) * BANK_TOKENS, :],
+                    in_=a[:].rearrange("p t j -> p j t"),
+                    func=ACT.Relu,
+                )
 
         def square(s):
             c, b = STEPS[s]
@@ -191,17 +175,17 @@ def tile_list_rwkv_channel_mix_kernel(
             cols = slice(j0, j0 + width)
             if b == H_PASSES - 1 and c >= 1:
                 before, wide = CHUNKS[c - 1]
-                place = 4 * N_TILES * before + 2 * N_TILES * wide - PACK * width
-                h_bf = results.tile([P, width, PACK], BF16, name="h_last%d" % c, align_bytes=64, offset=place)
-            elif s in VECTOR_SQUARE and s <= HELD_SQUARE:
-                place = 2 * PACK * width * ((s - 1) % 3)
-                h_bf = shared.tile([P, width, PACK], BF16, name="h_held%d" % s, align_bytes=64, offset=place)
+                middle = 4 * N_TILES * before + 2 * N_TILES * wide
+                h_bf = results.tile(
+                    [P, width, PACK], BF16, name="h_last%d" % c, align_bytes=64, offset=middle - PACK * width
+                )
+            elif s in EARLY_SQUARES:
+                place = held_bytes * ((s - EARLY_SQUARES.start) % HELD_PLACES)
+                h_bf = after_wk.tile([P, width, PACK], BF16, name="h_held%d" % s, align_bytes=64, offset=place)
             else:
                 h_bf = ring.tile([P, width, PACK], BF16, name="h_bf", tag="h_bf", align_bytes=64, bufs=SQUARE_BUFS)
             x = relu_of[s]
-            if s in GPSIMD_SQUARE:
-                nc.gpsimd.tensor_tensor(out=h_bf[:], in0=x[:], in1=x[:], op=ALU.mult)
-            elif s in VECTOR_SQUARE:
+            if s in VECTOR_SQUARES:
                 nc.vector.tensor_tensor(out=h_bf[:], in0=x[:], in1=x[:], op=ALU.mult)
             else:
                 nc.scalar.activation(out=h_bf[:], in_=x[:], func=ACT.Square)
@@ -213,13 +197,19 @@ def tile_list_rwkv_channel_mix_kernel(
 
         y_of = {}
         gated_of = {}
+        half = N_TILES // 2
+
+        def tiles_a_bank(c):
+            return half if c == LAST_CHUNK else BANK // CHUNKS[c][1]
 
         def values(c, b):
             j0, width = CHUNKS[c]
             cols = slice(j0, j0 + width)
-            share = BANK // width
+            share = tiles_a_bank(c)
             if b == 0:
-                y_of[c] = [value_bank([P, share, width]) for n in range(N_TILES // share)]
+                y_of[c] = [
+                    next_bank(value_turns, KEY_BANKS, VALUE_BANKS, [P, share, width]) for i in range(N_TILES // share)
+                ]
             for n in range(N_TILES):
                 nc.tensor.matmul_mx(
                     out=y_of[c][n // share][:, n % share, :],
@@ -233,11 +223,10 @@ def tile_list_rwkv_channel_mix_kernel(
 
         out_rows = out.rearrange("(n p) j -> p n j", p=P)
 
-        def finish(c):
+        def gate_values(c):
             j0, width = CHUNKS[c]
             cols = slice(j0, j0 + width)
-            share = BANK // width
-            half = N_TILES // 2
+            share = tiles_a_bank(c)
             gated = [keep.tile([P, half, width], F32, name="gated%d_%d" % (c, i)) for i in range(2)]
             gated_of[c] = gated
             for i in range(2):
@@ -252,7 +241,6 @@ def tile_list_rwkv_channel_mix_kernel(
         def add_and_store(c):
             j0, width = CHUNKS[c]
             cols = slice(j0, j0 + width)
-            half = N_TILES // 2
             gated = gated_of[c]
             for i in range(2):
                 n0 = i * half
@@ -277,32 +265,23 @@ def tile_list_rwkv_channel_mix_kernel(
         for j0, width in GATHERS:
             nc.vector.tensor_copy(v_w[:, j0 : j0 + width], tab_w[:].bitcast(U32).indirect(listed(j0, width)))
             receptance(j0, width)
-        for load in LOADS:
-            if load[0] == "k":
-                quantize_wk(int(load[1]))
-            elif load[0] == "g":
-                n = int(load[1])
-                nc.vector.tensor_copy(resid[:, n, :], g_tab[n][:].indirect(listed(FUSED_TOKENS, S - FUSED_TOKENS)))
-        keys(0)
+        for b in range(H_PASSES):
+            quantize_wk(b)
+        for n in range(N_TILES):
+            nc.vector.tensor_copy(resid[:, n, :], g_tab[n][:].indirect(listed(FUSED_TOKENS, S - FUSED_TOKENS)))
 
-        waiting = []
-        summed = []
-        for s in range(len(STEPS)):
+        def finish(c):
+            if c >= 1:
+                add_and_store(c - 1)
+            gate_values(c)
+
+        keys(0)
+        for s, (c, b) in enumerate(STEPS):
             if s + 1 < len(STEPS):
                 keys(s + 1)
             square(s)
-            waiting.append(STEPS[s])
-            waiting.sort()
-            for turn in range(PASSES_A_STEP if s >= FIRST_VALUE_STEP else 0):
-                if waiting:
-                    c, b = waiting.pop(0)
-                    values(c, b)
-                    if b == H_PASSES - 1:
-                        summed.append((s + FINISH_LAG, c))
-            while summed and (summed[0][0] <= s or s == len(STEPS) - 1):
-                c = summed.pop(0)[1]
-                if c >= 1:
-                    add_and_store(c - 1)
-                finish(c)
-                if c == len(CHUNKS) - 1:
-                    add_and_store(c)
+            values(c, b)
+            if s >= 1 and STEPS[s - 1][1] == H_PASSES - 1:
+                finish(STEPS[s - 1][0])
+        finish(LAST_CHUNK)
+        add_and_store(LAST_CHUNK)

@@ -37,13 +37,13 @@ WOVEN_STEPS = WOVEN_CHUNKS * H_PASSES
 STEPS = [(c, b) for b in range(H_PASSES) for c in range(WOVEN_CHUNKS)] + [
     (c, b) for c in range(WOVEN_CHUNKS, len(CHUNKS)) for b in range(H_PASSES)
 ]
-EARLY_SQUARES = range(1, 5)
-VECTOR_SQUARES = set(EARLY_SQUARES) | {WOVEN_STEPS - 1}
-HELD_PLACES = 3
+VECTOR_RELU_STEPS = range(WOVEN_STEPS // 2, WOVEN_STEPS)
+VECTOR_RELU_EXTRA = (WOVEN_STEPS, 1)
+GPSIMD_SQUARES = range(1, 3)
 
 ROUNDED_BUFS = 2
-RELU_BUFS = 7
-SQUARE_BUFS = 7
+RELU_BUFS = 5
+SQUARE_BUFS = 8
 KEY_BANKS = 4
 VALUE_BANKS = 4
 
@@ -56,6 +56,8 @@ def tile_list_rwkv_channel_mix_kernel(
         keep = ctx.enter_context(tc.tile_pool(name="keep", bufs=1))
         ring = ctx.enter_context(tc.tile_pool(name="ring", bufs=ROUNDED_BUFS))
         after_wk = ctx.enter_context(tc.tile_pool(name="after_wk", bufs=1))
+        after_square = ctx.enter_context(tc.tile_pool(name="after_square", bufs=1))
+        after_round = ctx.enter_context(tc.tile_pool(name="after_round", bufs=1))
         results = ctx.enter_context(tc.tile_pool(name="results", bufs=1))
         psum = ctx.enter_context(tc.psum_pool(name="psum", bufs=1))
 
@@ -109,8 +111,7 @@ def tile_list_rwkv_channel_mix_kernel(
         gate = keep.tile([P, N_TILES, S], F32, name="gate")
         resid = keep.tile([P, N_TILES, S - FUSED_TOKENS], F32, name="resid")
         h_w = keep.tile([P, H_PASSES, S], U32, name="h_w", align_bytes=64)
-        held_bytes = 2 * PACK * CHUNKS[0][1]
-        h_s = after_wk.tile([P, H_PASSES, S], U8, name="h_s", align_bytes=64, offset=HELD_PLACES * held_bytes)
+        h_s = after_square.tile([P, H_PASSES, S], U8, name="h_s", align_bytes=64, offset=0)
 
         def listed(j0, width):
             return offsets[:, j0 // LIST_ROWS : (j0 + width) // LIST_ROWS]
@@ -134,7 +135,10 @@ def tile_list_rwkv_channel_mix_kernel(
                 nc.scalar.activation(out=gate[:, n0 : n0 + share, cols], in_=z[:], func=ACT.Sigmoid)
 
         def quantize_wk(b):
-            wk_bf = ring.tile([P, PACK, P, PACK], BF16, name="wk_bf", tag="wk_bf", align_bytes=64)
+            if b == H_PASSES - 1:
+                wk_bf = after_round.tile([P, PACK, P, PACK], BF16, name="wk_bf_last", align_bytes=64, offset=0)
+            else:
+                wk_bf = ring.tile([P, PACK, P, PACK], BF16, name="wk_bf", tag="wk_bf", align_bytes=64)
             nc.vector.tensor_copy(
                 out=wk_bf[:].rearrange("p t m j -> p m j t"),
                 in_=wk_raw[b][:].rearrange("p j (m t) -> p m j t", t=PACK),
@@ -144,11 +148,18 @@ def tile_list_rwkv_channel_mix_kernel(
             )
 
         relu_of = {}
+        h_of = {}
 
         def keys(s):
             c, b = STEPS[s]
             j0, width = CHUNKS[c]
-            x = ring.tile([P, width, PACK], F32, name="x", tag="x", bufs=RELU_BUFS)
+            if s == GPSIMD_SQUARES[-1]:
+                x = after_square.tile([P, width, PACK], F32, name="x_gpsimd", align_bytes=64, offset=0)
+            elif s in VECTOR_RELU_STEPS and b < H_PASSES - 1:
+                place = 4 * PACK * width * c
+                x = after_wk.tile([P, width, PACK], F32, name="x_held%d" % s, align_bytes=64, offset=place)
+            else:
+                x = ring.tile([P, width, PACK], F32, name="x", tag="x", bufs=RELU_BUFS)
             relu_of[s] = x
             for bank in range(width // BANK_TOKENS):
                 cols = slice(j0 + bank * BANK_TOKENS, j0 + (bank + 1) * BANK_TOKENS)
@@ -163,36 +174,40 @@ def tile_list_rwkv_channel_mix_kernel(
                         start=True,
                         stop=True,
                     )
-                nc.scalar.activation(
-                    out=x[:, bank * BANK_TOKENS : (bank + 1) * BANK_TOKENS, :],
-                    in_=a[:].rearrange("p t j -> p j t"),
-                    func=ACT.Relu,
-                )
+                dst = x[:, bank * BANK_TOKENS : (bank + 1) * BANK_TOKENS, :]
+                src = a[:].rearrange("p t j -> p j t")
+                if s in VECTOR_RELU_STEPS or (s, bank) == VECTOR_RELU_EXTRA:
+                    nc.vector.tensor_scalar(out=dst, in0=src, scalar1=0.0, scalar2=None, op0=ALU.max)
+                else:
+                    nc.scalar.activation(out=dst, in_=src, func=ACT.Relu)
 
         def square(s):
             c, b = STEPS[s]
-            j0, width = CHUNKS[c]
-            cols = slice(j0, j0 + width)
+            width = CHUNKS[c][1]
             if b == H_PASSES - 1 and c >= 1:
                 before, wide = CHUNKS[c - 1]
-                middle = 4 * N_TILES * before + 2 * N_TILES * wide
-                h_bf = results.tile(
-                    [P, width, PACK], BF16, name="h_last%d" % c, align_bytes=64, offset=middle - PACK * width
-                )
-            elif s in EARLY_SQUARES:
-                place = held_bytes * ((s - EARLY_SQUARES.start) % HELD_PLACES)
-                h_bf = after_wk.tile([P, width, PACK], BF16, name="h_held%d" % s, align_bytes=64, offset=place)
+                place = 4 * N_TILES * before + 2 * N_TILES * wide - (PACK * width if c == LAST_CHUNK else 0)
+                h_bf = results.tile([P, width, PACK], BF16, name="h_last%d" % c, align_bytes=64, offset=place)
+            elif s in GPSIMD_SQUARES:
+                place = 2 * PACK * width * (s - GPSIMD_SQUARES.start)
+                h_bf = after_round.tile([P, width, PACK], BF16, name="h_gpsimd%d" % s, align_bytes=64, offset=place)
             else:
                 h_bf = ring.tile([P, width, PACK], BF16, name="h_bf", tag="h_bf", align_bytes=64, bufs=SQUARE_BUFS)
             x = relu_of[s]
-            if s in VECTOR_SQUARES:
-                nc.vector.tensor_tensor(out=h_bf[:], in0=x[:], in1=x[:], op=ALU.mult)
+            if s in GPSIMD_SQUARES:
+                nc.gpsimd.tensor_tensor(out=h_bf[:], in0=x[:], in1=x[:], op=ALU.mult)
             else:
                 nc.scalar.activation(out=h_bf[:], in_=x[:], func=ACT.Square)
+            h_of[s] = h_bf
+
+        def quantize_h(s):
+            c, b = STEPS[s]
+            j0, width = CHUNKS[c]
+            cols = slice(j0, j0 + width)
             nc.vector.quantize_mx(
                 out=h_w[:, b, cols].bitcast(FP8X4),
                 scales=h_s[:, b, cols],
-                in_=h_bf[:].rearrange("p j t -> p (j t)"),
+                in_=h_of[s][:].rearrange("p j t -> p (j t)"),
             )
 
         y_of = {}
@@ -276,12 +291,22 @@ def tile_list_rwkv_channel_mix_kernel(
             gate_values(c)
 
         keys(0)
-        for s, (c, b) in enumerate(STEPS):
+        for s in range(WOVEN_STEPS):
+            keys(s + 1)
+            square(s)
+        for c in range(WOVEN_CHUNKS):
+            for b in range(H_PASSES):
+                quantize_h(STEPS.index((c, b)))
+                values(c, b)
+        finish(0)
+        for s in range(WOVEN_STEPS, len(STEPS)):
             if s + 1 < len(STEPS):
                 keys(s + 1)
             square(s)
-            values(c, b)
-            if s >= 1 and STEPS[s - 1][1] == H_PASSES - 1:
-                finish(STEPS[s - 1][0])
+            quantize_h(s)
+            values(*STEPS[s])
+            c, b = STEPS[s - 1]
+            if b == H_PASSES - 1:
+                finish(c)
         finish(LAST_CHUNK)
         add_and_store(LAST_CHUNK)

@@ -40,6 +40,7 @@ STEPS = [(c, b) for b in range(H_PASSES) for c in range(WOVEN_CHUNKS)] + [
 VECTOR_RELU_STEPS = range(WOVEN_STEPS // 2, WOVEN_STEPS)
 VECTOR_RELU_EXTRA = (WOVEN_STEPS, 1)
 GPSIMD_SQUARES = range(1, 3)
+GPSIMD_LAST_TOKENS = 160
 
 ROUNDED_BUFS = 2
 RELU_BUFS = 5
@@ -194,7 +195,11 @@ def tile_list_rwkv_channel_mix_kernel(
             else:
                 h_bf = ring.tile([P, width, PACK], BF16, name="h_bf", tag="h_bf", align_bytes=64, bufs=SQUARE_BUFS)
             x = relu_of[s]
-            if s in GPSIMD_SQUARES:
+            if s == GPSIMD_SQUARES[-1]:
+                part = GPSIMD_LAST_TOKENS
+                nc.gpsimd.tensor_tensor(out=h_bf[:, :part, :], in0=x[:, :part, :], in1=x[:, :part, :], op=ALU.mult)
+                nc.scalar.activation(out=h_bf[:, part:, :], in_=x[:, part:, :], func=ACT.Square)
+            elif s in GPSIMD_SQUARES:
                 nc.gpsimd.tensor_tensor(out=h_bf[:], in0=x[:], in1=x[:], op=ALU.mult)
             else:
                 nc.scalar.activation(out=h_bf[:], in_=x[:], func=ACT.Square)

@@ -32,18 +32,19 @@ GATHERS = [(0, 256), (256, 256), (512, 512)]
 CHUNKS = [(0, 256), (256, 256), (512, 256), (768, 128), (896, 128)]
 LAST_CHUNK = len(CHUNKS) - 1
 FUSED_TOKENS = 768
-WOVEN_CHUNKS = 2
-WOVEN_STEPS = WOVEN_CHUNKS * H_PASSES
-STEPS = [(c, b) for b in range(H_PASSES) for c in range(WOVEN_CHUNKS)] + [
-    (c, b) for c in range(WOVEN_CHUNKS, len(CHUNKS)) for b in range(H_PASSES)
-]
-VECTOR_RELU_STEPS = range(WOVEN_STEPS // 2, WOVEN_STEPS)
-VECTOR_RELU_EXTRA = (WOVEN_STEPS, 1)
-GPSIMD_SQUARES = range(1, 3)
-GPSIMD_LAST_TOKENS = 160
+WIDE = 3
+EARLY_BLOCKS = 2
+STEPS = (
+    [(c, b) for b in range(EARLY_BLOCKS) for c in range(WIDE)]
+    + [(c, b) for c in range(WIDE) for b in range(EARLY_BLOCKS, H_PASSES)]
+    + [(c, b) for c in range(WIDE, len(CHUNKS)) for b in range(H_PASSES)]
+)
+VECTOR_STEPS = {1: [(2, 0)], 3: [(0, 2)]}
+LATE_STEPS = [(3, 0)]
+HOLDS = {(1, 3): (0, 1), (2, 3): (1, 1), (3, 3): (2, 0), (4, 3): (2, 1)}
+GPSIMD_SQUARES = {1: ((0, 0), 192), 3: ((1, 1), 192)}
 
-ROUNDED_BUFS = 2
-RELU_BUFS = 5
+RELU_BUFS = 4
 SQUARE_BUFS = 8
 KEY_BANKS = 4
 VALUE_BANKS = 4
@@ -55,10 +56,9 @@ def tile_list_rwkv_channel_mix_kernel(
     nc = tc.nc
     with ExitStack() as ctx:
         keep = ctx.enter_context(tc.tile_pool(name="keep", bufs=1))
-        ring = ctx.enter_context(tc.tile_pool(name="ring", bufs=ROUNDED_BUFS))
-        after_wk = ctx.enter_context(tc.tile_pool(name="after_wk", bufs=1))
-        after_square = ctx.enter_context(tc.tile_pool(name="after_square", bufs=1))
-        after_round = ctx.enter_context(tc.tile_pool(name="after_round", bufs=1))
+        ring = ctx.enter_context(tc.tile_pool(name="ring", bufs=RELU_BUFS))
+        raw_pool = ctx.enter_context(tc.tile_pool(name="raw_pool", bufs=1))
+        round_pool = ctx.enter_context(tc.tile_pool(name="round_pool", bufs=1))
         results = ctx.enter_context(tc.tile_pool(name="results", bufs=1))
         psum = ctx.enter_context(tc.psum_pool(name="psum", bufs=1))
 
@@ -91,8 +91,12 @@ def tile_list_rwkv_channel_mix_kernel(
             nc.sync.dma_start(out=wr_s[r:P:QUADRANT, :].bitcast(I32), in_=wr_scales[0, r:BLOCKS:PACK, :].bitcast(I32))
 
         wk_rows = wk.rearrange("(p j) c -> p j c", j=PACK)
-        wk_raw = [keep.tile([P, PACK, PASS], F32, name="wk_raw%d" % b) for b in range(H_PASSES - 1)]
-        wk_raw.append(after_wk.tile([P, PACK, PASS], F32, name="wk_raw_last", align_bytes=64, offset=0))
+        RAW_BYTES = 4 * PACK * PASS
+        ROUND_BYTES = 2 * PACK * PASS
+        wk_raw = [
+            raw_pool.tile([P, PACK, PASS], F32, name="wk_raw%d" % b, align_bytes=64, offset=RAW_BYTES * b)
+            for b in range(H_PASSES)
+        ]
         g_tab = [keep.tile([P, T], F32, name="g_tab%d" % n) for n in range(N_TILES)]
         for b in range(H_PASSES):
             nc.sync.dma_start(out=wk_raw[b][:], in_=wk_rows[:, :, b * PASS : (b + 1) * PASS])
@@ -112,15 +116,15 @@ def tile_list_rwkv_channel_mix_kernel(
         gate = keep.tile([P, N_TILES, S], F32, name="gate")
         resid = keep.tile([P, N_TILES, S - FUSED_TOKENS], F32, name="resid")
         h_w = keep.tile([P, H_PASSES, S], U32, name="h_w", align_bytes=64)
-        h_s = after_square.tile([P, H_PASSES, S], U8, name="h_s", align_bytes=64, offset=0)
+        h_s = keep.tile([P, H_PASSES, S], U8, name="h_s", align_bytes=64)
 
         def listed(j0, width):
             return offsets[:, j0 // LIST_ROWS : (j0 + width) // LIST_ROWS]
 
-        def receptance(j0, width):
+        def receptance(j0, width, tiles):
             cols = slice(j0, j0 + width)
             share = BANK // width
-            for n0 in range(0, N_TILES, share):
+            for n0 in range(tiles.start, tiles.stop, share):
                 z = next_bank(key_turns, 0, KEY_BANKS, [P, share, width])
                 for i in range(share):
                     n = n0 + i
@@ -135,84 +139,119 @@ def tile_list_rwkv_channel_mix_kernel(
                     )
                 nc.scalar.activation(out=gate[:, n0 : n0 + share, cols], in_=z[:], func=ACT.Sigmoid)
 
+        wk_bf = {}
+
+        def round_wk(b):
+            for u in range(0, PACK, 2):
+                wk_bf[(b, u)] = round_pool.tile(
+                    [P, 2, P, PACK],
+                    BF16,
+                    name="wk_bf%d_%d" % (b, u),
+                    align_bytes=64,
+                    offset=ROUND_BYTES * b + ROUND_BYTES // PACK * u,
+                )
+                nc.vector.tensor_copy(
+                    out=wk_bf[(b, u)][:].rearrange("p t m j -> p m j t"),
+                    in_=wk_raw[b][:].rearrange("p j (m t) -> p m j t", t=PACK)[:, :, :, u : u + 2],
+                )
+
         def quantize_wk(b):
-            if b == H_PASSES - 1:
-                wk_bf = after_round.tile([P, PACK, P, PACK], BF16, name="wk_bf_last", align_bytes=64, offset=0)
-            else:
-                wk_bf = ring.tile([P, PACK, P, PACK], BF16, name="wk_bf", tag="wk_bf", align_bytes=64)
-            nc.vector.tensor_copy(
-                out=wk_bf[:].rearrange("p t m j -> p m j t"),
-                in_=wk_raw[b][:].rearrange("p j (m t) -> p m j t", t=PACK),
-            )
-            nc.vector.quantize_mx(
-                out=wk_w[b][:].bitcast(FP8X4), scales=wk_s[b][:], in_=wk_bf[:].rearrange("p t m j -> p (t m j)")
-            )
+            for u in range(0, PACK, 2):
+                cols = slice(P * u, P * (u + 2))
+                nc.vector.quantize_mx(
+                    out=wk_w[b][:, cols].bitcast(FP8X4),
+                    scales=wk_s[b][:, cols],
+                    in_=wk_bf[(b, u)][:].rearrange("p t m j -> p (t m j)"),
+                )
+
+        def key_bank(c, b, bank, a):
+            j0 = CHUNKS[c][0] + bank * BANK_TOKENS
+            cols = slice(j0, j0 + BANK_TOKENS)
+            for t in range(PACK):
+                nc.tensor.matmul_mx(
+                    out=a[:, t, :],
+                    lhsT=wk_w[b][:, P * t : P * (t + 1)].bitcast(FP8X4),
+                    lhsT_scale=wk_s[b][:, P * t : P * (t + 1)],
+                    rhs=v_w[:, cols].bitcast(FP8X4),
+                    rhs_scale=v_s[:, cols],
+                    start=True,
+                    stop=True,
+                )
+            return a[:].rearrange("p t j -> p j t")
 
         relu_of = {}
         h_of = {}
+        gp_of = dict((step, (blk, tok)) for blk, (step, tok) in GPSIMD_SQUARES.items())
 
-        def keys(s):
-            c, b = STEPS[s]
-            j0, width = CHUNKS[c]
-            if s == GPSIMD_SQUARES[-1]:
-                x = after_square.tile([P, width, PACK], F32, name="x_gpsimd", align_bytes=64, offset=0)
-            elif s in VECTOR_RELU_STEPS and b < H_PASSES - 1:
-                place = 4 * PACK * width * c
-                x = after_wk.tile([P, width, PACK], F32, name="x_held%d" % s, align_bytes=64, offset=place)
+        def h_tile(c, b):
+            width = CHUNKS[c][1]
+            if (c, b) in gp_of:
+                return round_pool.tile(
+                    [P, width, PACK], BF16, name="h_gp%d_%d" % (c, b), align_bytes=64, offset=ROUND_BYTES * gp_of[(c, b)][0]
+                )
+            return ring.tile([P, width, PACK], BF16, name="h_bf", tag="h_bf", align_bytes=64, bufs=SQUARE_BUFS)
+
+        def scalar_relu(c, b):
+            width = CHUNKS[c][1]
+            if (c, b) in gp_of:
+                x = keep.tile([P, width, PACK], F32, name="x_gp%d_%d" % (c, b))
+            elif (c, b) in HOLDS:
+                held, part = HOLDS[(c, b)]
+                before, wide = CHUNKS[held]
+                place = 4 * N_TILES * before + 2 * N_TILES * wide * part
+                x = results.tile([P, width, PACK], F32, name="x_hold%d_%d" % (c, b), align_bytes=64, offset=place)
             else:
                 x = ring.tile([P, width, PACK], F32, name="x", tag="x", bufs=RELU_BUFS)
-            relu_of[s] = x
+            relu_of[(c, b)] = x
             for bank in range(width // BANK_TOKENS):
-                cols = slice(j0 + bank * BANK_TOKENS, j0 + (bank + 1) * BANK_TOKENS)
-                a = next_bank(key_turns, 0, KEY_BANKS, [P, PACK, BANK_TOKENS])
-                for t in range(PACK):
-                    nc.tensor.matmul_mx(
-                        out=a[:, t, :],
-                        lhsT=wk_w[b][:, P * t : P * (t + 1)].bitcast(FP8X4),
-                        lhsT_scale=wk_s[b][:, P * t : P * (t + 1)],
-                        rhs=v_w[:, cols].bitcast(FP8X4),
-                        rhs_scale=v_s[:, cols],
-                        start=True,
-                        stop=True,
-                    )
-                dst = x[:, bank * BANK_TOKENS : (bank + 1) * BANK_TOKENS, :]
-                src = a[:].rearrange("p t j -> p j t")
-                if s in VECTOR_RELU_STEPS or (s, bank) == VECTOR_RELU_EXTRA:
-                    nc.vector.tensor_scalar(out=dst, in0=src, scalar1=0.0, scalar2=None, op0=ALU.max)
-                else:
-                    nc.scalar.activation(out=dst, in_=src, func=ACT.Relu)
+                a = key_bank(c, b, bank, next_bank(key_turns, 0, KEY_BANKS, [P, PACK, BANK_TOKENS]))
+                nc.scalar.activation(out=x[:, bank * BANK_TOKENS : (bank + 1) * BANK_TOKENS, :], in_=a, func=ACT.Relu)
 
-        def square(s):
-            c, b = STEPS[s]
-            width = CHUNKS[c][1]
-            if b == H_PASSES - 1 and c >= 1:
-                before, wide = CHUNKS[c - 1]
-                place = 4 * N_TILES * before + 2 * N_TILES * wide - (PACK * width if c == LAST_CHUNK else 0)
-                h_bf = results.tile([P, width, PACK], BF16, name="h_last%d" % c, align_bytes=64, offset=place)
-            elif s in GPSIMD_SQUARES:
-                place = 2 * PACK * width * (s - GPSIMD_SQUARES.start)
-                h_bf = after_round.tile([P, width, PACK], BF16, name="h_gpsimd%d" % s, align_bytes=64, offset=place)
+        def scalar_square(c, b):
+            x = relu_of[(c, b)]
+            if (c, b) in gp_of:
+                part = gp_of[(c, b)][1]
+                if part < CHUNKS[c][1]:
+                    nc.scalar.activation(out=h_of[(c, b)][:, part:, :], in_=x[:, part:, :], func=ACT.Square)
             else:
-                h_bf = ring.tile([P, width, PACK], BF16, name="h_bf", tag="h_bf", align_bytes=64, bufs=SQUARE_BUFS)
-            x = relu_of[s]
-            if s == GPSIMD_SQUARES[-1]:
-                part = GPSIMD_LAST_TOKENS
-                nc.gpsimd.tensor_tensor(out=h_bf[:, :part, :], in0=x[:, :part, :], in1=x[:, :part, :], op=ALU.mult)
-                nc.scalar.activation(out=h_bf[:, part:, :], in_=x[:, part:, :], func=ACT.Square)
-            elif s in GPSIMD_SQUARES:
-                nc.gpsimd.tensor_tensor(out=h_bf[:], in0=x[:], in1=x[:], op=ALU.mult)
-            else:
-                nc.scalar.activation(out=h_bf[:], in_=x[:], func=ACT.Square)
-            h_of[s] = h_bf
+                h_of[(c, b)] = h_tile(c, b)
+                nc.scalar.activation(out=h_of[(c, b)][:], in_=x[:], func=ACT.Square)
 
-        def quantize_h(s):
-            c, b = STEPS[s]
+        def gpsimd_square(blk):
+            (c, b), part = GPSIMD_SQUARES[blk]
+            x = relu_of[(c, b)]
+            h_of[(c, b)] = h_tile(c, b)
+            nc.gpsimd.tensor_tensor(out=h_of[(c, b)][:, :part, :], in0=x[:, :part, :], in1=x[:, :part, :], op=ALU.mult)
+
+        def vector_steps(blk, steps, place):
+            units = []
+            place = place + RAW_BYTES * blk
+            for c, b in steps:
+                width = CHUNKS[c][1]
+                x = raw_pool.tile([P, width, PACK], F32, name="x_v%d_%d" % (c, b), align_bytes=64, offset=place)
+                place = place + 4 * PACK * width
+                h_of[(c, b)] = keep.tile([P, width, PACK], BF16, name="h_v%d_%d" % (c, b), align_bytes=64)
+                for bank in range(width // BANK_TOKENS):
+                    a = key_bank(c, b, bank, next_bank(value_turns, KEY_BANKS, VALUE_BANKS, [P, PACK, BANK_TOKENS]))
+                    rows = slice(bank * BANK_TOKENS, (bank + 1) * BANK_TOKENS)
+                    units.append((a, x[:, rows, :], h_of[(c, b)][:, rows, :]))
+            return units
+
+        def vector_relu(unit):
+            a, x, h = unit
+            nc.vector.tensor_scalar(out=x, in0=a, scalar1=0.0, scalar2=None, op0=ALU.max)
+
+        def vector_square(unit):
+            a, x, h = unit
+            nc.vector.scalar_tensor_tensor(out=h, in0=a, scalar=0.0, in1=x, op0=ALU.max, op1=ALU.mult)
+
+        def quantize_h(c, b):
             j0, width = CHUNKS[c]
             cols = slice(j0, j0 + width)
             nc.vector.quantize_mx(
                 out=h_w[:, b, cols].bitcast(FP8X4),
                 scales=h_s[:, b, cols],
-                in_=h_of[s][:].rearrange("p j t -> p (j t)"),
+                in_=h_of[(c, b)][:].rearrange("p j t -> p (j t)"),
             )
 
         y_of = {}
@@ -222,11 +261,11 @@ def tile_list_rwkv_channel_mix_kernel(
         def tiles_a_bank(c):
             return half if c == LAST_CHUNK else BANK // CHUNKS[c][1]
 
-        def values(c, b):
+        def values(c, b, first, last):
             j0, width = CHUNKS[c]
             cols = slice(j0, j0 + width)
             share = tiles_a_bank(c)
-            if b == 0:
+            if first:
                 y_of[c] = [
                     next_bank(value_turns, KEY_BANKS, VALUE_BANKS, [P, share, width]) for i in range(N_TILES // share)
                 ]
@@ -237,8 +276,8 @@ def tile_list_rwkv_channel_mix_kernel(
                     lhsT_scale=wv_s[PACK * b : P, P * n : P * (n + 1)],
                     rhs=h_w[:, b, cols].bitcast(FP8X4),
                     rhs_scale=h_s[:, b, cols],
-                    start=(b == 0 and n % share == 0),
-                    stop=(b == H_PASSES - 1 and n % share == share - 1),
+                    start=(first and n % share == 0),
+                    stop=(last and n % share == share - 1),
                 )
 
         out_rows = out.rearrange("(n p) j -> p n j", p=P)
@@ -284,34 +323,78 @@ def tile_list_rwkv_channel_mix_kernel(
         nc.vector.tensor_copy(v_s[:], tab_s[:].bitcast(U8).indirect(offsets[:]))
         for j0, width in GATHERS:
             nc.vector.tensor_copy(v_w[:, j0 : j0 + width], tab_w[:].bitcast(U32).indirect(listed(j0, width)))
-            receptance(j0, width)
-        for b in range(H_PASSES):
-            quantize_wk(b)
+            receptance(j0, width, range(N_TILES - 1 if j0 == GATHERS[-1][0] else N_TILES))
+
+        on_vector = [step for blk in VECTOR_STEPS for step in VECTOR_STEPS[blk]] + LATE_STEPS
+        scalar_steps = [step for step in STEPS if step not in on_vector]
+        done = []
+        squared = []
+
+        def relu_next():
+            step = scalar_steps[len(done)]
+            scalar_relu(*step)
+            done.append(step)
+
+        def square_next():
+            step = scalar_steps[len(squared)]
+            scalar_square(*step)
+            squared.append(step)
+
+        def weights(blk):
+            if blk in VECTOR_STEPS:
+                round_wk(blk)
+                units = first_units if blk == 1 else vector_steps(blk, VECTOR_STEPS[blk], 0)
+                quantize_wk(blk)
+                gpsimd_square(blk)
+                vector_relu(units[0])
+                for i in range(len(units)):
+                    if i + 1 < len(units):
+                        vector_relu(units[i + 1])
+                    vector_square(units[i])
+            else:
+                round_wk(blk)
+                quantize_wk(blk)
+
+        first_units = []
+        weights(0)
+        first_units.extend(vector_steps(1, VECTOR_STEPS[1], 0))
+        relu_next()
+        relu_next()
+        receptance(GATHERS[-1][0], GATHERS[-1][1], range(N_TILES - 1, N_TILES))
+        weights(1)
+        weights(2)
+        early = [step for step in scalar_steps if step[1] < EARLY_BLOCKS and step[0] < WIDE]
+        while len(done) < len(early):
+            if scalar_steps[len(squared)] != GPSIMD_SQUARES[3][0]:
+                square_next()
+            relu_next()
+        weights(3)
+        late_units = vector_steps(3, LATE_STEPS, RAW_BYTES // 2)
+        relu_next()
+        while len(squared) < len(early) + 1:
+            square_next()
+        ahead = [step for step in h_of]
+        relu_next()
+        while len(squared) < len(scalar_steps):
+            if len(done) < len(scalar_steps):
+                relu_next()
+            square_next()
+
+        for c in range(len(CHUNKS)):
+            for b in range(H_PASSES):
+                if (c, b) not in LATE_STEPS:
+                    quantize_h(c, b)
+        for unit in late_units:
+            vector_relu(unit)
+        for unit in late_units:
+            vector_square(unit)
+        for c, b in LATE_STEPS:
+            quantize_h(c, b)
+        for c in range(len(CHUNKS)):
+            for b in range(H_PASSES):
+                values(c, b, b == 0, b == H_PASSES - 1)
+            gate_values(c)
         for n in range(N_TILES):
             nc.vector.tensor_copy(resid[:, n, :], g_tab[n][:].indirect(listed(FUSED_TOKENS, S - FUSED_TOKENS)))
-
-        def finish(c):
-            if c >= 1:
-                add_and_store(c - 1)
-            gate_values(c)
-
-        keys(0)
-        for s in range(WOVEN_STEPS):
-            keys(s + 1)
-            square(s)
-        for c in range(WOVEN_CHUNKS):
-            for b in range(H_PASSES):
-                quantize_h(STEPS.index((c, b)))
-                values(c, b)
-        finish(0)
-        for s in range(WOVEN_STEPS, len(STEPS)):
-            if s + 1 < len(STEPS):
-                keys(s + 1)
-            square(s)
-            quantize_h(s)
-            values(*STEPS[s])
-            c, b = STEPS[s - 1]
-            if b == H_PASSES - 1:
-                finish(c)
-        finish(LAST_CHUNK)
-        add_and_store(LAST_CHUNK)
+        for c in range(len(CHUNKS)):
+            add_and_store(c)

@@ -34,18 +34,18 @@ LAST_CHUNK = len(CHUNKS) - 1
 FUSED_TOKENS = 768
 WIDE = 3
 EARLY_BLOCKS = 2
-STEPS = (
-    [(c, b) for b in range(EARLY_BLOCKS) for c in range(WIDE)]
-    + [(c, b) for c in range(WIDE) for b in range(EARLY_BLOCKS, H_PASSES)]
-    + [(c, b) for c in range(WIDE, len(CHUNKS)) for b in range(H_PASSES)]
-)
-VECTOR_STEPS = {1: [(2, 0)], 3: [(0, 2)]}
-LATE_STEPS = [(3, 0)]
-HOLDS = {(1, 3): (0, 1), (2, 3): (1, 1), (3, 3): (2, 0), (4, 3): (2, 1)}
-GPSIMD_SQUARES = {1: ((0, 0), 192), 3: ((1, 1), 192)}
+STEPS = [(c, b) for b in range(H_PASSES) for c in range(2)] + [
+    (c, b) for c in range(2, len(CHUNKS)) for b in range(H_PASSES)
+]
+VECTOR_STEPS = [(0, 2), (1, 2)]
+LATE_STEPS = []
+HOLDS = {(2, 3): 6, (3, 3): 10, (4, 1): 12, (4, 3): 14}
+PLACES = {(0, 0): 0, (0, 2): 2, (1, 0): 4, (1, 2): 6, (3, 0): 8, (3, 2): 9, (2, 0): 10, (2, 1): 11, (2, 2): 12, (4, 0): 13, (4, 1): 13.5, (2, 3): 14, (4, 2): 15, (4, 3): 15.5}
+EACH = [2, 2, 1, 4, 1]
+GPSIMD_SQUARES = [((1, 0), 192), ((1, 1), 256)]
 
 RELU_BUFS = 4
-SQUARE_BUFS = 8
+SQUARE_BUFS = 7
 KEY_BANKS = 4
 VALUE_BANKS = 4
 
@@ -116,7 +116,9 @@ def tile_list_rwkv_channel_mix_kernel(
         gate = keep.tile([P, N_TILES, S], F32, name="gate")
         resid = keep.tile([P, N_TILES, S - FUSED_TOKENS], F32, name="resid")
         h_w = keep.tile([P, H_PASSES, S], U32, name="h_w", align_bytes=64)
-        h_s = keep.tile([P, H_PASSES, S], U8, name="h_s", align_bytes=64)
+        h_s = round_pool.tile(
+            [P, H_PASSES, S], U8, name="h_s", align_bytes=64, offset=ROUND_BYTES * H_PASSES + 1984 - 64
+        )
 
         def listed(j0, width):
             return offsets[:, j0 // LIST_ROWS : (j0 + width) // LIST_ROWS]
@@ -148,7 +150,7 @@ def tile_list_rwkv_channel_mix_kernel(
                     BF16,
                     name="wk_bf%d_%d" % (b, u),
                     align_bytes=64,
-                    offset=ROUND_BYTES * b + ROUND_BYTES // PACK * u,
+                    offset=ROUND_BYTES * b + ROUND_BYTES // PACK * u + (1984 if (b, u) == (H_PASSES - 1, 2) else 0),
                 )
                 nc.vector.tensor_copy(
                     out=wk_bf[(b, u)][:].rearrange("p t m j -> p m j t"),
@@ -181,13 +183,19 @@ def tile_list_rwkv_channel_mix_kernel(
 
         relu_of = {}
         h_of = {}
-        gp_of = dict((step, (blk, tok)) for blk, (step, tok) in GPSIMD_SQUARES.items())
+        gp_of = dict((step, (i, tok)) for i, (step, tok) in enumerate(GPSIMD_SQUARES))
+
+        h_gp = round_pool.tile(
+            [P, 2, CHUNKS[1][1], PACK], BF16, name="h_gp", align_bytes=64, offset=ROUND_BYTES * (H_PASSES - 1) - ROUND_BYTES // 2
+        )
 
         def h_tile(c, b):
             width = CHUNKS[c][1]
             if (c, b) in gp_of:
+                return h_gp[:, gp_of[(c, b)][0]]
+            if (c, b) == (0, 1):
                 return round_pool.tile(
-                    [P, width, PACK], BF16, name="h_gp%d_%d" % (c, b), align_bytes=64, offset=ROUND_BYTES * gp_of[(c, b)][0]
+                    [P, width, PACK], BF16, name="h_held", align_bytes=64, offset=ROUND_BYTES * H_PASSES - ROUND_BYTES // 2
                 )
             return ring.tile([P, width, PACK], BF16, name="h_bf", tag="h_bf", align_bytes=64, bufs=SQUARE_BUFS)
 
@@ -196,9 +204,7 @@ def tile_list_rwkv_channel_mix_kernel(
             if (c, b) in gp_of:
                 x = keep.tile([P, width, PACK], F32, name="x_gp%d_%d" % (c, b))
             elif (c, b) in HOLDS:
-                held, part = HOLDS[(c, b)]
-                before, wide = CHUNKS[held]
-                place = 4 * N_TILES * before + 2 * N_TILES * wide * part
+                place = 1024 * HOLDS[(c, b)]
                 x = results.tile([P, width, PACK], F32, name="x_hold%d_%d" % (c, b), align_bytes=64, offset=place)
             else:
                 x = ring.tile([P, width, PACK], F32, name="x", tag="x", bufs=RELU_BUFS)
@@ -223,18 +229,19 @@ def tile_list_rwkv_channel_mix_kernel(
             h_of[(c, b)] = h_tile(c, b)
             nc.gpsimd.tensor_tensor(out=h_of[(c, b)][:, :part, :], in0=x[:, :part, :], in1=x[:, :part, :], op=ALU.mult)
 
-        def vector_steps(blk, steps, place):
+        def vector_steps(steps):
             units = []
-            place = place + RAW_BYTES * blk
             for c, b in steps:
                 width = CHUNKS[c][1]
-                x = raw_pool.tile([P, width, PACK], F32, name="x_v%d_%d" % (c, b), align_bytes=64, offset=place)
-                place = place + 4 * PACK * width
                 h_of[(c, b)] = keep.tile([P, width, PACK], BF16, name="h_v%d_%d" % (c, b), align_bytes=64)
                 for bank in range(width // BANK_TOKENS):
+                    place = RAW_BYTES * (H_PASSES - 1) + BANK_BYTES * (len(units) % PACK)
+                    x = raw_pool.tile(
+                        [P, BANK_TOKENS, PACK], F32, name="x_v%d" % len(units), align_bytes=64, offset=place
+                    )
                     a = key_bank(c, b, bank, next_bank(value_turns, KEY_BANKS, VALUE_BANKS, [P, PACK, BANK_TOKENS]))
                     rows = slice(bank * BANK_TOKENS, (bank + 1) * BANK_TOKENS)
-                    units.append((a, x[:, rows, :], h_of[(c, b)][:, rows, :]))
+                    units.append((a, x[:], h_of[(c, b)][:, rows, :]))
             return units
 
         def vector_relu(unit):
@@ -259,7 +266,7 @@ def tile_list_rwkv_channel_mix_kernel(
         half = N_TILES // 2
 
         def tiles_a_bank(c):
-            return half if c == LAST_CHUNK else BANK // CHUNKS[c][1]
+            return 1 if c == LAST_CHUNK else BANK // CHUNKS[c][1]
 
         def values(c, b, first, last):
             j0, width = CHUNKS[c]
@@ -282,119 +289,95 @@ def tile_list_rwkv_channel_mix_kernel(
 
         out_rows = out.rearrange("(n p) j -> p n j", p=P)
 
-        def gate_values(c):
+        def gate_values(c, tiles):
             j0, width = CHUNKS[c]
             cols = slice(j0, j0 + width)
             share = tiles_a_bank(c)
-            gated = [keep.tile([P, half, width], F32, name="gated%d_%d" % (c, i)) for i in range(2)]
-            gated_of[c] = gated
-            for i in range(2):
-                n0 = i * half
+            if c not in gated_of:
+                gated_of[c] = keep.tile([P, N_TILES, width], F32, name="gated%d" % c)
+            gated = gated_of[c]
+            for n0 in range(tiles.start, tiles.stop, share):
                 nc.vector.tensor_tensor(
-                    out=gated[i][:],
-                    in0=y_of[c][n0 // share][:, n0 % share : n0 % share + half, :],
-                    in1=gate[:, n0 : n0 + half, cols],
+                    out=gated[:, n0 : n0 + share, :],
+                    in0=y_of[c][n0 // share][:],
+                    in1=gate[:, n0 : n0 + share, cols],
                     op=ALU.mult,
                 )
 
-        def add_and_store(c):
+        def add_and_store(c, tiles):
             j0, width = CHUNKS[c]
             cols = slice(j0, j0 + width)
             gated = gated_of[c]
-            for i in range(2):
-                n0 = i * half
-                place = 4 * (N_TILES * j0 + n0 * width)
-                result = results.tile([P, half, width], F32, name="result%d_%d" % (c, i), align_bytes=64, offset=place)
+            each = EACH[c]
+            for n0 in range(tiles.start, tiles.stop, each):
+                place = int(1024 * PLACES[(c, n0)])
+                result = results.tile([P, each, width], F32, name="result%d_%d" % (c, n0), align_bytes=64, offset=place)
                 if j0 < FUSED_TOKENS:
-                    for n in range(n0, n0 + half):
+                    for n in range(n0, n0 + each):
                         nc.vector.tensor_tensor(
                             out=result[:, n - n0, :],
                             in0=g_tab[n][:].indirect(listed(j0, width)),
-                            in1=gated[i][:, n - n0, :],
+                            in1=gated[:, n, :],
                             op=ALU.add,
                         )
                 else:
                     lo = j0 - FUSED_TOKENS
                     nc.vector.tensor_tensor(
-                        out=result[:], in0=gated[i][:], in1=resid[:, n0 : n0 + half, lo : lo + width], op=ALU.add
+                        out=result[:],
+                        in0=gated[:, n0 : n0 + each, :],
+                        in1=resid[:, n0 : n0 + each, lo : lo + width],
+                        op=ALU.add,
                     )
-                nc.sync.dma_start(out=out_rows[:, n0 : n0 + half, cols], in_=result[:])
+                nc.sync.dma_start(out=out_rows[:, n0 : n0 + each, cols], in_=result[:])
 
         nc.vector.tensor_copy(v_s[:], tab_s[:].bitcast(U8).indirect(offsets[:]))
         for j0, width in GATHERS:
             nc.vector.tensor_copy(v_w[:, j0 : j0 + width], tab_w[:].bitcast(U32).indirect(listed(j0, width)))
-            receptance(j0, width, range(N_TILES - 1 if j0 == GATHERS[-1][0] else N_TILES))
+            receptance(j0, width, range(N_TILES))
 
-        on_vector = [step for blk in VECTOR_STEPS for step in VECTOR_STEPS[blk]] + LATE_STEPS
-        scalar_steps = [step for step in STEPS if step not in on_vector]
-        done = []
-        squared = []
+        for b in range(H_PASSES):
+            round_wk(b)
+            quantize_wk(b)
+        scalar_steps = [step for step in STEPS if step not in VECTOR_STEPS]
+        first_late = scalar_steps.index((0, H_PASSES - 1))
+        for i in range(first_late):
+            scalar_relu(*scalar_steps[i])
+            if i >= 1 and scalar_steps[i - 1] not in gp_of:
+                scalar_square(*scalar_steps[i - 1])
+        units = vector_steps(VECTOR_STEPS)
+        for i in range(len(GPSIMD_SQUARES)):
+            gpsimd_square(i)
+        vector_relu(units[0])
+        for i in range(len(units)):
+            if i + 1 < len(units):
+                vector_relu(units[i + 1])
+            vector_square(units[i])
+        for i in range(first_late, len(scalar_steps)):
+            scalar_relu(*scalar_steps[i])
+            if scalar_steps[i - 1] not in gp_of:
+                scalar_square(*scalar_steps[i - 1])
+            if i == first_late + 1:
+                for step in gp_of:
+                    scalar_square(*step)
+                for b in range(H_PASSES):
+                    quantize_h(0, b)
+                    values(0, b, b == 0, b == H_PASSES - 1)
+        scalar_square(*scalar_steps[-1])
 
-        def relu_next():
-            step = scalar_steps[len(done)]
-            scalar_relu(*step)
-            done.append(step)
-
-        def square_next():
-            step = scalar_steps[len(squared)]
-            scalar_square(*step)
-            squared.append(step)
-
-        def weights(blk):
-            if blk in VECTOR_STEPS:
-                round_wk(blk)
-                units = first_units if blk == 1 else vector_steps(blk, VECTOR_STEPS[blk], 0)
-                quantize_wk(blk)
-                gpsimd_square(blk)
-                vector_relu(units[0])
-                for i in range(len(units)):
-                    if i + 1 < len(units):
-                        vector_relu(units[i + 1])
-                    vector_square(units[i])
-            else:
-                round_wk(blk)
-                quantize_wk(blk)
-
-        first_units = []
-        weights(0)
-        first_units.extend(vector_steps(1, VECTOR_STEPS[1], 0))
-        relu_next()
-        relu_next()
-        receptance(GATHERS[-1][0], GATHERS[-1][1], range(N_TILES - 1, N_TILES))
-        weights(1)
-        weights(2)
-        early = [step for step in scalar_steps if step[1] < EARLY_BLOCKS and step[0] < WIDE]
-        while len(done) < len(early):
-            if scalar_steps[len(squared)] != GPSIMD_SQUARES[3][0]:
-                square_next()
-            relu_next()
-        weights(3)
-        late_units = vector_steps(3, LATE_STEPS, RAW_BYTES // 2)
-        relu_next()
-        while len(squared) < len(early) + 1:
-            square_next()
-        ahead = [step for step in h_of]
-        relu_next()
-        while len(squared) < len(scalar_steps):
-            if len(done) < len(scalar_steps):
-                relu_next()
-            square_next()
-
-        for c in range(len(CHUNKS)):
+        for c in range(1, len(CHUNKS)):
             for b in range(H_PASSES):
-                if (c, b) not in LATE_STEPS:
-                    quantize_h(c, b)
-        for unit in late_units:
-            vector_relu(unit)
-        for unit in late_units:
-            vector_square(unit)
-        for c, b in LATE_STEPS:
-            quantize_h(c, b)
+                quantize_h(c, b)
         for c in range(len(CHUNKS)):
-            for b in range(H_PASSES):
+            for b in range(H_PASSES if c else 0):
                 values(c, b, b == 0, b == H_PASSES - 1)
-            gate_values(c)
+            if c < LAST_CHUNK:
+                gate_values(c, range(N_TILES))
         for n in range(N_TILES):
             nc.vector.tensor_copy(resid[:, n, :], g_tab[n][:].indirect(listed(FUSED_TOKENS, S - FUSED_TOKENS)))
-        for c in range(len(CHUNKS)):
-            add_and_store(c)
+        for c in range(LAST_CHUNK):
+            add_and_store(c, range(N_TILES))
+        for n in range(N_TILES):
+            gate_values(LAST_CHUNK, range(n, n + 1))
+            if n >= half:
+                add_and_store(LAST_CHUNK, range(n - half, n - half + 1))
+        add_and_store(LAST_CHUNK, range(half, N_TILES))

@@ -116,9 +116,7 @@ def tile_list_rwkv_channel_mix_kernel(
         gate = keep.tile([P, N_TILES, S], F32, name="gate")
         resid = keep.tile([P, N_TILES, S - FUSED_TOKENS], F32, name="resid")
         h_w = keep.tile([P, H_PASSES, S], U32, name="h_w", align_bytes=64)
-        h_s = round_pool.tile(
-            [P, H_PASSES, S], U8, name="h_s", align_bytes=64, offset=ROUND_BYTES * H_PASSES + 1984 - 64
-        )
+        h_s = keep.tile([P, H_PASSES, S], U8, name="h_s", align_bytes=64)
 
         def listed(j0, width):
             return offsets[:, j0 // LIST_ROWS : (j0 + width) // LIST_ROWS]
@@ -333,7 +331,9 @@ def tile_list_rwkv_channel_mix_kernel(
         nc.vector.tensor_copy(v_s[:], tab_s[:].bitcast(U8).indirect(offsets[:]))
         for j0, width in GATHERS:
             nc.vector.tensor_copy(v_w[:, j0 : j0 + width], tab_w[:].bitcast(U32).indirect(listed(j0, width)))
-            receptance(j0, width, range(N_TILES))
+            for lo, wide in CHUNKS[:LAST_CHUNK]:
+                if j0 <= lo < j0 + width:
+                    receptance(lo, wide, range(N_TILES))
 
         for b in range(H_PASSES):
             round_wk(b)
@@ -342,8 +342,8 @@ def tile_list_rwkv_channel_mix_kernel(
         first_late = scalar_steps.index((0, H_PASSES - 1))
         for i in range(first_late):
             scalar_relu(*scalar_steps[i])
-            if i >= 1 and scalar_steps[i - 1] not in gp_of:
-                scalar_square(*scalar_steps[i - 1])
+            if scalar_steps[i] not in gp_of:
+                scalar_square(*scalar_steps[i])
         units = vector_steps(VECTOR_STEPS)
         for i in range(len(GPSIMD_SQUARES)):
             gpsimd_square(i)
@@ -363,6 +363,8 @@ def tile_list_rwkv_channel_mix_kernel(
                     quantize_h(0, b)
                     values(0, b, b == 0, b == H_PASSES - 1)
         scalar_square(*scalar_steps[-1])
+        key_turns.extend(range(2))
+        receptance(CHUNKS[LAST_CHUNK][0], CHUNKS[LAST_CHUNK][1], range(N_TILES))
 
         for c in range(1, len(CHUNKS)):
             for b in range(H_PASSES):

@@ -21,28 +21,35 @@ PACK = 4
 PASS = P * PACK
 BLOCKS = PASS // 32
 QUADRANT = 32
-H_PASSES = H // PASS
+PARTS = H // PASS
+LAST_PART = PARTS - 1
 N_TILES = N // P
 LIST_ROWS = 16
 BANK = 512
 BANK_BYTES = 4 * BANK
 BANK_TOKENS = BANK // PACK
+PAIR = 2
 
 GATHERS = [(0, 256), (256, 256), (512, 512)]
 CHUNKS = [(0, 256), (256, 256), (512, 256), (768, 128), (896, 128)]
 LAST_CHUNK = len(CHUNKS) - 1
 FUSED_TOKENS = 768
-WIDE = 3
-EARLY_BLOCKS = 2
-STEPS = [(c, b) for b in range(H_PASSES) for c in range(2)] + [
-    (c, b) for c in range(2, len(CHUNKS)) for b in range(H_PASSES)
+WOVEN_CHUNKS = 2
+STEPS = [(c, b) for b in range(PARTS) for c in range(WOVEN_CHUNKS)] + [
+    (c, b) for c in range(WOVEN_CHUNKS, len(CHUNKS)) for b in range(PARTS)
 ]
-VECTOR_STEPS = [(0, 2), (1, 2)]
-LATE_STEPS = []
-HOLDS = {(2, 3): 6, (3, 3): 10, (4, 1): 12, (4, 3): 14}
-PLACES = {(0, 0): 0, (0, 2): 2, (1, 0): 4, (1, 2): 6, (3, 0): 8, (3, 2): 9, (2, 0): 10, (2, 1): 11, (2, 2): 12, (4, 0): 13, (4, 1): 13.5, (2, 3): 14, (4, 2): 15, (4, 3): 15.5}
-EACH = [2, 2, 1, 4, 1]
-GPSIMD_SQUARES = [((1, 0), 192), ((1, 1), 256)]
+VECTOR_STEPS = [(c, LAST_PART - 1) for c in range(WOVEN_CHUNKS)]
+GPSIMD_STEPS = [(WOVEN_CHUNKS - 1, b) for b in range(LAST_PART - 1)]
+GPSIMD_FIRST_TOKENS = 160
+WAITING_SQUARE = (0, LAST_PART - 2)
+TILES_A_RESULT = [2, 2, 1, N_TILES, 1]
+HELD_ADDS = {
+    (2, LAST_PART): [(1, 2)],
+    (3, LAST_PART): [(2, 0), (2, 1)],
+    (LAST_CHUNK, 1): [(2, 2)],
+    (LAST_CHUNK, LAST_PART): [(2, 3)],
+}
+ADD_LAG = 2
 
 RELU_BUFS = 4
 SQUARE_BUFS = 7
@@ -57,18 +64,29 @@ def tile_list_rwkv_channel_mix_kernel(
     with ExitStack() as ctx:
         keep = ctx.enter_context(tc.tile_pool(name="keep", bufs=1))
         ring = ctx.enter_context(tc.tile_pool(name="ring", bufs=RELU_BUFS))
-        raw_pool = ctx.enter_context(tc.tile_pool(name="raw_pool", bufs=1))
-        round_pool = ctx.enter_context(tc.tile_pool(name="round_pool", bufs=1))
-        results = ctx.enter_context(tc.tile_pool(name="results", bufs=1))
         psum = ctx.enter_context(tc.psum_pool(name="psum", bufs=1))
+        last_raw = ctx.enter_context(tc.tile_pool(name="last_raw", bufs=1))
+        last_rounded = [ctx.enter_context(tc.tile_pool(name="last_rounded%d" % u, bufs=1)) for u in range(PACK // PAIR)]
+        holder = {}
+        held_in = {}
+        for step, results in HELD_ADDS.items():
+            holder[step] = ctx.enter_context(tc.tile_pool(name="holder%d_%d" % step, bufs=1))
+            for i, result in enumerate(results):
+                held_in[result] = (holder[step], i)
 
         key_turns = []
         value_turns = []
 
-        def next_bank(turns, first, count, shape):
-            turn = len(turns)
-            turns.append(turn)
-            return psum.tile(shape, F32, name="bank%d_%d" % (first, turn), offset=BANK_BYTES * (first + turn % count))
+        def bank_tile(name, bank, shape):
+            return psum.tile(shape, F32, name=name, offset=BANK_BYTES * bank)
+
+        def next_key_bank(shape):
+            key_turns.append(len(key_turns) % KEY_BANKS)
+            return bank_tile("key%d" % len(key_turns), key_turns[-1], shape)
+
+        def next_value_bank(shape):
+            value_turns.append(KEY_BANKS + len(value_turns) % VALUE_BANKS)
+            return bank_tile("value%d" % len(value_turns), value_turns[-1], shape)
 
         offsets = keep.tile([P, S // LIST_ROWS], U16, name="offsets")
         tab_w = keep.tile([P, T], I32, name="tab_w", align_bytes=64)
@@ -76,7 +94,7 @@ def tile_list_rwkv_channel_mix_kernel(
         wr_w = keep.tile([P, 2 * N], U8, name="wr_w", align_bytes=64)
         wr_s = keep.tile([P, N], U8, name="wr_s", align_bytes=64)
         wv_s = keep.tile([P, N], U8, name="wv_s", align_bytes=64)
-        wv_w = keep.tile([P, H_PASSES, N], I32, name="wv_w", align_bytes=64)
+        wv_w = keep.tile([P, PARTS, N], I32, name="wv_w", align_bytes=64)
 
         nc.vector.memset(tab_s[:], 0)
         nc.vector.memset(wr_s[:].bitcast(I32), 0)
@@ -91,18 +109,14 @@ def tile_list_rwkv_channel_mix_kernel(
             nc.sync.dma_start(out=wr_s[r:P:QUADRANT, :].bitcast(I32), in_=wr_scales[0, r:BLOCKS:PACK, :].bitcast(I32))
 
         wk_rows = wk.rearrange("(p j) c -> p j c", j=PACK)
-        RAW_BYTES = 4 * PACK * PASS
-        ROUND_BYTES = 2 * PACK * PASS
-        wk_raw = [
-            raw_pool.tile([P, PACK, PASS], F32, name="wk_raw%d" % b, align_bytes=64, offset=RAW_BYTES * b)
-            for b in range(H_PASSES)
-        ]
+        wk_raw = [keep.tile([P, PACK, PASS], F32, name="wk_raw%d" % b, align_bytes=64) for b in range(LAST_PART)]
+        wk_raw.append(last_raw.tile([P, PACK, PASS], F32, name="wk_raw_last", align_bytes=64, offset=0))
         g_tab = [keep.tile([P, T], F32, name="g_tab%d" % n) for n in range(N_TILES)]
-        for b in range(H_PASSES):
+        for b in range(PARTS):
             nc.sync.dma_start(out=wk_raw[b][:], in_=wk_rows[:, :, b * PASS : (b + 1) * PASS])
         for q in range(P // QUADRANT):
             nc.sync.dma_start(
-                out=wv_s[QUADRANT * q : QUADRANT * q + PACK * H_PASSES, :].bitcast(I32),
+                out=wv_s[QUADRANT * q : QUADRANT * q + PACK * PARTS, :].bitcast(I32),
                 in_=wv_scales[:, PACK * q : PACK * (q + 1), :].bitcast(I32),
             )
         nc.sync.dma_start(out=wv_w[:], in_=wv_words.rearrange("a p c i -> p a (c i)").bitcast(I32))
@@ -111,65 +125,61 @@ def tile_list_rwkv_channel_mix_kernel(
 
         v_w = keep.tile([P, S], U32, name="v_w", align_bytes=64)
         v_s = keep.tile([P, S], U8, name="v_s", align_bytes=64)
-        wk_w = [keep.tile([P, PASS], U32, name="wk_w%d" % b, align_bytes=64) for b in range(H_PASSES)]
-        wk_s = [keep.tile([P, PASS], U8, name="wk_s%d" % b, align_bytes=64) for b in range(H_PASSES)]
+        wk_w = [keep.tile([P, PASS], U32, name="wk_w%d" % b, align_bytes=64) for b in range(PARTS)]
+        wk_s = [keep.tile([P, PASS], U8, name="wk_s%d" % b, align_bytes=64) for b in range(PARTS)]
         gate = keep.tile([P, N_TILES, S], F32, name="gate")
         resid = keep.tile([P, N_TILES, S - FUSED_TOKENS], F32, name="resid")
-        h_w = keep.tile([P, H_PASSES, S], U32, name="h_w", align_bytes=64)
-        h_s = keep.tile([P, H_PASSES, S], U8, name="h_s", align_bytes=64)
+        h_w = keep.tile([P, PARTS, S], U32, name="h_w", align_bytes=64)
+        h_s = keep.tile([P, PARTS, S], U8, name="h_s", align_bytes=64)
+        gated = [keep.tile([P, N_TILES, width], F32, name="gated%d" % j0) for j0, width in CHUNKS]
+        out_rows = out.rearrange("(n p) j -> p n j", p=P)
 
         def listed(j0, width):
             return offsets[:, j0 // LIST_ROWS : (j0 + width) // LIST_ROWS]
 
-        def receptance(j0, width, tiles):
+        def receptance(c, n0, z):
+            j0, width = CHUNKS[c]
             cols = slice(j0, j0 + width)
             share = BANK // width
-            for n0 in range(tiles.start, tiles.stop, share):
-                z = next_bank(key_turns, 0, KEY_BANKS, [P, share, width])
-                for i in range(share):
-                    n = n0 + i
-                    nc.tensor.matmul_mx(
-                        out=z[:, i, :],
-                        lhsT=wr_w[:, 2 * P * n : 2 * P * (n + 1)].bitcast(FP4X4),
-                        lhsT_scale=wr_s[:, P * n : P * (n + 1)],
-                        rhs=v_w[:, cols].bitcast(FP8X4),
-                        rhs_scale=v_s[:, cols],
-                        start=True,
-                        stop=True,
-                    )
-                nc.scalar.activation(out=gate[:, n0 : n0 + share, cols], in_=z[:], func=ACT.Sigmoid)
-
-        wk_bf = {}
-
-        def round_wk(b):
-            for u in range(0, PACK, 2):
-                wk_bf[(b, u)] = round_pool.tile(
-                    [P, 2, P, PACK],
-                    BF16,
-                    name="wk_bf%d_%d" % (b, u),
-                    align_bytes=64,
-                    offset=ROUND_BYTES * b + ROUND_BYTES // PACK * u + (1984 if (b, u) == (H_PASSES - 1, 2) else 0),
+            for i in range(share):
+                n = n0 + i
+                nc.tensor.matmul_mx(
+                    out=z[:, i, :],
+                    lhsT=wr_w[:, 2 * P * n : 2 * P * (n + 1)].bitcast(FP4X4),
+                    lhsT_scale=wr_s[:, P * n : P * (n + 1)],
+                    rhs=v_w[:, cols].bitcast(FP8X4),
+                    rhs_scale=v_s[:, cols],
+                    start=True,
+                    stop=True,
                 )
-                nc.vector.tensor_copy(
-                    out=wk_bf[(b, u)][:].rearrange("p t m j -> p m j t"),
-                    in_=wk_raw[b][:].rearrange("p j (m t) -> p m j t", t=PACK)[:, :, :, u : u + 2],
-                )
+            nc.scalar.activation(out=gate[:, n0 : n0 + share, cols], in_=z[:], func=ACT.Sigmoid)
 
         def quantize_wk(b):
-            for u in range(0, PACK, 2):
-                cols = slice(P * u, P * (u + 2))
+            rounded = []
+            for u in range(PACK // PAIR):
+                name = "rounded%d_%d" % (b, u)
+                if b == LAST_PART:
+                    half = last_rounded[u].tile([P, PAIR, P, PACK], BF16, name=name, align_bytes=64, offset=0)
+                else:
+                    half = keep.tile([P, PAIR, P, PACK], BF16, name=name, align_bytes=64)
+                rounded.append(half)
+                nc.vector.tensor_copy(
+                    out=half[:].rearrange("p t m j -> p m j t"),
+                    in_=wk_raw[b][:].rearrange("p j (m t) -> p m j t", t=PACK)[:, :, :, PAIR * u : PAIR * (u + 1)],
+                )
+            for u in range(PACK // PAIR):
+                cols = slice(PAIR * P * u, PAIR * P * (u + 1))
                 nc.vector.quantize_mx(
                     out=wk_w[b][:, cols].bitcast(FP8X4),
                     scales=wk_s[b][:, cols],
-                    in_=wk_bf[(b, u)][:].rearrange("p t m j -> p (t m j)"),
+                    in_=rounded[u][:].rearrange("p t m j -> p (t m j)"),
                 )
 
-        def key_bank(c, b, bank, a):
-            j0 = CHUNKS[c][0] + bank * BANK_TOKENS
+        def keys(j0, b, bank):
             cols = slice(j0, j0 + BANK_TOKENS)
             for t in range(PACK):
                 nc.tensor.matmul_mx(
-                    out=a[:, t, :],
+                    out=bank[:, t, :],
                     lhsT=wk_w[b][:, P * t : P * (t + 1)].bitcast(FP8X4),
                     lhsT_scale=wk_s[b][:, P * t : P * (t + 1)],
                     rhs=v_w[:, cols].bitcast(FP8X4),
@@ -177,103 +187,87 @@ def tile_list_rwkv_channel_mix_kernel(
                     start=True,
                     stop=True,
                 )
-            return a[:].rearrange("p t j -> p j t")
+            return bank[:].rearrange("p t j -> p j t")
 
         relu_of = {}
         h_of = {}
-        gp_of = dict((step, (i, tok)) for i, (step, tok) in enumerate(GPSIMD_SQUARES))
 
-        h_gp = round_pool.tile(
-            [P, 2, CHUNKS[1][1], PACK], BF16, name="h_gp", align_bytes=64, offset=ROUND_BYTES * (H_PASSES - 1) - ROUND_BYTES // 2
-        )
-
-        def h_tile(c, b):
-            width = CHUNKS[c][1]
-            if (c, b) in gp_of:
-                return h_gp[:, gp_of[(c, b)][0]]
-            if (c, b) == (0, 1):
-                return round_pool.tile(
-                    [P, width, PACK], BF16, name="h_held", align_bytes=64, offset=ROUND_BYTES * H_PASSES - ROUND_BYTES // 2
-                )
-            return ring.tile([P, width, PACK], BF16, name="h_bf", tag="h_bf", align_bytes=64, bufs=SQUARE_BUFS)
-
-        def scalar_relu(c, b):
-            width = CHUNKS[c][1]
-            if (c, b) in gp_of:
-                x = keep.tile([P, width, PACK], F32, name="x_gp%d_%d" % (c, b))
-            elif (c, b) in HOLDS:
-                place = 1024 * HOLDS[(c, b)]
-                x = results.tile([P, width, PACK], F32, name="x_hold%d_%d" % (c, b), align_bytes=64, offset=place)
+        def scalar_relu(step):
+            c, b = step
+            j0, width = CHUNKS[c]
+            shape = [P, width, PACK]
+            if step in GPSIMD_STEPS:
+                x = keep.tile(shape, F32, name="relu_gpsimd%d" % b)
+            elif step in holder:
+                x = holder[step].tile(shape, F32, name="relu_holder%d_%d" % step, align_bytes=64, offset=0)
             else:
-                x = ring.tile([P, width, PACK], F32, name="x", tag="x", bufs=RELU_BUFS)
-            relu_of[(c, b)] = x
-            for bank in range(width // BANK_TOKENS):
-                a = key_bank(c, b, bank, next_bank(key_turns, 0, KEY_BANKS, [P, PACK, BANK_TOKENS]))
-                nc.scalar.activation(out=x[:, bank * BANK_TOKENS : (bank + 1) * BANK_TOKENS, :], in_=a, func=ACT.Relu)
+                x = ring.tile(shape, F32, name="relu", tag="relu", bufs=RELU_BUFS)
+            relu_of[step] = x
+            for lo in range(0, width, BANK_TOKENS):
+                a = keys(j0 + lo, b, next_key_bank([P, PACK, BANK_TOKENS]))
+                nc.scalar.activation(out=x[:, lo : lo + BANK_TOKENS, :], in_=a, func=ACT.Relu)
 
-        def scalar_square(c, b):
-            x = relu_of[(c, b)]
-            if (c, b) in gp_of:
-                part = gp_of[(c, b)][1]
-                if part < CHUNKS[c][1]:
-                    nc.scalar.activation(out=h_of[(c, b)][:, part:, :], in_=x[:, part:, :], func=ACT.Square)
+        def scalar_square(step):
+            shape = [P, CHUNKS[step[0]][1], PACK]
+            if step == WAITING_SQUARE:
+                h = last_rounded[-1].tile(shape, BF16, name="h_waiting", align_bytes=64, offset=0)
             else:
-                h_of[(c, b)] = h_tile(c, b)
-                nc.scalar.activation(out=h_of[(c, b)][:], in_=x[:], func=ACT.Square)
+                h = ring.tile(shape, BF16, name="h", tag="h", align_bytes=64, bufs=SQUARE_BUFS)
+            h_of[step] = h[:]
+            nc.scalar.activation(out=h[:], in_=relu_of[step][:], func=ACT.Square)
 
-        def gpsimd_square(blk):
-            (c, b), part = GPSIMD_SQUARES[blk]
-            x = relu_of[(c, b)]
-            h_of[(c, b)] = h_tile(c, b)
-            nc.gpsimd.tensor_tensor(out=h_of[(c, b)][:, :part, :], in0=x[:, :part, :], in1=x[:, :part, :], op=ALU.mult)
+        def gpsimd_squares():
+            width = CHUNKS[WOVEN_CHUNKS - 1][1]
+            h = last_rounded[0].tile([P, len(GPSIMD_STEPS), width, PACK], BF16, name="h_gpsimd", align_bytes=64, offset=0)
+            for i, step in enumerate(GPSIMD_STEPS):
+                tokens = GPSIMD_FIRST_TOKENS if i == 0 else width
+                x = relu_of[step][:, :tokens, :]
+                h_of[step] = h[:, i]
+                nc.gpsimd.tensor_tensor(out=h[:, i, :tokens, :], in0=x, in1=x, op=ALU.mult)
 
-        def vector_steps(steps):
-            units = []
-            for c, b in steps:
-                width = CHUNKS[c][1]
-                h_of[(c, b)] = keep.tile([P, width, PACK], BF16, name="h_v%d_%d" % (c, b), align_bytes=64)
-                for bank in range(width // BANK_TOKENS):
-                    place = RAW_BYTES * (H_PASSES - 1) + BANK_BYTES * (len(units) % PACK)
-                    x = raw_pool.tile(
-                        [P, BANK_TOKENS, PACK], F32, name="x_v%d" % len(units), align_bytes=64, offset=place
+        def vector_keys():
+            banks = []
+            for step in VECTOR_STEPS:
+                c, b = step
+                j0, width = CHUNKS[c]
+                h = keep.tile([P, width, PACK], BF16, name="h_vector%d" % c, align_bytes=64)
+                h_of[step] = h[:]
+                for lo in range(0, width, BANK_TOKENS):
+                    place = BANK_BYTES * len(banks)
+                    x = last_raw.tile(
+                        [P, BANK_TOKENS, PACK], F32, name="relu_vector%d" % place, align_bytes=64, offset=place
                     )
-                    a = key_bank(c, b, bank, next_bank(value_turns, KEY_BANKS, VALUE_BANKS, [P, PACK, BANK_TOKENS]))
-                    rows = slice(bank * BANK_TOKENS, (bank + 1) * BANK_TOKENS)
-                    units.append((a, x[:], h_of[(c, b)][:, rows, :]))
-            return units
+                    a = keys(j0 + lo, b, next_value_bank([P, PACK, BANK_TOKENS]))
+                    banks.append((a, x[:], h[:, lo : lo + BANK_TOKENS, :]))
+            return banks
 
-        def vector_relu(unit):
-            a, x, h = unit
-            nc.vector.tensor_scalar(out=x, in0=a, scalar1=0.0, scalar2=None, op0=ALU.max)
-
-        def vector_square(unit):
-            a, x, h = unit
-            nc.vector.scalar_tensor_tensor(out=h, in0=a, scalar=0.0, in1=x, op0=ALU.max, op1=ALU.mult)
+        def vector_run(banks):
+            for i in range(len(banks) + 1):
+                if i < len(banks):
+                    a, x, h = banks[i]
+                    nc.vector.tensor_scalar(out=x, in0=a, scalar1=0.0, scalar2=None, op0=ALU.max)
+                if i >= 1:
+                    a, x, h = banks[i - 1]
+                    nc.vector.scalar_tensor_tensor(out=h, in0=a, scalar=0.0, in1=x, op0=ALU.max, op1=ALU.mult)
 
         def quantize_h(c, b):
             j0, width = CHUNKS[c]
             cols = slice(j0, j0 + width)
             nc.vector.quantize_mx(
-                out=h_w[:, b, cols].bitcast(FP8X4),
-                scales=h_s[:, b, cols],
-                in_=h_of[(c, b)][:].rearrange("p j t -> p (j t)"),
+                out=h_w[:, b, cols].bitcast(FP8X4), scales=h_s[:, b, cols], in_=h_of[(c, b)].rearrange("p j t -> p (j t)")
             )
 
         y_of = {}
-        gated_of = {}
-        half = N_TILES // 2
 
         def tiles_a_bank(c):
             return 1 if c == LAST_CHUNK else BANK // CHUNKS[c][1]
 
-        def values(c, b, first, last):
+        def values(c, b):
             j0, width = CHUNKS[c]
             cols = slice(j0, j0 + width)
             share = tiles_a_bank(c)
-            if first:
-                y_of[c] = [
-                    next_bank(value_turns, KEY_BANKS, VALUE_BANKS, [P, share, width]) for i in range(N_TILES // share)
-                ]
+            if b == 0:
+                y_of[c] = [next_value_bank([P, share, width]) for i in range(N_TILES // share)]
             for n in range(N_TILES):
                 nc.tensor.matmul_mx(
                     out=y_of[c][n // share][:, n % share, :],
@@ -281,105 +275,103 @@ def tile_list_rwkv_channel_mix_kernel(
                     lhsT_scale=wv_s[PACK * b : P, P * n : P * (n + 1)],
                     rhs=h_w[:, b, cols].bitcast(FP8X4),
                     rhs_scale=h_s[:, b, cols],
-                    start=(first and n % share == 0),
-                    stop=(last and n % share == share - 1),
+                    start=(b == 0 and n % share == 0),
+                    stop=(b == LAST_PART and n % share == share - 1),
                 )
 
-        out_rows = out.rearrange("(n p) j -> p n j", p=P)
-
-        def gate_values(c, tiles):
+        def gate_values(c, n0):
             j0, width = CHUNKS[c]
-            cols = slice(j0, j0 + width)
             share = tiles_a_bank(c)
-            if c not in gated_of:
-                gated_of[c] = keep.tile([P, N_TILES, width], F32, name="gated%d" % c)
-            gated = gated_of[c]
-            for n0 in range(tiles.start, tiles.stop, share):
-                nc.vector.tensor_tensor(
-                    out=gated[:, n0 : n0 + share, :],
-                    in0=y_of[c][n0 // share][:],
-                    in1=gate[:, n0 : n0 + share, cols],
-                    op=ALU.mult,
-                )
+            nc.vector.tensor_tensor(
+                out=gated[c][:, n0 : n0 + share, :],
+                in0=y_of[c][n0 // share][:],
+                in1=gate[:, n0 : n0 + share, j0 : j0 + width],
+                op=ALU.mult,
+            )
 
-        def add_and_store(c, tiles):
+        def add_and_store(c, n0):
             j0, width = CHUNKS[c]
-            cols = slice(j0, j0 + width)
-            gated = gated_of[c]
-            each = EACH[c]
-            for n0 in range(tiles.start, tiles.stop, each):
-                place = int(1024 * PLACES[(c, n0)])
-                result = results.tile([P, each, width], F32, name="result%d_%d" % (c, n0), align_bytes=64, offset=place)
-                if j0 < FUSED_TOKENS:
-                    for n in range(n0, n0 + each):
-                        nc.vector.tensor_tensor(
-                            out=result[:, n - n0, :],
-                            in0=g_tab[n][:].indirect(listed(j0, width)),
-                            in1=gated[:, n, :],
-                            op=ALU.add,
-                        )
-                else:
-                    lo = j0 - FUSED_TOKENS
+            count = TILES_A_RESULT[c]
+            shape = [P, count, width]
+            name = "result%d_%d" % (c, n0)
+            if (c, n0) in held_in:
+                pool, i = held_in[(c, n0)]
+                result = pool.tile(shape, F32, name=name, align_bytes=64, offset=4 * count * width * i)
+            else:
+                result = keep.tile(shape, F32, name=name, align_bytes=64)
+            if j0 < FUSED_TOKENS:
+                for n in range(n0, n0 + count):
                     nc.vector.tensor_tensor(
-                        out=result[:],
-                        in0=gated[:, n0 : n0 + each, :],
-                        in1=resid[:, n0 : n0 + each, lo : lo + width],
+                        out=result[:, n - n0, :],
+                        in0=g_tab[n][:].indirect(listed(j0, width)),
+                        in1=gated[c][:, n, :],
                         op=ALU.add,
                     )
-                nc.sync.dma_start(out=out_rows[:, n0 : n0 + each, cols], in_=result[:])
+            else:
+                lo = j0 - FUSED_TOKENS
+                nc.vector.tensor_tensor(
+                    out=result[:],
+                    in0=gated[c][:, n0 : n0 + count, :],
+                    in1=resid[:, n0 : n0 + count, lo : lo + width],
+                    op=ALU.add,
+                )
+            nc.sync.dma_start(out=out_rows[:, n0 : n0 + count, j0 : j0 + width], in_=result[:])
 
         nc.vector.tensor_copy(v_s[:], tab_s[:].bitcast(U8).indirect(offsets[:]))
         for j0, width in GATHERS:
             nc.vector.tensor_copy(v_w[:, j0 : j0 + width], tab_w[:].bitcast(U32).indirect(listed(j0, width)))
-            for lo, wide in CHUNKS[:LAST_CHUNK]:
-                if j0 <= lo < j0 + width:
-                    receptance(lo, wide, range(N_TILES))
-
-        for b in range(H_PASSES):
-            round_wk(b)
+            for c in range(LAST_CHUNK):
+                first, count = CHUNKS[c]
+                if j0 <= first < j0 + width:
+                    for n0 in range(0, N_TILES, BANK // count):
+                        receptance(c, n0, next_key_bank([P, BANK // count, count]))
+        for b in range(PARTS):
             quantize_wk(b)
+
         scalar_steps = [step for step in STEPS if step not in VECTOR_STEPS]
-        first_late = scalar_steps.index((0, H_PASSES - 1))
-        for i in range(first_late):
-            scalar_relu(*scalar_steps[i])
-            if scalar_steps[i] not in gp_of:
-                scalar_square(*scalar_steps[i])
-        units = vector_steps(VECTOR_STEPS)
-        for i in range(len(GPSIMD_SQUARES)):
-            gpsimd_square(i)
-        vector_relu(units[0])
-        for i in range(len(units)):
-            if i + 1 < len(units):
-                vector_relu(units[i + 1])
-            vector_square(units[i])
-        for i in range(first_late, len(scalar_steps)):
-            scalar_relu(*scalar_steps[i])
-            if scalar_steps[i - 1] not in gp_of:
-                scalar_square(*scalar_steps[i - 1])
-            if i == first_late + 1:
-                for step in gp_of:
-                    scalar_square(*step)
-                for b in range(H_PASSES):
-                    quantize_h(0, b)
-                    values(0, b, b == 0, b == H_PASSES - 1)
-        scalar_square(*scalar_steps[-1])
-        key_turns.extend(range(2))
-        receptance(CHUNKS[LAST_CHUNK][0], CHUNKS[LAST_CHUNK][1], range(N_TILES))
+        early = scalar_steps.index((0, LAST_PART))
+        for step in scalar_steps[:early]:
+            scalar_relu(step)
+            if step not in GPSIMD_STEPS:
+                scalar_square(step)
+        banks = vector_keys()
+        gpsimd_squares()
+        vector_run(banks)
+
+        late = scalar_steps[early:]
+        scalar_relu(late[0])
+        scalar_relu(late[1])
+        scalar_square(late[0])
+        shared = GPSIMD_STEPS[0]
+        nc.scalar.activation(
+            out=h_of[shared][:, GPSIMD_FIRST_TOKENS:, :], in_=relu_of[shared][:, GPSIMD_FIRST_TOKENS:, :], func=ACT.Square
+        )
+        for b in range(PARTS):
+            quantize_h(0, b)
+            values(0, b)
+        for i in range(2, len(late)):
+            scalar_relu(late[i])
+            scalar_square(late[i - 1])
+        scalar_square(late[-1])
+        receptance(LAST_CHUNK, 0, bank_tile("last_gate", key_turns[-2], [P, N_TILES, CHUNKS[LAST_CHUNK][1]]))
 
         for c in range(1, len(CHUNKS)):
-            for b in range(H_PASSES):
+            for b in range(PARTS):
                 quantize_h(c, b)
         for c in range(len(CHUNKS)):
-            for b in range(H_PASSES if c else 0):
-                values(c, b, b == 0, b == H_PASSES - 1)
+            if c >= 1:
+                for b in range(PARTS):
+                    values(c, b)
             if c < LAST_CHUNK:
-                gate_values(c, range(N_TILES))
+                for n0 in range(0, N_TILES, tiles_a_bank(c)):
+                    gate_values(c, n0)
         for n in range(N_TILES):
             nc.vector.tensor_copy(resid[:, n, :], g_tab[n][:].indirect(listed(FUSED_TOKENS, S - FUSED_TOKENS)))
         for c in range(LAST_CHUNK):
-            add_and_store(c, range(N_TILES))
-        for n in range(N_TILES):
-            gate_values(LAST_CHUNK, range(n, n + 1))
-            if n >= half:
-                add_and_store(LAST_CHUNK, range(n - half, n - half + 1))
-        add_and_store(LAST_CHUNK, range(half, N_TILES))
+            for n0 in range(0, N_TILES, TILES_A_RESULT[c]):
+                add_and_store(c, n0)
+        for n in range(N_TILES + ADD_LAG):
+            if n < N_TILES:
+                gate_values(LAST_CHUNK, n)
+            if n >= ADD_LAG:
+                add_and_store(LAST_CHUNK, n - ADD_LAG)

@@ -28,31 +28,31 @@ LIST_ROWS = 16
 BANK = 512
 BANK_BYTES = 4 * BANK
 BANK_TOKENS = BANK // PACK
+HALF_BYTES = 2048
 PAIR = 2
 
-GATHERS = [(0, 256), (256, 256), (512, 512)]
+GATHERS = [(0, 128), (128, 128), (256, 256), (512, 512)]
 CHUNKS = [(0, 256), (256, 256), (512, 256), (768, 128), (896, 128)]
 LAST_CHUNK = len(CHUNKS) - 1
-FUSED_TOKENS = 768
-WOVEN_CHUNKS = 2
-STEPS = [(c, b) for b in range(PARTS) for c in range(WOVEN_CHUNKS)] + [
-    (c, b) for c in range(WOVEN_CHUNKS, len(CHUNKS)) for b in range(PARTS)
-]
-VECTOR_STEPS = [(c, LAST_PART - 1) for c in range(WOVEN_CHUNKS)]
-GPSIMD_STEPS = [(WOVEN_CHUNKS - 1, b) for b in range(LAST_PART - 1)]
-GPSIMD_FIRST_TOKENS = 160
+LAST_TOKENS = CHUNKS[LAST_CHUNK]
+VECTOR_STEPS = [(0, LAST_PART - 1), (1, LAST_PART - 1)]
+GPSIMD_TOKENS = {(1, 0): 160, (1, 1): 256, (2, 0): 96, (2, 1): 64, (LAST_CHUNK, 0): 64}
 WAITING_SQUARE = (0, LAST_PART - 2)
-TILES_A_RESULT = [2, 2, 1, N_TILES, 1]
-HELD_ADDS = {
-    (2, LAST_PART): [(1, 2)],
-    (3, LAST_PART): [(2, 0), (2, 1)],
-    (LAST_CHUNK, 1): [(2, 2)],
-    (LAST_CHUNK, LAST_PART): [(2, 3)],
+HELD = {
+    (2, 0): [("add", 0, 0), ("gate", 1)],
+    (2, 2): [("add", 0, 2), ("add", 1, 2)],
+    (2, LAST_PART): [("add", 0, 3), ("add", 1, 3)],
+    (3, 0): [("gate", 2)],
+    (3, 2): [("add", 2, 1)],
+    (3, LAST_PART): [("add", 2, 2)],
+    (LAST_CHUNK, 1): [("add", 3, 0), ("add", 3, 1), ("add", 3, 2)],
+    (LAST_CHUNK, 2): [("add", 3, 3)],
+    (LAST_CHUNK, LAST_PART): [("add", 2, 3)],
 }
 ADD_LAG = 2
 
-RELU_BUFS = 4
-SQUARE_BUFS = 7
+RELU_BUFS = 2
+SQUARE_BUFS = 6
 KEY_BANKS = 4
 VALUE_BANKS = 4
 
@@ -67,12 +67,22 @@ def tile_list_rwkv_channel_mix_kernel(
         psum = ctx.enter_context(tc.psum_pool(name="psum", bufs=1))
         last_raw = ctx.enter_context(tc.tile_pool(name="last_raw", bufs=1))
         last_rounded = [ctx.enter_context(tc.tile_pool(name="last_rounded%d" % u, bufs=1)) for u in range(PACK // PAIR)]
+        window_h = ctx.enter_context(tc.tile_pool(name="window_h", bufs=1))
         holder = {}
-        held_in = {}
-        for step, results in HELD_ADDS.items():
+        place = {}
+        for step, outputs in HELD.items():
             holder[step] = ctx.enter_context(tc.tile_pool(name="holder%d_%d" % step, bufs=1))
-            for i, result in enumerate(results):
-                held_in[result] = (holder[step], i)
+            offset = 0
+            for output in outputs:
+                place[output] = (holder[step], offset)
+                offset = offset + 4 * CHUNKS[output[1]][1]
+
+        def float_tile(output, shape):
+            name = "_".join(str(word) for word in output)
+            if output in place:
+                pool, offset = place[output]
+                return pool.tile(shape, F32, name=name, align_bytes=64, offset=offset)
+            return keep.tile(shape, F32, name=name, align_bytes=64)
 
         key_turns = []
         value_turns = []
@@ -96,17 +106,21 @@ def tile_list_rwkv_channel_mix_kernel(
         wv_s = keep.tile([P, N], U8, name="wv_s", align_bytes=64)
         wv_w = keep.tile([P, PARTS, N], I32, name="wv_w", align_bytes=64)
 
-        nc.vector.memset(tab_s[:], 0)
         nc.vector.memset(wr_s[:].bitcast(I32), 0)
+        nc.vector.memset(tab_s[:], 0)
         nc.vector.memset(wv_s[:].bitcast(I32), 0)
 
+        def load_wr_scales(r):
+            nc.sync.dma_start(out=wr_s[r:P:QUADRANT, :].bitcast(I32), in_=wr_scales[0, r:BLOCKS:PACK, :].bitcast(I32))
+
         nc.sync.dma_start(offsets[:], offs)
-        nc.sync.dma_start(out=wr_w[:].bitcast(I32), in_=wr_words[0].bitcast(I32))
+        load_wr_scales(0)
         for r in range(PACK):
             nc.sync.dma_start(out=tab_s[r:P:QUADRANT, :], in_=tab_scales[0, r:BLOCKS:PACK, :].bitcast(I32))
         nc.sync.dma_start(out=tab_w[:], in_=tab_words[0].rearrange("p t i -> p (t i)").bitcast(I32))
-        for r in range(PACK):
-            nc.sync.dma_start(out=wr_s[r:P:QUADRANT, :].bitcast(I32), in_=wr_scales[0, r:BLOCKS:PACK, :].bitcast(I32))
+        nc.sync.dma_start(out=wr_w[:].bitcast(I32), in_=wr_words[0].bitcast(I32))
+        for r in range(1, PACK):
+            load_wr_scales(r)
 
         wk_rows = wk.rearrange("(p j) c -> p j c", j=PACK)
         wk_raw = [keep.tile([P, PACK, PASS], F32, name="wk_raw%d" % b, align_bytes=64) for b in range(LAST_PART)]
@@ -128,19 +142,16 @@ def tile_list_rwkv_channel_mix_kernel(
         wk_w = [keep.tile([P, PASS], U32, name="wk_w%d" % b, align_bytes=64) for b in range(PARTS)]
         wk_s = [keep.tile([P, PASS], U8, name="wk_s%d" % b, align_bytes=64) for b in range(PARTS)]
         gate = keep.tile([P, N_TILES, S], F32, name="gate")
-        resid = keep.tile([P, N_TILES, S - FUSED_TOKENS], F32, name="resid")
+        resid = keep.tile([P, N_TILES, LAST_TOKENS[1]], F32, name="resid")
         h_w = keep.tile([P, PARTS, S], U32, name="h_w", align_bytes=64)
         h_s = keep.tile([P, PARTS, S], U8, name="h_s", align_bytes=64)
-        gated = [keep.tile([P, N_TILES, width], F32, name="gated%d" % j0) for j0, width in CHUNKS]
         out_rows = out.rearrange("(n p) j -> p n j", p=P)
 
         def listed(j0, width):
             return offsets[:, j0 // LIST_ROWS : (j0 + width) // LIST_ROWS]
 
-        def receptance(c, n0, z):
-            j0, width = CHUNKS[c]
+        def receptance(j0, width, n0, share, z):
             cols = slice(j0, j0 + width)
-            share = BANK // width
             for i in range(share):
                 n = n0 + i
                 nc.tensor.matmul_mx(
@@ -159,7 +170,7 @@ def tile_list_rwkv_channel_mix_kernel(
             for u in range(PACK // PAIR):
                 name = "rounded%d_%d" % (b, u)
                 if b == LAST_PART:
-                    half = last_rounded[u].tile([P, PAIR, P, PACK], BF16, name=name, align_bytes=64, offset=0)
+                    half = last_rounded[u].tile([P, PAIR, P, PACK], BF16, name=name, align_bytes=64, offset=HALF_BYTES // 2)
                 else:
                     half = keep.tile([P, PAIR, P, PACK], BF16, name=name, align_bytes=64)
                 rounded.append(half)
@@ -175,13 +186,14 @@ def tile_list_rwkv_channel_mix_kernel(
                     in_=rounded[u][:].rearrange("p t m j -> p (t m j)"),
                 )
 
-        def keys(j0, b, bank):
-            cols = slice(j0, j0 + BANK_TOKENS)
-            for t in range(PACK):
+        def keys(j0, width, b, t0, bank):
+            cols = slice(j0, j0 + width)
+            for t in range(BANK // width):
+                first = P * (t0 + t)
                 nc.tensor.matmul_mx(
                     out=bank[:, t, :],
-                    lhsT=wk_w[b][:, P * t : P * (t + 1)].bitcast(FP8X4),
-                    lhsT_scale=wk_s[b][:, P * t : P * (t + 1)],
+                    lhsT=wk_w[b][:, first : first + P].bitcast(FP8X4),
+                    lhsT_scale=wk_s[b][:, first : first + P],
                     rhs=v_w[:, cols].bitcast(FP8X4),
                     rhs_scale=v_s[:, cols],
                     start=True,
@@ -192,52 +204,75 @@ def tile_list_rwkv_channel_mix_kernel(
         relu_of = {}
         h_of = {}
 
-        def scalar_relu(step):
+        def paired(step):
+            return CHUNKS[step[0]][1] > BANK_TOKENS and step not in GPSIMD_TOKENS
+
+        def relu(step, i):
             c, b = step
             j0, width = CHUNKS[c]
-            shape = [P, width, PACK]
-            if step in GPSIMD_STEPS:
-                x = keep.tile(shape, F32, name="relu_gpsimd%d" % b)
-            elif step in holder:
-                x = holder[step].tile(shape, F32, name="relu_holder%d_%d" % step, align_bytes=64, offset=0)
+            if i == 0:
+                shape = [P, PACK // PAIR, width, PAIR] if paired(step) else [P, width, PACK]
+                if step in holder:
+                    x = holder[step].tile(shape, F32, name="relu%d_%d" % step, align_bytes=64, offset=0)
+                elif step in GPSIMD_TOKENS:
+                    x = keep.tile(shape, F32, name="relu%d_%d" % step)
+                else:
+                    x = ring.tile(shape, F32, name="relu", tag="relu", bufs=RELU_BUFS)
+                relu_of[step] = x
+            if paired(step):
+                a = keys(j0, width, b, PAIR * i, next_key_bank([P, PAIR, width]))
+                nc.scalar.activation(out=relu_of[step][:, i], in_=a, func=ACT.Relu)
             else:
-                x = ring.tile(shape, F32, name="relu", tag="relu", bufs=RELU_BUFS)
-            relu_of[step] = x
-            for lo in range(0, width, BANK_TOKENS):
-                a = keys(j0 + lo, b, next_key_bank([P, PACK, BANK_TOKENS]))
-                nc.scalar.activation(out=x[:, lo : lo + BANK_TOKENS, :], in_=a, func=ACT.Relu)
+                lo = BANK_TOKENS * i
+                a = keys(j0 + lo, BANK_TOKENS, b, 0, next_key_bank([P, PACK, BANK_TOKENS]))
+                nc.scalar.activation(out=relu_of[step][:, lo : lo + BANK_TOKENS, :], in_=a, func=ACT.Relu)
 
-        def scalar_square(step):
+        def relus(step):
+            for i in range(CHUNKS[step[0]][1] // BANK_TOKENS):
+                relu(step, i)
+
+        def square(step):
+            if step in GPSIMD_TOKENS:
+                lo = GPSIMD_TOKENS[step]
+                nc.scalar.activation(out=h_of[step][:, lo:, :], in_=relu_of[step][:, lo:, :], func=ACT.Square)
+                return
             shape = [P, CHUNKS[step[0]][1], PACK]
             if step == WAITING_SQUARE:
                 h = last_rounded[-1].tile(shape, BF16, name="h_waiting", align_bytes=64, offset=0)
             else:
                 h = ring.tile(shape, BF16, name="h", tag="h", align_bytes=64, bufs=SQUARE_BUFS)
             h_of[step] = h[:]
-            nc.scalar.activation(out=h[:], in_=relu_of[step][:], func=ACT.Square)
+            if paired(step):
+                nc.scalar.activation(
+                    out=h[:].rearrange("p j (u t) -> p j u t", t=PAIR),
+                    in_=relu_of[step][:].rearrange("p u j t -> p j u t"),
+                    func=ACT.Square,
+                )
+            else:
+                nc.scalar.activation(out=h[:], in_=relu_of[step][:], func=ACT.Square)
 
-        def gpsimd_squares():
-            width = CHUNKS[WOVEN_CHUNKS - 1][1]
-            h = last_rounded[0].tile([P, len(GPSIMD_STEPS), width, PACK], BF16, name="h_gpsimd", align_bytes=64, offset=0)
-            for i, step in enumerate(GPSIMD_STEPS):
-                tokens = GPSIMD_FIRST_TOKENS if i == 0 else width
-                x = relu_of[step][:, :tokens, :]
-                h_of[step] = h[:, i]
-                nc.gpsimd.tensor_tensor(out=h[:, i, :tokens, :], in0=x, in1=x, op=ALU.mult)
+        def gpsimd_square(step, pool, offset):
+            h = pool.tile([P, CHUNKS[step[0]][1], PACK], BF16, name="h%d_%d" % step, align_bytes=64, offset=offset)
+            h_of[step] = h[:]
+            x = relu_of[step][:, : GPSIMD_TOKENS[step], :]
+            nc.gpsimd.tensor_tensor(out=h[:, : GPSIMD_TOKENS[step], :], in0=x, in1=x, op=ALU.mult)
 
         def vector_keys():
             banks = []
             for step in VECTOR_STEPS:
                 c, b = step
                 j0, width = CHUNKS[c]
-                h = keep.tile([P, width, PACK], BF16, name="h_vector%d" % c, align_bytes=64)
+                if step == VECTOR_STEPS[-1]:
+                    h = window_h.tile([P, width, PACK], BF16, name="h%d_%d" % step, align_bytes=64, offset=0)
+                else:
+                    h = keep.tile([P, width, PACK], BF16, name="h%d_%d" % step, align_bytes=64)
                 h_of[step] = h[:]
                 for lo in range(0, width, BANK_TOKENS):
-                    place = BANK_BYTES * len(banks)
+                    offset = BANK_BYTES * len(banks)
                     x = last_raw.tile(
-                        [P, BANK_TOKENS, PACK], F32, name="relu_vector%d" % place, align_bytes=64, offset=place
+                        [P, BANK_TOKENS, PACK], F32, name="relu_vector%d" % offset, align_bytes=64, offset=offset
                     )
-                    a = keys(j0 + lo, b, next_value_bank([P, PACK, BANK_TOKENS]))
+                    a = keys(j0 + lo, BANK_TOKENS, b, 0, next_value_bank([P, PACK, BANK_TOKENS]))
                     banks.append((a, x[:], h[:, lo : lo + BANK_TOKENS, :]))
             return banks
 
@@ -250,19 +285,22 @@ def tile_list_rwkv_channel_mix_kernel(
                     a, x, h = banks[i - 1]
                     nc.vector.scalar_tensor_tensor(out=h, in0=a, scalar=0.0, in1=x, op0=ALU.max, op1=ALU.mult)
 
-        def quantize_h(c, b):
+        def quantize_h(step):
+            c, b = step
             j0, width = CHUNKS[c]
             cols = slice(j0, j0 + width)
             nc.vector.quantize_mx(
-                out=h_w[:, b, cols].bitcast(FP8X4), scales=h_s[:, b, cols], in_=h_of[(c, b)].rearrange("p j t -> p (j t)")
+                out=h_w[:, b, cols].bitcast(FP8X4), scales=h_s[:, b, cols], in_=h_of[step].rearrange("p j t -> p (j t)")
             )
 
         y_of = {}
+        gated = {}
 
         def tiles_a_bank(c):
             return 1 if c == LAST_CHUNK else BANK // CHUNKS[c][1]
 
-        def values(c, b):
+        def values(step):
+            c, b = step
             j0, width = CHUNKS[c]
             cols = slice(j0, j0 + width)
             share = tiles_a_bank(c)
@@ -282,6 +320,8 @@ def tile_list_rwkv_channel_mix_kernel(
         def gate_values(c, n0):
             j0, width = CHUNKS[c]
             share = tiles_a_bank(c)
+            if n0 == 0:
+                gated[c] = float_tile(("gate", c), [P, N_TILES, width])
             nc.vector.tensor_tensor(
                 out=gated[c][:, n0 : n0 + share, :],
                 in0=y_of[c][n0 // share][:],
@@ -289,87 +329,102 @@ def tile_list_rwkv_channel_mix_kernel(
                 op=ALU.mult,
             )
 
-        def add_and_store(c, n0):
+        def gate_chunk(c):
+            for n0 in range(0, N_TILES, tiles_a_bank(c)):
+                gate_values(c, n0)
+
+        def add_and_store(c, n):
             j0, width = CHUNKS[c]
-            count = TILES_A_RESULT[c]
-            shape = [P, count, width]
-            name = "result%d_%d" % (c, n0)
-            if (c, n0) in held_in:
-                pool, i = held_in[(c, n0)]
-                result = pool.tile(shape, F32, name=name, align_bytes=64, offset=4 * count * width * i)
-            else:
-                result = keep.tile(shape, F32, name=name, align_bytes=64)
-            if j0 < FUSED_TOKENS:
-                for n in range(n0, n0 + count):
-                    nc.vector.tensor_tensor(
-                        out=result[:, n - n0, :],
-                        in0=g_tab[n][:].indirect(listed(j0, width)),
-                        in1=gated[c][:, n, :],
-                        op=ALU.add,
-                    )
-            else:
-                lo = j0 - FUSED_TOKENS
-                nc.vector.tensor_tensor(
-                    out=result[:],
-                    in0=gated[c][:, n0 : n0 + count, :],
-                    in1=resid[:, n0 : n0 + count, lo : lo + width],
-                    op=ALU.add,
-                )
-            nc.sync.dma_start(out=out_rows[:, n0 : n0 + count, j0 : j0 + width], in_=result[:])
+            result = float_tile(("add", c, n), [P, width])
+            residual = resid[:, n, :] if c == LAST_CHUNK else g_tab[n][:].indirect(listed(j0, width))
+            nc.vector.tensor_tensor(out=result[:], in0=residual, in1=gated[c][:, n, :], op=ALU.add)
+            nc.sync.dma_start(out=out_rows[:, n, j0 : j0 + width], in_=result[:])
 
         nc.vector.tensor_copy(v_s[:], tab_s[:].bitcast(U8).indirect(offsets[:]))
         for j0, width in GATHERS:
             nc.vector.tensor_copy(v_w[:, j0 : j0 + width], tab_w[:].bitcast(U32).indirect(listed(j0, width)))
-            for c in range(LAST_CHUNK):
-                first, count = CHUNKS[c]
-                if j0 <= first < j0 + width:
-                    for n0 in range(0, N_TILES, BANK // count):
-                        receptance(c, n0, next_key_bank([P, BANK // count, count]))
+            last = min(j0 + width, LAST_TOKENS[0])
+            for first in range(j0, last, 2 * BANK_TOKENS):
+                count = min(2 * BANK_TOKENS, last - first)
+                share = PAIR if first == 0 else BANK // count
+                for n0 in range(0, N_TILES, share):
+                    receptance(first, count, n0, share, next_key_bank([P, share, count]))
         for b in range(PARTS):
             quantize_wk(b)
 
-        scalar_steps = [step for step in STEPS if step not in VECTOR_STEPS]
-        early = scalar_steps.index((0, LAST_PART))
-        for step in scalar_steps[:early]:
-            scalar_relu(step)
-            if step not in GPSIMD_STEPS:
-                scalar_square(step)
+        relus((0, 0))
+        square((0, 0))
+        relus((1, 0))
+        relus((0, 1))
+        square((0, 1))
+        relus((1, 1))
+        relu((2, 0), 0)
         banks = vector_keys()
-        gpsimd_squares()
+        gpsimd_square((1, 0), last_rounded[0], 0)
+        gpsimd_square((1, 1), last_rounded[0], HALF_BYTES)
         vector_run(banks)
 
-        late = scalar_steps[early:]
-        scalar_relu(late[0])
-        scalar_relu(late[1])
-        scalar_square(late[0])
-        shared = GPSIMD_STEPS[0]
-        nc.scalar.activation(
-            out=h_of[shared][:, GPSIMD_FIRST_TOKENS:, :], in_=relu_of[shared][:, GPSIMD_FIRST_TOKENS:, :], func=ACT.Square
-        )
+        relus((0, 3))
+        relus((1, 3))
+        square((0, 3))
+        square((1, 0))
         for b in range(PARTS):
-            quantize_h(0, b)
-            values(0, b)
-        for i in range(2, len(late)):
-            scalar_relu(late[i])
-            scalar_square(late[i - 1])
-        scalar_square(late[-1])
-        receptance(LAST_CHUNK, 0, bank_tile("last_gate", key_turns[-2], [P, N_TILES, CHUNKS[LAST_CHUNK][1]]))
+            quantize_h((0, b))
+            values((0, b))
+        for b in range(LAST_PART):
+            quantize_h((1, b))
+        gate_chunk(0)
+        relu((2, 0), 1)
+        square((1, 3))
+        quantize_h((1, 3))
+        gpsimd_square((2, 0), window_h, 0)
+        square((2, 0))
+        quantize_h((2, 0))
+        add_and_store(0, 0)
+        relus((2, 1))
+        for b in range(PARTS):
+            values((1, b))
+        gate_chunk(1)
+        gpsimd_square((2, 1), window_h, 0)
+        relus((2, 2))
+        square((2, 1))
+        relus((2, 3))
+        square((2, 2))
+        relus((3, 0))
+        square((2, 3))
+        relus((4, 0))
+        gpsimd_square((4, 0), *place[("gate", 1)])
+        square((3, 0))
+        relus((3, 1))
+        relus((3, 2))
+        square((3, 1))
+        relus((3, 3))
+        square((3, 2))
+        relus((4, 1))
+        square((3, 3))
+        square((4, 0))
+        relus((4, 2))
+        square((4, 1))
+        relus((4, 3))
+        square((4, 2))
+        square((4, 3))
+        receptance(*LAST_TOKENS, 0, N_TILES, bank_tile("last_gate", key_turns[-2], [P, N_TILES, LAST_TOKENS[1]]))
 
-        for c in range(1, len(CHUNKS)):
+        for c in range(2, len(CHUNKS)):
             for b in range(PARTS):
-                quantize_h(c, b)
-        for c in range(len(CHUNKS)):
-            if c >= 1:
-                for b in range(PARTS):
-                    values(c, b)
+                if (c, b) != (2, 0):
+                    quantize_h((c, b))
+        for c in range(2, len(CHUNKS)):
+            for b in range(PARTS):
+                values((c, b))
             if c < LAST_CHUNK:
-                for n0 in range(0, N_TILES, tiles_a_bank(c)):
-                    gate_values(c, n0)
+                gate_chunk(c)
         for n in range(N_TILES):
-            nc.vector.tensor_copy(resid[:, n, :], g_tab[n][:].indirect(listed(FUSED_TOKENS, S - FUSED_TOKENS)))
+            nc.vector.tensor_copy(resid[:, n, :], g_tab[n][:].indirect(listed(*LAST_TOKENS)))
         for c in range(LAST_CHUNK):
-            for n0 in range(0, N_TILES, TILES_A_RESULT[c]):
-                add_and_store(c, n0)
+            for n in range(N_TILES):
+                if (c, n) != (0, 0):
+                    add_and_store(c, n)
         for n in range(N_TILES + ADD_LAG):
             if n < N_TILES:
                 gate_values(LAST_CHUNK, n)

@@ -28,7 +28,6 @@ LIST_ROWS = 16
 BANK = 512
 BANK_BYTES = 4 * BANK
 BANK_TOKENS = BANK // PACK
-HALF_BYTES = 2048
 PAIR = 2
 
 GATHERS = [(0, 128), (128, 128), (256, 256), (512, 512)]
@@ -36,7 +35,9 @@ CHUNKS = [(0, 256), (256, 256), (512, 256), (768, 128), (896, 128)]
 LAST_CHUNK = len(CHUNKS) - 1
 LAST_TOKENS = CHUNKS[LAST_CHUNK]
 VECTOR_STEPS = [(0, LAST_PART - 1), (1, LAST_PART - 1)]
-GPSIMD_TOKENS = {(1, 0): 160, (1, 1): 256, (2, 0): 96, (2, 1): 64, (LAST_CHUNK, 0): 64}
+GPSIMD_TOKENS = {(2, 0): 96, (2, 1): 64, (LAST_CHUNK, 0): 64}
+JOINT_STEPS = [(1, 0), (1, 1)]
+JOINT_FIRST = 64
 WAITING_SQUARE = (0, LAST_PART - 2)
 HELD = {
     (2, 0): [("add", 0, 0), ("gate", 1)],
@@ -170,7 +171,7 @@ def tile_list_rwkv_channel_mix_kernel(
             for u in range(PACK // PAIR):
                 name = "rounded%d_%d" % (b, u)
                 if b == LAST_PART:
-                    half = last_rounded[u].tile([P, PAIR, P, PACK], BF16, name=name, align_bytes=64, offset=HALF_BYTES // 2)
+                    half = last_rounded[u].tile([P, PAIR, P, PACK], BF16, name=name, align_bytes=64, offset=0)
                 else:
                     half = keep.tile([P, PAIR, P, PACK], BF16, name=name, align_bytes=64)
                 rounded.append(half)
@@ -205,14 +206,18 @@ def tile_list_rwkv_channel_mix_kernel(
         h_of = {}
 
         def paired(step):
-            return CHUNKS[step[0]][1] > BANK_TOKENS and step not in GPSIMD_TOKENS
+            return CHUNKS[step[0]][1] > BANK_TOKENS and step not in GPSIMD_TOKENS and step not in JOINT_STEPS
+
+        joint_relu = keep.tile([P, len(JOINT_STEPS), CHUNKS[1][1], PACK], F32, name="joint_relu")
 
         def relu(step, i):
             c, b = step
             j0, width = CHUNKS[c]
             if i == 0:
                 shape = [P, PACK // PAIR, width, PAIR] if paired(step) else [P, width, PACK]
-                if step in holder:
+                if step in JOINT_STEPS:
+                    x = joint_relu[:, JOINT_STEPS.index(step)]
+                elif step in holder:
                     x = holder[step].tile(shape, F32, name="relu%d_%d" % step, align_bytes=64, offset=0)
                 elif step in GPSIMD_TOKENS:
                     x = keep.tile(shape, F32, name="relu%d_%d" % step)
@@ -232,6 +237,11 @@ def tile_list_rwkv_channel_mix_kernel(
                 relu(step, i)
 
         def square(step):
+            if step == JOINT_STEPS[0]:
+                nc.scalar.activation(
+                    out=h_of[step][:, :JOINT_FIRST, :], in_=relu_of[step][:, :JOINT_FIRST, :], func=ACT.Square
+                )
+                return
             if step in GPSIMD_TOKENS:
                 lo = GPSIMD_TOKENS[step]
                 nc.scalar.activation(out=h_of[step][:, lo:, :], in_=relu_of[step][:, lo:, :], func=ACT.Square)
@@ -256,6 +266,17 @@ def tile_list_rwkv_channel_mix_kernel(
             h_of[step] = h[:]
             x = relu_of[step][:, : GPSIMD_TOKENS[step], :]
             nc.gpsimd.tensor_tensor(out=h[:, : GPSIMD_TOKENS[step], :], in0=x, in1=x, op=ALU.mult)
+
+        def joint_square():
+            h = last_rounded[0].tile(
+                [P, len(JOINT_STEPS), CHUNKS[1][1], PACK], BF16, name="h_joint", align_bytes=64, offset=0
+            )
+            for i, step in enumerate(JOINT_STEPS):
+                h_of[step] = h[:, i]
+            x = joint_relu[:].rearrange("p s j t -> p (s j) t")[:, JOINT_FIRST:, :]
+            nc.gpsimd.tensor_tensor(
+                out=h[:].rearrange("p s j t -> p (s j) t")[:, JOINT_FIRST:, :], in0=x, in1=x, op=ALU.mult
+            )
 
         def vector_keys():
             banks = []
@@ -297,7 +318,7 @@ def tile_list_rwkv_channel_mix_kernel(
         gated = {}
 
         def tiles_a_bank(c):
-            return 1 if c == LAST_CHUNK else BANK // CHUNKS[c][1]
+            return 1 if c == LAST_CHUNK else PAIR
 
         def values(step):
             c, b = step
@@ -355,13 +376,12 @@ def tile_list_rwkv_channel_mix_kernel(
         relus((0, 0))
         square((0, 0))
         relus((1, 0))
+        relus((1, 1))
         relus((0, 1))
         square((0, 1))
-        relus((1, 1))
         relu((2, 0), 0)
         banks = vector_keys()
-        gpsimd_square((1, 0), last_rounded[0], 0)
-        gpsimd_square((1, 1), last_rounded[0], HALF_BYTES)
+        joint_square()
         vector_run(banks)
 
         relus((0, 3))
@@ -375,13 +395,14 @@ def tile_list_rwkv_channel_mix_kernel(
             quantize_h((1, b))
         gate_chunk(0)
         relu((2, 0), 1)
+        relu((2, 1), 0)
         square((1, 3))
         quantize_h((1, 3))
         gpsimd_square((2, 0), window_h, 0)
         square((2, 0))
         quantize_h((2, 0))
         add_and_store(0, 0)
-        relus((2, 1))
+        relu((2, 1), 1)
         for b in range(PARTS):
             values((1, b))
         gate_chunk(1)
@@ -400,8 +421,8 @@ def tile_list_rwkv_channel_mix_kernel(
         square((3, 1))
         relus((3, 3))
         square((3, 2))
-        relus((4, 1))
         square((3, 3))
+        relus((4, 1))
         square((4, 0))
         relus((4, 2))
         square((4, 1))

@@ -30,14 +30,15 @@ BANK_BYTES = 4 * BANK
 BANK_TOKENS = BANK // PACK
 PAIR = 2
 
-GATHERS = [(0, 128), (128, 128), (256, 256), (512, 512)]
+GATHERS = [(0, 128), (128, 128), (256, 256), (512, 384)]
 CHUNKS = [(0, 256), (256, 256), (512, 256), (768, 128), (896, 128)]
 LAST_CHUNK = len(CHUNKS) - 1
 LAST_TOKENS = CHUNKS[LAST_CHUNK]
 VECTOR_STEPS = [(0, LAST_PART - 1), (1, LAST_PART - 1)]
-GPSIMD_TOKENS = {(2, 0): 96, (2, 1): 64, (LAST_CHUNK, 0): 64}
 JOINT_STEPS = [(1, 0), (1, 1)]
-JOINT_FIRST = 64
+JOINT_FIRST = 48
+WINDOW_STEPS = [(2, 0), (2, 1), (LAST_CHUNK, 0)]
+GPSIMD_TOKENS = dict(zip(WINDOW_STEPS, [80, 64, 64]))
 WAITING_SQUARE = (0, LAST_PART - 2)
 HELD = {
     (2, 0): [("add", 0, 0), ("gate", 1)],
@@ -68,6 +69,7 @@ def tile_list_rwkv_channel_mix_kernel(
         psum = ctx.enter_context(tc.psum_pool(name="psum", bufs=1))
         last_raw = ctx.enter_context(tc.tile_pool(name="last_raw", bufs=1))
         last_rounded = [ctx.enter_context(tc.tile_pool(name="last_rounded%d" % u, bufs=1)) for u in range(PACK // PAIR)]
+        first_raw = ctx.enter_context(tc.tile_pool(name="first_raw", bufs=1))
         window_h = ctx.enter_context(tc.tile_pool(name="window_h", bufs=1))
         holder = {}
         place = {}
@@ -124,7 +126,8 @@ def tile_list_rwkv_channel_mix_kernel(
             load_wr_scales(r)
 
         wk_rows = wk.rearrange("(p j) c -> p j c", j=PACK)
-        wk_raw = [keep.tile([P, PACK, PASS], F32, name="wk_raw%d" % b, align_bytes=64) for b in range(LAST_PART)]
+        wk_raw = [first_raw.tile([P, PACK, PASS], F32, name="wk_raw0", align_bytes=64, offset=0)]
+        wk_raw.extend(keep.tile([P, PACK, PASS], F32, name="wk_raw%d" % b, align_bytes=64) for b in range(1, LAST_PART))
         wk_raw.append(last_raw.tile([P, PACK, PASS], F32, name="wk_raw_last", align_bytes=64, offset=0))
         g_tab = [keep.tile([P, T], F32, name="g_tab%d" % n) for n in range(N_TILES)]
         for b in range(PARTS):
@@ -138,7 +141,8 @@ def tile_list_rwkv_channel_mix_kernel(
         for n in range(N_TILES):
             nc.sync.dma_start(out=g_tab[n][:], in_=gT[n * P : (n + 1) * P, :])
 
-        v_w = keep.tile([P, S], U32, name="v_w", align_bytes=64)
+        v_w = keep.tile([P, LAST_TOKENS[0]], U32, name="v_w", align_bytes=64)
+        v_w_last = first_raw.tile([P, LAST_TOKENS[1]], U32, name="v_w_last", align_bytes=64, offset=0)
         v_s = keep.tile([P, S], U8, name="v_s", align_bytes=64)
         wk_w = [keep.tile([P, PASS], U32, name="wk_w%d" % b, align_bytes=64) for b in range(PARTS)]
         wk_s = [keep.tile([P, PASS], U8, name="wk_s%d" % b, align_bytes=64) for b in range(PARTS)]
@@ -151,6 +155,9 @@ def tile_list_rwkv_channel_mix_kernel(
         def listed(j0, width):
             return offsets[:, j0 // LIST_ROWS : (j0 + width) // LIST_ROWS]
 
+        def words(j0, width):
+            return v_w_last[:] if j0 == LAST_TOKENS[0] else v_w[:, j0 : j0 + width]
+
         def receptance(j0, width, n0, share, z):
             cols = slice(j0, j0 + width)
             for i in range(share):
@@ -159,7 +166,7 @@ def tile_list_rwkv_channel_mix_kernel(
                     out=z[:, i, :],
                     lhsT=wr_w[:, 2 * P * n : 2 * P * (n + 1)].bitcast(FP4X4),
                     lhsT_scale=wr_s[:, P * n : P * (n + 1)],
-                    rhs=v_w[:, cols].bitcast(FP8X4),
+                    rhs=words(j0, width).bitcast(FP8X4),
                     rhs_scale=v_s[:, cols],
                     start=True,
                     stop=True,
@@ -195,7 +202,7 @@ def tile_list_rwkv_channel_mix_kernel(
                     out=bank[:, t, :],
                     lhsT=wk_w[b][:, first : first + P].bitcast(FP8X4),
                     lhsT_scale=wk_s[b][:, first : first + P],
-                    rhs=v_w[:, cols].bitcast(FP8X4),
+                    rhs=words(j0, width).bitcast(FP8X4),
                     rhs_scale=v_s[:, cols],
                     start=True,
                     stop=True,
@@ -364,76 +371,72 @@ def tile_list_rwkv_channel_mix_kernel(
         nc.vector.tensor_copy(v_s[:], tab_s[:].bitcast(U8).indirect(offsets[:]))
         for j0, width in GATHERS:
             nc.vector.tensor_copy(v_w[:, j0 : j0 + width], tab_w[:].bitcast(U32).indirect(listed(j0, width)))
-            last = min(j0 + width, LAST_TOKENS[0])
-            for first in range(j0, last, 2 * BANK_TOKENS):
-                count = min(2 * BANK_TOKENS, last - first)
+            for first in range(j0, j0 + width, 2 * BANK_TOKENS):
+                count = min(2 * BANK_TOKENS, j0 + width - first)
                 share = PAIR if first == 0 else BANK // count
                 for n0 in range(0, N_TILES, share):
                     receptance(first, count, n0, share, next_key_bank([P, share, count]))
         for b in range(PARTS):
             quantize_wk(b)
+        nc.vector.tensor_copy(v_w_last[:], tab_w[:].bitcast(U32).indirect(listed(*LAST_TOKENS)))
 
         relus((0, 0))
         square((0, 0))
-        relus((1, 0))
-        relus((1, 1))
-        relus((0, 1))
-        square((0, 1))
-        relu((2, 0), 0)
+        for step in JOINT_STEPS:
+            relus(step)
+        relus(WAITING_SQUARE)
+        square(WAITING_SQUARE)
+        relu(WINDOW_STEPS[0], 0)
         banks = vector_keys()
         joint_square()
         vector_run(banks)
 
-        relus((0, 3))
-        relus((1, 3))
-        square((0, 3))
-        square((1, 0))
+        relus((0, LAST_PART))
+        relus((1, LAST_PART))
+        square((0, LAST_PART))
+        square(JOINT_STEPS[0])
         for b in range(PARTS):
             quantize_h((0, b))
             values((0, b))
         for b in range(LAST_PART):
             quantize_h((1, b))
         gate_chunk(0)
-        relu((2, 0), 1)
-        relu((2, 1), 0)
-        square((1, 3))
-        quantize_h((1, 3))
-        gpsimd_square((2, 0), window_h, 0)
-        square((2, 0))
-        quantize_h((2, 0))
+        relu(WINDOW_STEPS[0], 1)
+        relu(WINDOW_STEPS[1], 0)
+        square((1, LAST_PART))
+        quantize_h((1, LAST_PART))
+        gpsimd_square(WINDOW_STEPS[0], window_h, 0)
+        square(WINDOW_STEPS[0])
+        quantize_h(WINDOW_STEPS[0])
         add_and_store(0, 0)
-        relu((2, 1), 1)
+        relu(WINDOW_STEPS[1], 1)
         for b in range(PARTS):
             values((1, b))
         gate_chunk(1)
-        gpsimd_square((2, 1), window_h, 0)
-        relus((2, 2))
-        square((2, 1))
-        relus((2, 3))
-        square((2, 2))
+        gpsimd_square(WINDOW_STEPS[1], window_h, 0)
+
+        for b in range(2, PARTS):
+            relus((2, b))
+            square((2, b - 1))
         relus((3, 0))
-        square((2, 3))
-        relus((4, 0))
-        gpsimd_square((4, 0), *place[("gate", 1)])
+        square((2, LAST_PART))
+        relus(WINDOW_STEPS[2])
+        gpsimd_square(WINDOW_STEPS[2], *place[("gate", 1)])
         square((3, 0))
         relus((3, 1))
-        relus((3, 2))
-        square((3, 1))
-        relus((3, 3))
-        square((3, 2))
-        square((3, 3))
-        relus((4, 1))
-        square((4, 0))
-        relus((4, 2))
-        square((4, 1))
-        relus((4, 3))
-        square((4, 2))
-        square((4, 3))
+        for b in range(2, PARTS):
+            relus((3, b))
+            square((3, b - 1))
+        square((3, LAST_PART))
+        for b in range(1, PARTS):
+            relus((LAST_CHUNK, b))
+            square((LAST_CHUNK, b - 1))
+        square((LAST_CHUNK, LAST_PART))
         receptance(*LAST_TOKENS, 0, N_TILES, bank_tile("last_gate", key_turns[-2], [P, N_TILES, LAST_TOKENS[1]]))
 
         for c in range(2, len(CHUNKS)):
             for b in range(PARTS):
-                if (c, b) != (2, 0):
+                if (c, b) != WINDOW_STEPS[0]:
                     quantize_h((c, b))
         for c in range(2, len(CHUNKS)):
             for b in range(PARTS):

@@ -47,10 +47,11 @@ HELD = {
     (3, 0): [("gate", 2)],
     (3, 2): [("add", 2, 1)],
     (3, LAST_PART): [("add", 2, 2)],
-    (LAST_CHUNK, 1): [("add", 3, 0), ("add", 3, 1), ("add", 3, 2)],
+    (LAST_CHUNK, 1): [("add", 3, 0)],
     (LAST_CHUNK, 2): [("add", 3, 3)],
     (LAST_CHUNK, LAST_PART): [("add", 2, 3)],
 }
+SHARED_STORES = {(3, 0): 3}
 ADD_LAG = 2
 
 RELU_BUFS = 2
@@ -361,12 +362,15 @@ def tile_list_rwkv_channel_mix_kernel(
             for n0 in range(0, N_TILES, tiles_a_bank(c)):
                 gate_values(c, n0)
 
-        def add_and_store(c, n):
+        def add_and_store(c, n0):
             j0, width = CHUNKS[c]
-            result = float_tile(("add", c, n), [P, width])
-            residual = resid[:, n, :] if c == LAST_CHUNK else g_tab[n][:].indirect(listed(j0, width))
-            nc.vector.tensor_tensor(out=result[:], in0=residual, in1=gated[c][:, n, :], op=ALU.add)
-            nc.sync.dma_start(out=out_rows[:, n, j0 : j0 + width], in_=result[:])
+            count = SHARED_STORES.get((c, n0), 1)
+            result = float_tile(("add", c, n0), [P, count, width])
+            for n in range(n0, n0 + count):
+                residual = resid[:, n, :] if c == LAST_CHUNK else g_tab[n][:].indirect(listed(j0, width))
+                nc.vector.tensor_tensor(out=result[:, n - n0, :], in0=residual, in1=gated[c][:, n, :], op=ALU.add)
+            nc.sync.dma_start(out=out_rows[:, n0 : n0 + count, j0 : j0 + width], in_=result[:])
+            return count
 
         nc.vector.tensor_copy(v_s[:], tab_s[:].bitcast(U8).indirect(offsets[:]))
         for j0, width in GATHERS:
@@ -446,9 +450,9 @@ def tile_list_rwkv_channel_mix_kernel(
         for n in range(N_TILES):
             nc.vector.tensor_copy(resid[:, n, :], g_tab[n][:].indirect(listed(*LAST_TOKENS)))
         for c in range(LAST_CHUNK):
-            for n in range(N_TILES):
-                if (c, n) != (0, 0):
-                    add_and_store(c, n)
+            n = 1 if c == 0 else 0
+            while n < N_TILES:
+                n = n + add_and_store(c, n)
         for n in range(N_TILES + ADD_LAG):
             if n < N_TILES:
                 gate_values(LAST_CHUNK, n)

@@ -30,15 +30,15 @@ BANK_BYTES = 4 * BANK
 BANK_TOKENS = BANK // PACK
 PAIR = 2
 
-GATHERS = [(0, 128), (128, 128), (256, 256), (512, 384)]
+GATHERS = [(0, 128), (128, 128), (256, 256), (512, 512)]
 CHUNKS = [(0, 256), (256, 256), (512, 256), (768, 128), (896, 128)]
 LAST_CHUNK = len(CHUNKS) - 1
 LAST_TOKENS = CHUNKS[LAST_CHUNK]
 VECTOR_STEPS = [(0, LAST_PART - 1), (1, LAST_PART - 1)]
 JOINT_STEPS = [(1, 0), (1, 1)]
-JOINT_FIRST = 48
+JOINT_FIRST = 64
 WINDOW_STEPS = [(2, 0), (2, 1), (LAST_CHUNK, 0)]
-GPSIMD_TOKENS = dict(zip(WINDOW_STEPS, [80, 64, 64]))
+GPSIMD_TOKENS = dict(zip(WINDOW_STEPS, [96, 64, 64]))
 WAITING_SQUARE = (0, LAST_PART - 2)
 HELD = {
     (2, 0): [("add", 0, 0), ("gate", 1)],
@@ -70,7 +70,6 @@ def tile_list_rwkv_channel_mix_kernel(
         psum = ctx.enter_context(tc.psum_pool(name="psum", bufs=1))
         last_raw = ctx.enter_context(tc.tile_pool(name="last_raw", bufs=1))
         last_rounded = [ctx.enter_context(tc.tile_pool(name="last_rounded%d" % u, bufs=1)) for u in range(PACK // PAIR)]
-        first_raw = ctx.enter_context(tc.tile_pool(name="first_raw", bufs=1))
         window_h = ctx.enter_context(tc.tile_pool(name="window_h", bufs=1))
         holder = {}
         place = {}
@@ -127,8 +126,7 @@ def tile_list_rwkv_channel_mix_kernel(
             load_wr_scales(r)
 
         wk_rows = wk.rearrange("(p j) c -> p j c", j=PACK)
-        wk_raw = [first_raw.tile([P, PACK, PASS], F32, name="wk_raw0", align_bytes=64, offset=0)]
-        wk_raw.extend(keep.tile([P, PACK, PASS], F32, name="wk_raw%d" % b, align_bytes=64) for b in range(1, LAST_PART))
+        wk_raw = [keep.tile([P, PACK, PASS], F32, name="wk_raw%d" % b, align_bytes=64) for b in range(LAST_PART)]
         wk_raw.append(last_raw.tile([P, PACK, PASS], F32, name="wk_raw_last", align_bytes=64, offset=0))
         g_tab = [keep.tile([P, T], F32, name="g_tab%d" % n) for n in range(N_TILES)]
         for b in range(PARTS):
@@ -142,8 +140,7 @@ def tile_list_rwkv_channel_mix_kernel(
         for n in range(N_TILES):
             nc.sync.dma_start(out=g_tab[n][:], in_=gT[n * P : (n + 1) * P, :])
 
-        v_w = keep.tile([P, LAST_TOKENS[0]], U32, name="v_w", align_bytes=64)
-        v_w_last = first_raw.tile([P, LAST_TOKENS[1]], U32, name="v_w_last", align_bytes=64, offset=0)
+        v_w = keep.tile([P, S], U32, name="v_w", align_bytes=64)
         v_s = keep.tile([P, S], U8, name="v_s", align_bytes=64)
         wk_w = [keep.tile([P, PASS], U32, name="wk_w%d" % b, align_bytes=64) for b in range(PARTS)]
         wk_s = [keep.tile([P, PASS], U8, name="wk_s%d" % b, align_bytes=64) for b in range(PARTS)]
@@ -156,9 +153,6 @@ def tile_list_rwkv_channel_mix_kernel(
         def listed(j0, width):
             return offsets[:, j0 // LIST_ROWS : (j0 + width) // LIST_ROWS]
 
-        def words(j0, width):
-            return v_w_last[:] if j0 == LAST_TOKENS[0] else v_w[:, j0 : j0 + width]
-
         def receptance(j0, width, n0, share, z):
             cols = slice(j0, j0 + width)
             for i in range(share):
@@ -167,7 +161,7 @@ def tile_list_rwkv_channel_mix_kernel(
                     out=z[:, i, :],
                     lhsT=wr_w[:, 2 * P * n : 2 * P * (n + 1)].bitcast(FP4X4),
                     lhsT_scale=wr_s[:, P * n : P * (n + 1)],
-                    rhs=words(j0, width).bitcast(FP8X4),
+                    rhs=v_w[:, cols].bitcast(FP8X4),
                     rhs_scale=v_s[:, cols],
                     start=True,
                     stop=True,
@@ -203,7 +197,7 @@ def tile_list_rwkv_channel_mix_kernel(
                     out=bank[:, t, :],
                     lhsT=wk_w[b][:, first : first + P].bitcast(FP8X4),
                     lhsT_scale=wk_s[b][:, first : first + P],
-                    rhs=words(j0, width).bitcast(FP8X4),
+                    rhs=v_w[:, cols].bitcast(FP8X4),
                     rhs_scale=v_s[:, cols],
                     start=True,
                     stop=True,
@@ -375,14 +369,14 @@ def tile_list_rwkv_channel_mix_kernel(
         nc.vector.tensor_copy(v_s[:], tab_s[:].bitcast(U8).indirect(offsets[:]))
         for j0, width in GATHERS:
             nc.vector.tensor_copy(v_w[:, j0 : j0 + width], tab_w[:].bitcast(U32).indirect(listed(j0, width)))
-            for first in range(j0, j0 + width, 2 * BANK_TOKENS):
-                count = min(2 * BANK_TOKENS, j0 + width - first)
+            last = min(j0 + width, LAST_TOKENS[0])
+            for first in range(j0, last, 2 * BANK_TOKENS):
+                count = min(2 * BANK_TOKENS, last - first)
                 share = PAIR if first == 0 else BANK // count
                 for n0 in range(0, N_TILES, share):
                     receptance(first, count, n0, share, next_key_bank([P, share, count]))
         for b in range(PARTS):
             quantize_wk(b)
-        nc.vector.tensor_copy(v_w_last[:], tab_w[:].bitcast(U32).indirect(listed(*LAST_TOKENS)))
 
         relus((0, 0))
         square((0, 0))

@@ -109,21 +109,20 @@ def tile_list_rwkv_channel_mix_kernel(
         wv_s = keep.tile([P, N], U8, name="wv_s", align_bytes=64)
         wv_w = keep.tile([P, PARTS, N], I32, name="wv_w", align_bytes=64)
 
-        nc.vector.memset(wr_s[:].bitcast(I32), 0)
         nc.vector.memset(tab_s[:], 0)
+        nc.vector.memset(wr_s[:].bitcast(I32), 0)
         nc.vector.memset(wv_s[:].bitcast(I32), 0)
 
-        def load_wr_scales(r):
-            nc.sync.dma_start(out=wr_s[r:P:QUADRANT, :].bitcast(I32), in_=wr_scales[0, r:BLOCKS:PACK, :].bitcast(I32))
+        wr_rows = keep.tile([PACK, P // QUADRANT, N // 4], I32, name="wr_rows", align_bytes=64)
 
         nc.sync.dma_start(offsets[:], offs)
-        load_wr_scales(0)
+        nc.sync.dma_start(out=wr_rows[:], in_=wr_scales[0].bitcast(I32).rearrange("(q r) c -> r q c", r=PACK))
         for r in range(PACK):
             nc.sync.dma_start(out=tab_s[r:P:QUADRANT, :], in_=tab_scales[0, r:BLOCKS:PACK, :].bitcast(I32))
         nc.sync.dma_start(out=tab_w[:], in_=tab_words[0].rearrange("p t i -> p (t i)").bitcast(I32))
         nc.sync.dma_start(out=wr_w[:].bitcast(I32), in_=wr_words[0].bitcast(I32))
-        for r in range(1, PACK):
-            load_wr_scales(r)
+        for q in range(P // QUADRANT):
+            nc.vector.tensor_copy(wr_s[QUADRANT * q : QUADRANT * q + PACK, :].bitcast(I32), wr_rows[:, q, :])
 
         wk_rows = wk.rearrange("(p j) c -> p j c", j=PACK)
         wk_raw = [keep.tile([P, PACK, PASS], F32, name="wk_raw%d" % b, align_bytes=64) for b in range(LAST_PART)]
@@ -233,6 +232,16 @@ def tile_list_rwkv_channel_mix_kernel(
                 lo = BANK_TOKENS * i
                 a = keys(j0 + lo, BANK_TOKENS, b, 0, next_key_bank([P, PACK, BANK_TOKENS]))
                 nc.scalar.activation(out=relu_of[step][:, lo : lo + BANK_TOKENS, :], in_=a, func=ACT.Relu)
+
+        def early_relu(step):
+            c, b = step
+            j0, width = CHUNKS[c]
+            relu_of[step] = holder[step].tile([P, width, PACK], F32, name="relu%d_%d" % step, align_bytes=64, offset=0)
+            bank = bank_tile("early", KEY_BANKS + VALUE_BANKS - 1, [P, PACK, BANK_TOKENS])
+            a = keys(j0, BANK_TOKENS, b, 0, bank)
+            nc.vector.tensor_scalar(
+                out=relu_of[step][:, :BANK_TOKENS, :], in0=a, scalar1=0.0, scalar2=None, op0=ALU.max
+            )
 
         def relus(step):
             for i in range(CHUNKS[step[0]][1] // BANK_TOKENS):
@@ -377,6 +386,8 @@ def tile_list_rwkv_channel_mix_kernel(
                     receptance(first, count, n0, share, next_key_bank([P, share, count]))
         for b in range(PARTS):
             quantize_wk(b)
+            if b == 1:
+                early_relu(WINDOW_STEPS[0])
 
         relus((0, 0))
         square((0, 0))
@@ -384,7 +395,6 @@ def tile_list_rwkv_channel_mix_kernel(
             relus(step)
         relus(WAITING_SQUARE)
         square(WAITING_SQUARE)
-        relu(WINDOW_STEPS[0], 0)
         banks = vector_keys()
         joint_square()
         vector_run(banks)

@@ -119,8 +119,8 @@ def tile_list_rwkv_channel_mix_kernel(
         nc.sync.dma_start(out=wr_rows[:], in_=wr_scales[0].bitcast(I32).rearrange("(q r) c -> r q c", r=PACK))
         for r in range(PACK):
             nc.sync.dma_start(out=tab_s[r:P:QUADRANT, :], in_=tab_scales[0, r:BLOCKS:PACK, :].bitcast(I32))
-        nc.sync.dma_start(out=tab_w[:], in_=tab_words[0].rearrange("p t i -> p (t i)").bitcast(I32))
         nc.sync.dma_start(out=wr_w[:].bitcast(I32), in_=wr_words[0].bitcast(I32))
+        nc.sync.dma_start(out=tab_w[:], in_=tab_words[0].rearrange("p t i -> p (t i)").bitcast(I32))
         for q in range(P // QUADRANT):
             nc.vector.tensor_copy(wr_s[QUADRANT * q : QUADRANT * q + PACK, :].bitcast(I32), wr_rows[:, q, :])
 
@@ -232,16 +232,6 @@ def tile_list_rwkv_channel_mix_kernel(
                 lo = BANK_TOKENS * i
                 a = keys(j0 + lo, BANK_TOKENS, b, 0, next_key_bank([P, PACK, BANK_TOKENS]))
                 nc.scalar.activation(out=relu_of[step][:, lo : lo + BANK_TOKENS, :], in_=a, func=ACT.Relu)
-
-        def early_relu(step):
-            c, b = step
-            j0, width = CHUNKS[c]
-            relu_of[step] = holder[step].tile([P, width, PACK], F32, name="relu%d_%d" % step, align_bytes=64, offset=0)
-            bank = bank_tile("early", KEY_BANKS + VALUE_BANKS - 1, [P, PACK, BANK_TOKENS])
-            a = keys(j0, BANK_TOKENS, b, 0, bank)
-            nc.vector.tensor_scalar(
-                out=relu_of[step][:, :BANK_TOKENS, :], in0=a, scalar1=0.0, scalar2=None, op0=ALU.max
-            )
 
         def relus(step):
             for i in range(CHUNKS[step[0]][1] // BANK_TOKENS):
@@ -386,8 +376,6 @@ def tile_list_rwkv_channel_mix_kernel(
                     receptance(first, count, n0, share, next_key_bank([P, share, count]))
         for b in range(PARTS):
             quantize_wk(b)
-            if b == 1:
-                early_relu(WINDOW_STEPS[0])
 
         relus((0, 0))
         square((0, 0))
@@ -395,6 +383,7 @@ def tile_list_rwkv_channel_mix_kernel(
             relus(step)
         relus(WAITING_SQUARE)
         square(WAITING_SQUARE)
+        relu(WINDOW_STEPS[0], 0)
         banks = vector_keys()
         joint_square()
         vector_run(banks)

@@ -36,14 +36,14 @@ LAST_CHUNK = len(CHUNKS) - 1
 LAST_TOKENS = CHUNKS[LAST_CHUNK]
 VECTOR_STEPS = [(0, LAST_PART - 1), (1, LAST_PART - 1)]
 JOINT_STEPS = [(1, 0), (1, 1)]
-JOINT_FIRST = 64
+JOINT_FIRST = 32
 WINDOW_STEPS = [(2, 0), (2, 1), (LAST_CHUNK, 0)]
-GPSIMD_TOKENS = dict(zip(WINDOW_STEPS, [96, 64, 64]))
+GPSIMD_TOKENS = dict(zip(WINDOW_STEPS, [96, 96, 96]))
 WAITING_SQUARE = (0, LAST_PART - 2)
 HELD = {
     (2, 0): [("add", 0, 0), ("gate", 1)],
-    (2, 2): [("add", 0, 2), ("add", 1, 2)],
-    (2, LAST_PART): [("add", 0, 3), ("add", 1, 3)],
+    (2, 2): [("add", 0, 2)],
+    (2, LAST_PART): [("add", 0, 3)],
     (3, 0): [("gate", 2)],
     (3, 2): [("add", 2, 1)],
     (3, LAST_PART): [("add", 2, 2)],
@@ -71,6 +71,7 @@ def tile_list_rwkv_channel_mix_kernel(
         last_raw = ctx.enter_context(tc.tile_pool(name="last_raw", bufs=1))
         last_rounded = [ctx.enter_context(tc.tile_pool(name="last_rounded%d" % u, bufs=1)) for u in range(PACK // PAIR)]
         window_h = ctx.enter_context(tc.tile_pool(name="window_h", bufs=1))
+        joint_gated = ctx.enter_context(tc.tile_pool(name="joint_gated", bufs=1))
         holder = {}
         place = {}
         for step, outputs in HELD.items():
@@ -342,10 +343,25 @@ def tile_list_rwkv_channel_mix_kernel(
         def gate_values(c, n0):
             j0, width = CHUNKS[c]
             share = tiles_a_bank(c)
-            if n0 == 0:
-                gated[c] = float_tile(("gate", c), [P, N_TILES, width])
+            if c < PAIR and n0 == 0:
+                first = float_tile(("gate", c), [P, PAIR, width])
+                for n in range(PAIR):
+                    gated[(c, n)] = first[:, n, :]
+                product = first[:]
+            elif c < PAIR:
+                if c == 0:
+                    gated["joint"] = joint_gated.tile([P, PAIR, PAIR * width], F32, name="gate_joint", align_bytes=64, offset=0)
+                    for n in range(PAIR):
+                        gated[(c, PAIR + n)] = gated["joint"][:, n, :]
+                product = gated["joint"][:, :, j0 : j0 + width]
+            else:
+                if n0 == 0:
+                    gated[c] = float_tile(("gate", c), [P, N_TILES, width])
+                    for n in range(N_TILES):
+                        gated[(c, n)] = gated[c][:, n, :]
+                product = gated[c][:, n0 : n0 + share, :]
             nc.vector.tensor_tensor(
-                out=gated[c][:, n0 : n0 + share, :],
+                out=product,
                 in0=y_of[c][n0 // share][:],
                 in1=gate[:, n0 : n0 + share, j0 : j0 + width],
                 op=ALU.mult,
@@ -357,11 +373,13 @@ def tile_list_rwkv_channel_mix_kernel(
 
         def add_and_store(c, n0):
             j0, width = CHUNKS[c]
+            if c == 0 and n0 >= PAIR:
+                width = PAIR * width
             count = SHARED_STORES.get((c, n0), 1)
             result = float_tile(("add", c, n0), [P, count, width])
             for n in range(n0, n0 + count):
                 residual = resid[:, n, :] if c == LAST_CHUNK else g_tab[n][:].indirect(listed(j0, width))
-                nc.vector.tensor_tensor(out=result[:, n - n0, :], in0=residual, in1=gated[c][:, n, :], op=ALU.add)
+                nc.vector.tensor_tensor(out=result[:, n - n0, :], in0=residual, in1=gated[(c, n)], op=ALU.add)
             nc.sync.dma_start(out=out_rows[:, n0 : n0 + count, j0 : j0 + width], in_=result[:])
             return count
 
@@ -418,7 +436,7 @@ def tile_list_rwkv_channel_mix_kernel(
         relus((3, 0))
         square((2, LAST_PART))
         relus(WINDOW_STEPS[2])
-        gpsimd_square(WINDOW_STEPS[2], *place[("gate", 1)])
+        gpsimd_square(WINDOW_STEPS[2], joint_gated, 0)
         square((3, 0))
         relus((3, 1))
         for b in range(2, PARTS):
@@ -444,7 +462,7 @@ def tile_list_rwkv_channel_mix_kernel(
             nc.vector.tensor_copy(resid[:, n, :], g_tab[n][:].indirect(listed(*LAST_TOKENS)))
         for c in range(LAST_CHUNK):
             n = 1 if c == 0 else 0
-            while n < N_TILES:
+            while n < (PAIR if c == 1 else N_TILES):
                 n = n + add_and_store(c, n)
         for n in range(N_TILES + ADD_LAG):
             if n < N_TILES:

@@ -36,7 +36,8 @@ LAST_CHUNK = len(CHUNKS) - 1
 LAST_TOKENS = CHUNKS[LAST_CHUNK]
 VECTOR_STEPS = [(0, LAST_PART - 1), (1, LAST_PART - 1)]
 JOINT_STEPS = [(1, 0), (1, 1)]
-JOINT_FIRST = 32
+JOINT_FIRST = 64
+RUN_REST = 64
 WINDOW_STEPS = [(2, 0), (2, 1), (LAST_CHUNK, 0)]
 GPSIMD_TOKENS = dict(zip(WINDOW_STEPS, [96, 96, 96]))
 WAITING_SQUARE = (0, LAST_PART - 2)
@@ -306,6 +307,8 @@ def tile_list_rwkv_channel_mix_kernel(
                     nc.vector.tensor_scalar(out=x, in0=a, scalar1=0.0, scalar2=None, op0=ALU.max)
                 if i >= 1:
                     a, x, h = banks[i - 1]
+                    if i == len(banks):
+                        a, x, h = [part[:, : BANK_TOKENS - RUN_REST, :] for part in (a, x, h)]
                     nc.vector.scalar_tensor_tensor(out=h, in0=a, scalar=0.0, in1=x, op0=ALU.max, op1=ALU.mult)
 
         def quantize_h(step):
@@ -386,7 +389,7 @@ def tile_list_rwkv_channel_mix_kernel(
         nc.vector.tensor_copy(v_s[:], tab_s[:].bitcast(U8).indirect(offsets[:]))
         for j0, width in GATHERS:
             nc.vector.tensor_copy(v_w[:, j0 : j0 + width], tab_w[:].bitcast(U32).indirect(listed(j0, width)))
-            last = min(j0 + width, LAST_TOKENS[0])
+            last = min(j0 + width, CHUNKS[LAST_CHUNK - 1][0])
             for first in range(j0, last, 2 * BANK_TOKENS):
                 count = min(2 * BANK_TOKENS, last - first)
                 share = PAIR if first == 0 else BANK // count
@@ -409,6 +412,8 @@ def tile_list_rwkv_channel_mix_kernel(
         relus((0, LAST_PART))
         relus((1, LAST_PART))
         square((0, LAST_PART))
+        rest_x, rest_h = [part[:, BANK_TOKENS - RUN_REST :, :] for part in banks[-1][1:]]
+        nc.scalar.activation(out=rest_h, in_=rest_x, func=ACT.Square)
         square(JOINT_STEPS[0])
         for b in range(PARTS):
             quantize_h((0, b))
@@ -436,6 +441,7 @@ def tile_list_rwkv_channel_mix_kernel(
         relus((3, 0))
         square((2, LAST_PART))
         relus(WINDOW_STEPS[2])
+        receptance(*CHUNKS[3], 0, N_TILES, next_key_bank([P, N_TILES, CHUNKS[3][1]]))
         gpsimd_square(WINDOW_STEPS[2], joint_gated, 0)
         square((3, 0))
         relus((3, 1))

@@ -36,8 +36,8 @@ LAST_CHUNK = len(CHUNKS) - 1
 LAST_TOKENS = CHUNKS[LAST_CHUNK]
 VECTOR_STEPS = [(0, LAST_PART - 1), (1, LAST_PART - 1)]
 JOINT_STEPS = [(1, 0), (1, 1)]
-JOINT_FIRST = 64
-RUN_REST = 64
+JOINT_FIRST = 48
+RUN_REST = 32
 WINDOW_STEPS = [(2, 0), (2, 1), (LAST_CHUNK, 0)]
 GPSIMD_TOKENS = dict(zip(WINDOW_STEPS, [96, 96, 96]))
 WAITING_SQUARE = (0, LAST_PART - 2)

@@ -46,17 +46,18 @@ HELD = {
     (2, 2): [("add", 0, 2)],
     (2, LAST_PART): [("add", 0, 3)],
     (3, 0): [("gate", 2)],
-    (3, 2): [("add", 2, 1)],
-    (3, LAST_PART): [("add", 2, 2)],
+    (3, 1): [("add", 2, 1)],
+    (3, 2): [("add", 2, 2)],
+    (3, LAST_PART): [("add", 2, 3)],
     (LAST_CHUNK, 1): [("add", 3, 0)],
-    (LAST_CHUNK, 2): [("add", 3, 3)],
-    (LAST_CHUNK, LAST_PART): [("add", 2, 3)],
+    (LAST_CHUNK, 2): [("add", 3, 1)],
+    (LAST_CHUNK, LAST_PART): [("add", 3, 2)],
 }
-SHARED_STORES = {(3, 0): 3}
+SHARED_STORES = {(3, 2): 2}
 ADD_LAG = 2
 
 RELU_BUFS = 2
-SQUARE_BUFS = 6
+SQUARE_BUFS = 5
 KEY_BANKS = 4
 VALUE_BANKS = 4
 

from contextlib import ExitStack

import concourse.mybir as mybir

K, H, N, T, S = 512, 2048, 512, 2048, 1024
FLOPS = 2 * S * (K * H + K * N + H * N)

F32 = mybir.dt.float32
BF16 = mybir.dt.bfloat16
I32 = mybir.dt.int32
U32 = mybir.dt.uint32
U16 = mybir.dt.uint16
U8 = mybir.dt.uint8
FP8X4 = mybir.dt.float8_e4m3fn_x4
FP4X4 = mybir.dt.float4_e2m1fn_x4
ACT = mybir.ActivationFunctionType
ALU = mybir.AluOpType

P = 128
PACK = 4
PASS = P * PACK
BLOCKS = PASS // 32
QUADRANT = 32
PARTS = H // PASS
LAST_PART = PARTS - 1
N_TILES = N // P
LIST_ROWS = 16
BANK = 512
BANK_BYTES = 4 * BANK
BANK_TOKENS = BANK // PACK
PAIR = 2

GATHERS = [(0, 128), (128, 128), (256, 256), (512, 512)]
CHUNKS = [(0, 256), (256, 256), (512, 256), (768, 128), (896, 128)]
LAST_CHUNK = len(CHUNKS) - 1
LAST_TOKENS = CHUNKS[LAST_CHUNK]
VECTOR_STEPS = [(0, LAST_PART - 1), (1, LAST_PART - 1)]
JOINT_STEPS = [(1, 0), (1, 1)]
JOINT_FIRST = 48
RUN_REST = 32
WINDOW_STEPS = [(2, 0), (2, 1), (LAST_CHUNK, 0)]
GPSIMD_TOKENS = dict(zip(WINDOW_STEPS, [96, 96, 96]))
WAITING_SQUARE = (0, LAST_PART - 2)
HELD = {
    (2, 0): [("add", 0, 0), ("gate", 1)],
    (2, 2): [("add", 0, 2)],
    (2, LAST_PART): [("add", 0, 3)],
    (3, 0): [("gate", 2)],
    (3, 1): [("add", 2, 1)],
    (3, 2): [("add", 2, 2)],
    (3, LAST_PART): [("add", 2, 3)],
    (LAST_CHUNK, 1): [("add", 3, 0)],
    (LAST_CHUNK, 2): [("add", 3, 1)],
    (LAST_CHUNK, LAST_PART): [("add", 3, 2)],
}
SHARED_STORES = {(3, 2): 2}
ADD_LAG = 2

RELU_BUFS = 2
SQUARE_BUFS = 5
KEY_BANKS = 4
VALUE_BANKS = 4


def tile_list_rwkv_channel_mix_kernel(
    tc, tab_words, tab_scales, offs, wk, wr_words, wr_scales, wv_words, wv_scales, gT, out
):
    nc = tc.nc
    with ExitStack() as ctx:
        keep = ctx.enter_context(tc.tile_pool(name="keep", bufs=1))
        ring = ctx.enter_context(tc.tile_pool(name="ring", bufs=RELU_BUFS))
        psum = ctx.enter_context(tc.psum_pool(name="psum", bufs=1))
        last_raw = ctx.enter_context(tc.tile_pool(name="last_raw", bufs=1))
        last_rounded = [ctx.enter_context(tc.tile_pool(name="last_rounded%d" % u, bufs=1)) for u in range(PACK // PAIR)]
        window_h = ctx.enter_context(tc.tile_pool(name="window_h", bufs=1))
        joint_gated = ctx.enter_context(tc.tile_pool(name="joint_gated", bufs=1))
        holder = {}
        place = {}
        for step, outputs in HELD.items():
            holder[step] = ctx.enter_context(tc.tile_pool(name="holder%d_%d" % step, bufs=1))
            offset = 0
            for output in outputs:
                place[output] = (holder[step], offset)
                offset = offset + 4 * CHUNKS[output[1]][1]

        def float_tile(output, shape):
            name = "_".join(str(word) for word in output)
            if output in place:
                pool, offset = place[output]
                return pool.tile(shape, F32, name=name, align_bytes=64, offset=offset)
            return keep.tile(shape, F32, name=name, align_bytes=64)

        key_turns = []
        value_turns = []

        def bank_tile(name, bank, shape):
            return psum.tile(shape, F32, name=name, offset=BANK_BYTES * bank)

        def next_key_bank(shape):
            key_turns.append(len(key_turns) % KEY_BANKS)
            return bank_tile("key%d" % len(key_turns), key_turns[-1], shape)

        def next_value_bank(shape):
            value_turns.append(KEY_BANKS + len(value_turns) % VALUE_BANKS)
            return bank_tile("value%d" % len(value_turns), value_turns[-1], shape)

        offsets = keep.tile([P, S // LIST_ROWS], U16, name="offsets")
        tab_w = keep.tile([P, T], I32, name="tab_w", align_bytes=64)
        tab_s = keep.tile([P, T // 4], I32, name="tab_s", align_bytes=64)
        wr_w = keep.tile([P, 2 * N], U8, name="wr_w", align_bytes=64)
        wr_s = keep.tile([P, N], U8, name="wr_s", align_bytes=64)
        wv_s = keep.tile([P, N], U8, name="wv_s", align_bytes=64)
        wv_w = keep.tile([P, PARTS, N], I32, name="wv_w", align_bytes=64)

        nc.vector.memset(tab_s[:], 0)
        nc.vector.memset(wr_s[:].bitcast(I32), 0)
        nc.vector.memset(wv_s[:].bitcast(I32), 0)

        wr_rows = keep.tile([PACK, P // QUADRANT, N // 4], I32, name="wr_rows", align_bytes=64)

        nc.sync.dma_start(offsets[:], offs)
        nc.sync.dma_start(out=wr_rows[:], in_=wr_scales[0].bitcast(I32).rearrange("(q r) c -> r q c", r=PACK))
        for r in range(PACK):
            nc.sync.dma_start(out=tab_s[r:P:QUADRANT, :], in_=tab_scales[0, r:BLOCKS:PACK, :].bitcast(I32))
        nc.sync.dma_start(out=wr_w[:].bitcast(I32), in_=wr_words[0].bitcast(I32))
        nc.sync.dma_start(out=tab_w[:], in_=tab_words[0].rearrange("p t i -> p (t i)").bitcast(I32))
        for q in range(P // QUADRANT):
            nc.vector.tensor_copy(wr_s[QUADRANT * q : QUADRANT * q + PACK, :].bitcast(I32), wr_rows[:, q, :])

        wk_rows = wk.rearrange("(p j) c -> p j c", j=PACK)
        wk_raw = [keep.tile([P, PACK, PASS], F32, name="wk_raw%d" % b, align_bytes=64) for b in range(LAST_PART)]
        wk_raw.append(last_raw.tile([P, PACK, PASS], F32, name="wk_raw_last", align_bytes=64, offset=0))
        g_tab = [keep.tile([P, T], F32, name="g_tab%d" % n) for n in range(N_TILES)]
        for b in range(PARTS):
            nc.sync.dma_start(out=wk_raw[b][:], in_=wk_rows[:, :, b * PASS : (b + 1) * PASS])
        for q in range(P // QUADRANT):
            nc.sync.dma_start(
                out=wv_s[QUADRANT * q : QUADRANT * q + PACK * PARTS, :].bitcast(I32),
                in_=wv_scales[:, PACK * q : PACK * (q + 1), :].bitcast(I32),
            )
        nc.sync.dma_start(out=wv_w[:], in_=wv_words.rearrange("a p c i -> p a (c i)").bitcast(I32))
        for n in range(N_TILES):
            nc.sync.dma_start(out=g_tab[n][:], in_=gT[n * P : (n + 1) * P, :])

        v_w = keep.tile([P, S], U32, name="v_w", align_bytes=64)
        v_s = keep.tile([P, S], U8, name="v_s", align_bytes=64)
        wk_w = [keep.tile([P, PASS], U32, name="wk_w%d" % b, align_bytes=64) for b in range(PARTS)]
        wk_s = [keep.tile([P, PASS], U8, name="wk_s%d" % b, align_bytes=64) for b in range(PARTS)]
        gate = keep.tile([P, N_TILES, S], F32, name="gate")
        resid = keep.tile([P, N_TILES, LAST_TOKENS[1]], F32, name="resid")
        h_w = keep.tile([P, PARTS, S], U32, name="h_w", align_bytes=64)
        h_s = keep.tile([P, PARTS, S], U8, name="h_s", align_bytes=64)
        out_rows = out.rearrange("(n p) j -> p n j", p=P)

        def listed(j0, width):
            return offsets[:, j0 // LIST_ROWS : (j0 + width) // LIST_ROWS]

        def receptance(j0, width, n0, share, z):
            cols = slice(j0, j0 + width)
            for i in range(share):
                n = n0 + i
                nc.tensor.matmul_mx(
                    out=z[:, i, :],
                    lhsT=wr_w[:, 2 * P * n : 2 * P * (n + 1)].bitcast(FP4X4),
                    lhsT_scale=wr_s[:, P * n : P * (n + 1)],
                    rhs=v_w[:, cols].bitcast(FP8X4),
                    rhs_scale=v_s[:, cols],
                    start=True,
                    stop=True,
                )
            nc.scalar.activation(out=gate[:, n0 : n0 + share, cols], in_=z[:], func=ACT.Sigmoid)

        def quantize_wk(b):
            rounded = []
            for u in range(PACK // PAIR):
                name = "rounded%d_%d" % (b, u)
                if b == LAST_PART:
                    half = last_rounded[u].tile([P, PAIR, P, PACK], BF16, name=name, align_bytes=64, offset=0)
                else:
                    half = keep.tile([P, PAIR, P, PACK], BF16, name=name, align_bytes=64)
                rounded.append(half)
                nc.vector.tensor_copy(
                    out=half[:].rearrange("p t m j -> p m j t"),
                    in_=wk_raw[b][:].rearrange("p j (m t) -> p m j t", t=PACK)[:, :, :, PAIR * u : PAIR * (u + 1)],
                )
            for u in range(PACK // PAIR):
                cols = slice(PAIR * P * u, PAIR * P * (u + 1))
                nc.vector.quantize_mx(
                    out=wk_w[b][:, cols].bitcast(FP8X4),
                    scales=wk_s[b][:, cols],
                    in_=rounded[u][:].rearrange("p t m j -> p (t m j)"),
                )

        def keys(j0, width, b, t0, bank):
            cols = slice(j0, j0 + width)
            for t in range(BANK // width):
                first = P * (t0 + t)
                nc.tensor.matmul_mx(
                    out=bank[:, t, :],
                    lhsT=wk_w[b][:, first : first + P].bitcast(FP8X4),
                    lhsT_scale=wk_s[b][:, first : first + P],
                    rhs=v_w[:, cols].bitcast(FP8X4),
                    rhs_scale=v_s[:, cols],
                    start=True,
                    stop=True,
                )
            return bank[:].rearrange("p t j -> p j t")

        relu_of = {}
        h_of = {}

        def paired(step):
            return CHUNKS[step[0]][1] > BANK_TOKENS and step not in GPSIMD_TOKENS and step not in JOINT_STEPS

        joint_relu = keep.tile([P, len(JOINT_STEPS), CHUNKS[1][1], PACK], F32, name="joint_relu")

        def relu(step, i):
            c, b = step
            j0, width = CHUNKS[c]
            if i == 0:
                shape = [P, PACK // PAIR, width, PAIR] if paired(step) else [P, width, PACK]
                if step in JOINT_STEPS:
                    x = joint_relu[:, JOINT_STEPS.index(step)]
                elif step in holder:
                    x = holder[step].tile(shape, F32, name="relu%d_%d" % step, align_bytes=64, offset=0)
                elif step in GPSIMD_TOKENS:
                    x = keep.tile(shape, F32, name="relu%d_%d" % step)
                else:
                    x = ring.tile(shape, F32, name="relu", tag="relu", bufs=RELU_BUFS)
                relu_of[step] = x
            if paired(step):
                a = keys(j0, width, b, PAIR * i, next_key_bank([P, PAIR, width]))
                nc.scalar.activation(out=relu_of[step][:, i], in_=a, func=ACT.Relu)
            else:
                lo = BANK_TOKENS * i
                a = keys(j0 + lo, BANK_TOKENS, b, 0, next_key_bank([P, PACK, BANK_TOKENS]))
                nc.scalar.activation(out=relu_of[step][:, lo : lo + BANK_TOKENS, :], in_=a, func=ACT.Relu)

        def relus(step):
            for i in range(CHUNKS[step[0]][1] // BANK_TOKENS):
                relu(step, i)

        def square(step):
            if step == JOINT_STEPS[0]:
                nc.scalar.activation(
                    out=h_of[step][:, :JOINT_FIRST, :], in_=relu_of[step][:, :JOINT_FIRST, :], func=ACT.Square
                )
                return
            if step in GPSIMD_TOKENS:
                lo = GPSIMD_TOKENS[step]
                nc.scalar.activation(out=h_of[step][:, lo:, :], in_=relu_of[step][:, lo:, :], func=ACT.Square)
                return
            shape = [P, CHUNKS[step[0]][1], PACK]
            if step == WAITING_SQUARE:
                h = last_rounded[-1].tile(shape, BF16, name="h_waiting", align_bytes=64, offset=0)
            else:
                h = ring.tile(shape, BF16, name="h", tag="h", align_bytes=64, bufs=SQUARE_BUFS)
            h_of[step] = h[:]
            if paired(step):
                nc.scalar.activation(
                    out=h[:].rearrange("p j (u t) -> p j u t", t=PAIR),
                    in_=relu_of[step][:].rearrange("p u j t -> p j u t"),
                    func=ACT.Square,
                )
            else:
                nc.scalar.activation(out=h[:], in_=relu_of[step][:], func=ACT.Square)

        def gpsimd_square(step, pool, offset):
            h = pool.tile([P, CHUNKS[step[0]][1], PACK], BF16, name="h%d_%d" % step, align_bytes=64, offset=offset)
            h_of[step] = h[:]
            x = relu_of[step][:, : GPSIMD_TOKENS[step], :]
            nc.gpsimd.tensor_tensor(out=h[:, : GPSIMD_TOKENS[step], :], in0=x, in1=x, op=ALU.mult)

        def joint_square():
            h = last_rounded[0].tile(
                [P, len(JOINT_STEPS), CHUNKS[1][1], PACK], BF16, name="h_joint", align_bytes=64, offset=0
            )
            for i, step in enumerate(JOINT_STEPS):
                h_of[step] = h[:, i]
            x = joint_relu[:].rearrange("p s j t -> p (s j) t")[:, JOINT_FIRST:, :]
            nc.gpsimd.tensor_tensor(
                out=h[:].rearrange("p s j t -> p (s j) t")[:, JOINT_FIRST:, :], in0=x, in1=x, op=ALU.mult
            )

        def vector_keys():
            banks = []
            for step in VECTOR_STEPS:
                c, b = step
                j0, width = CHUNKS[c]
                if step == VECTOR_STEPS[-1]:
                    h = window_h.tile([P, width, PACK], BF16, name="h%d_%d" % step, align_bytes=64, offset=0)
                else:
                    h = keep.tile([P, width, PACK], BF16, name="h%d_%d" % step, align_bytes=64)
                h_of[step] = h[:]
                for lo in range(0, width, BANK_TOKENS):
                    offset = BANK_BYTES * len(banks)
                    x = last_raw.tile(
                        [P, BANK_TOKENS, PACK], F32, name="relu_vector%d" % offset, align_bytes=64, offset=offset
                    )
                    a = keys(j0 + lo, BANK_TOKENS, b, 0, next_value_bank([P, PACK, BANK_TOKENS]))
                    banks.append((a, x[:], h[:, lo : lo + BANK_TOKENS, :]))
            return banks

        def vector_run(banks):
            for i in range(len(banks) + 1):
                if i < len(banks):
                    a, x, h = banks[i]
                    nc.vector.tensor_scalar(out=x, in0=a, scalar1=0.0, scalar2=None, op0=ALU.max)
                if i >= 1:
                    a, x, h = banks[i - 1]
                    if i == len(banks):
                        a, x, h = [part[:, : BANK_TOKENS - RUN_REST, :] for part in (a, x, h)]
                    nc.vector.scalar_tensor_tensor(out=h, in0=a, scalar=0.0, in1=x, op0=ALU.max, op1=ALU.mult)

        def quantize_h(step):
            c, b = step
            j0, width = CHUNKS[c]
            cols = slice(j0, j0 + width)
            nc.vector.quantize_mx(
                out=h_w[:, b, cols].bitcast(FP8X4), scales=h_s[:, b, cols], in_=h_of[step].rearrange("p j t -> p (j t)")
            )

        y_of = {}
        gated = {}

        def tiles_a_bank(c):
            return 1 if c == LAST_CHUNK else PAIR

        def values(step):
            c, b = step
            j0, width = CHUNKS[c]
            cols = slice(j0, j0 + width)
            share = tiles_a_bank(c)
            if b == 0:
                y_of[c] = [next_value_bank([P, share, width]) for i in range(N_TILES // share)]
            for n in range(N_TILES):
                nc.tensor.matmul_mx(
                    out=y_of[c][n // share][:, n % share, :],
                    lhsT=wv_w[:, b, P * n : P * (n + 1)].bitcast(FP8X4),
                    lhsT_scale=wv_s[PACK * b : P, P * n : P * (n + 1)],
                    rhs=h_w[:, b, cols].bitcast(FP8X4),
                    rhs_scale=h_s[:, b, cols],
                    start=(b == 0 and n % share == 0),
                    stop=(b == LAST_PART and n % share == share - 1),
                )

        def gate_values(c, n0):
            j0, width = CHUNKS[c]
            share = tiles_a_bank(c)
            if c < PAIR and n0 == 0:
                first = float_tile(("gate", c), [P, PAIR, width])
                for n in range(PAIR):
                    gated[(c, n)] = first[:, n, :]
                product = first[:]
            elif c < PAIR:
                if c == 0:
                    gated["joint"] = joint_gated.tile([P, PAIR, PAIR * width], F32, name="gate_joint", align_bytes=64, offset=0)
                    for n in range(PAIR):
                        gated[(c, PAIR + n)] = gated["joint"][:, n, :]
                product = gated["joint"][:, :, j0 : j0 + width]
            else:
                if n0 == 0:
                    gated[c] = float_tile(("gate", c), [P, N_TILES, width])
                    for n in range(N_TILES):
                        gated[(c, n)] = gated[c][:, n, :]
                product = gated[c][:, n0 : n0 + share, :]
            nc.vector.tensor_tensor(
                out=product,
                in0=y_of[c][n0 // share][:],
                in1=gate[:, n0 : n0 + share, j0 : j0 + width],
                op=ALU.mult,
            )

        def gate_chunk(c):
            for n0 in range(0, N_TILES, tiles_a_bank(c)):
                gate_values(c, n0)

        def add_and_store(c, n0):
            j0, width = CHUNKS[c]
            if c == 0 and n0 >= PAIR:
                width = PAIR * width
            count = SHARED_STORES.get((c, n0), 1)
            result = float_tile(("add", c, n0), [P, count, width])
            for n in range(n0, n0 + count):
                residual = resid[:, n, :] if c == LAST_CHUNK else g_tab[n][:].indirect(listed(j0, width))
                nc.vector.tensor_tensor(out=result[:, n - n0, :], in0=residual, in1=gated[(c, n)], op=ALU.add)
            nc.sync.dma_start(out=out_rows[:, n0 : n0 + count, j0 : j0 + width], in_=result[:])
            return count

        nc.vector.tensor_copy(v_s[:], tab_s[:].bitcast(U8).indirect(offsets[:]))
        for j0, width in GATHERS:
            nc.vector.tensor_copy(v_w[:, j0 : j0 + width], tab_w[:].bitcast(U32).indirect(listed(j0, width)))
            last = min(j0 + width, CHUNKS[LAST_CHUNK - 1][0])
            for first in range(j0, last, 2 * BANK_TOKENS):
                count = min(2 * BANK_TOKENS, last - first)
                share = PAIR if first == 0 else BANK // count
                for n0 in range(0, N_TILES, share):
                    receptance(first, count, n0, share, next_key_bank([P, share, count]))
        for b in range(PARTS):
            quantize_wk(b)

        relus((0, 0))
        square((0, 0))
        for step in JOINT_STEPS:
            relus(step)
        relus(WAITING_SQUARE)
        square(WAITING_SQUARE)
        relu(WINDOW_STEPS[0], 0)
        banks = vector_keys()
        joint_square()
        vector_run(banks)

        relus((0, LAST_PART))
        relus((1, LAST_PART))
        square((0, LAST_PART))
        rest_x, rest_h = [part[:, BANK_TOKENS - RUN_REST :, :] for part in banks[-1][1:]]
        nc.scalar.activation(out=rest_h, in_=rest_x, func=ACT.Square)
        square(JOINT_STEPS[0])
        for b in range(PARTS):
            quantize_h((0, b))
            values((0, b))
        for b in range(LAST_PART):
            quantize_h((1, b))
        gate_chunk(0)
        relu(WINDOW_STEPS[0], 1)
        relu(WINDOW_STEPS[1], 0)
        square((1, LAST_PART))
        quantize_h((1, LAST_PART))
        gpsimd_square(WINDOW_STEPS[0], window_h, 0)
        square(WINDOW_STEPS[0])
        quantize_h(WINDOW_STEPS[0])
        add_and_store(0, 0)
        relu(WINDOW_STEPS[1], 1)
        for b in range(PARTS):
            values((1, b))
        gate_chunk(1)
        gpsimd_square(WINDOW_STEPS[1], window_h, 0)

        for b in range(2, PARTS):
            relus((2, b))
            square((2, b - 1))
        relus((3, 0))
        square((2, LAST_PART))
        relus(WINDOW_STEPS[2])
        receptance(*CHUNKS[3], 0, N_TILES, next_key_bank([P, N_TILES, CHUNKS[3][1]]))
        gpsimd_square(WINDOW_STEPS[2], joint_gated, 0)
        square((3, 0))
        relus((3, 1))
        for b in range(2, PARTS):
            relus((3, b))
            square((3, b - 1))
        square((3, LAST_PART))
        for b in range(1, PARTS):
            relus((LAST_CHUNK, b))
            square((LAST_CHUNK, b - 1))
        square((LAST_CHUNK, LAST_PART))
        receptance(*LAST_TOKENS, 0, N_TILES, bank_tile("last_gate", key_turns[-2], [P, N_TILES, LAST_TOKENS[1]]))

        for c in range(2, len(CHUNKS)):
            for b in range(PARTS):
                if (c, b) != WINDOW_STEPS[0]:
                    quantize_h((c, b))
        for c in range(2, len(CHUNKS)):
            for b in range(PARTS):
                values((c, b))
            if c < LAST_CHUNK:
                gate_chunk(c)
        for n in range(N_TILES):
            nc.vector.tensor_copy(resid[:, n, :], g_tab[n][:].indirect(listed(*LAST_TOKENS)))
        for c in range(LAST_CHUNK):
            n = 1 if c == 0 else 0
            while n < (PAIR if c == 1 else N_TILES):
                n = n + add_and_store(c, n)
        for n in range(N_TILES + ADD_LAG):
            if n < N_TILES:
                gate_values(LAST_CHUNK, n)
            if n >= ADD_LAG:
                add_and_store(LAST_CHUNK, n - ADD_LAG)
